import numpy as np
import ml_dtypes


def mxq(x, axis, fmt="e4m3"):
    dtype, down = {"e4m3": (ml_dtypes.float8_e4m3fn, 7), "e5m2": (ml_dtypes.float8_e5m2, 14)}[fmt]
    v = np.moveaxis(np.asarray(x, np.float32).astype(ml_dtypes.bfloat16).astype(np.float64), axis, -1)
    blocks = v.reshape(v.shape[:-1] + (-1, 32))
    amax = np.abs(blocks).max(-1, keepdims=True)
    byte = np.maximum(np.where(amax > 0, np.frexp(amax)[1] - 1 + 127, 0) - down, 1)
    scale = np.exp2(byte - 127.0)
    codes = (blocks / scale).astype(np.float32).astype(dtype).astype(np.float64)
    return np.moveaxis((codes * scale).reshape(v.shape), -1, axis)


WIDE = False


def mx_kscale(k):
    if not WIDE:
        return np.ones(k)
    levels = np.array([10, -10, 5, -5, 0])
    if k % 512:
        return np.exp2(np.random.permutation(np.resize(levels, k // 32))).repeat(32)
    a = np.empty((k // 512, 16))
    for p in range(k // 512):
        a[p, :8] = np.random.permutation(np.resize(levels, 8))
        for g in range(8):
            far = levels[np.abs(levels - a[p, g]) >= 10]
            a[p, g + 8] = far[np.random.randint(len(far))]
    return np.exp2(a.ravel()).repeat(32)


def f64(x):
    return np.asarray(x).astype(np.float64)


def striped(idx):
    return np.tile(idx.reshape(-1, 16).T, (8, 1)).astype(np.uint16)


def unstriped(offs):
    return offs[:16].T.reshape(-1).astype(np.int64)


E2M1 = np.array([0.0, 0.5, 1.0, 1.5, 2.0, 3.0, 4.0, 6.0, -0.0, -0.5, -1.0, -1.5, -2.0, -3.0, -4.0, -6.0])


def pack_weight(w, fmt):
    k, n = w.shape
    w = f64(np.asarray(w, np.float32).astype(ml_dtypes.bfloat16)).reshape(k // 32, 32, n)
    amax = np.abs(w).max(1)
    if fmt == "e4m3":
        byte = np.frexp(amax)[1] - 1 + 127 - 7
    else:
        mant, ex = np.frexp(amax / 6.0)
        byte = np.where(mant > 0.5, ex, ex - 1) + 127
    byte = np.clip(np.where(amax > 0, byte, 1), 1, 254)
    scaled = (w * np.exp2(127.0 - byte)[:, None, :]).reshape(k, n).astype(np.float32)
    by_word = np.ascontiguousarray(scaled.reshape(k // 512, 128, 4, n).transpose(0, 1, 3, 2))
    if fmt == "e4m3":
        words = by_word.astype(ml_dtypes.float8_e4m3fn).view(np.uint8)
    else:
        c = by_word.astype(ml_dtypes.float4_e2m1fn).view(np.uint8) & 0xF
        words = (c[..., 0::2] | (c[..., 1::2] << 4)).reshape(k // 512, 128, 2 * n)
    return np.ascontiguousarray(words), np.ascontiguousarray(byte.astype(np.uint8).reshape(k // 512, 16, n))


def unpack_weight(words, scales, fmt):
    g, _, n = scales.shape
    words = np.ascontiguousarray(words).reshape(g, 128, n, -1)
    if fmt == "e4m3":
        vals = words.view(ml_dtypes.float8_e4m3fn).astype(np.float64)
    else:
        nib = np.empty((g, 128, n, 4), np.uint8)
        nib[..., 0::2] = words & 0xF
        nib[..., 1::2] = words >> 4
        vals = E2M1[nib]
    vals = vals * np.repeat(np.exp2(scales.astype(np.float64) - 127.0), 8, axis=1)[..., None]
    return vals.transpose(0, 1, 3, 2).reshape(g * 512, n)


def gelu(v):
    return 0.5 * v * (1.0 + np.tanh(np.sqrt(2.0 / np.pi) * (v + 0.044715 * v**3)))


K, T, S, P, H = 1536, 2048, 1024, 512, 1024

def setup_inputs():
    n = np.random.standard_normal
    s = mx_kscale(K)[:, None]
    u = mx_kscale(H)[:, None]
    tab_words, tab_scales = pack_weight(n((K, T)) * s, "e4m3")
    w1_words, w1_scales = pack_weight(0.4 * n((K, H)) / np.sqrt(K) / s, "e2m1")
    w2 = (n((H, H)) / np.sqrt(H) / u).astype(np.float32)
    phase = np.random.uniform(-0.5, 0.5, H).astype(np.float32)
    amp = (np.random.uniform(1.0, 2.0, H) * u[:, 0]).astype(np.float32)
    mrg = np.random.uniform(0.5, 2.0, H).astype(np.float32)
    offs = striped(np.random.permutation(T)[:S])
    pos1 = striped(np.random.permutation(S)[:P])
    pos2 = striped(np.random.permutation(S)[:P])
    return {"tab_words": tab_words, "tab_scales": tab_scales,
            "offs": offs, "pos1": pos1, "pos2": pos2,
            "w1_words": w1_words, "w1_scales": w1_scales,
            "w2": w2, "phase": phase, "amp": amp, "mrg": mrg}

def reference(tab_words, tab_scales, offs, pos1, pos2, w1_words, w1_scales,
              w2, phase, amp, mrg):
    v = unpack_weight(tab_words, tab_scales, "e4m3")[:, unstriped(offs)]
    w1 = unpack_weight(w1_words, w1_scales, "e2m1")
    h = w1.T @ v
    theme = h[:, unstriped(pos1)]
    z = f64(amp)[:, None] * np.sin(theme + f64(phase)[:, None])
    y = mxq(f64(w2), 0, "e4m3").T @ mxq(z, 0, "e4m3")
    actual = h[:, unstriped(pos2)]
    return f64(mrg)[:, None] * np.square(y - actual)

@@ -1,0 +1,286 @@
+from contextlib import ExitStack
+
+import concourse.mybir as mybir
+from concourse.masks import make_identity
+
+K, T, S, NP, H = 1536, 2048, 1024, 512, 1024
+FLOPS = 2 * K * S * H + 2 * H * H * NP
+
+F32 = mybir.dt.float32
+BF16 = mybir.dt.bfloat16
+I32 = mybir.dt.int32
+U32 = mybir.dt.uint32
+U16 = mybir.dt.uint16
+U8 = mybir.dt.uint8
+FP8X4 = mybir.dt.float8_e4m3fn_x4
+FP4X4 = mybir.dt.float4_e2m1fn_x4
+ACT = mybir.ActivationFunctionType
+ALU = mybir.AluOpType
+
+P = 128
+PASSES = K // 512
+GROUPS = H // 512
+TILES = H // P
+BANK = 512
+ROW0 = 20
+SPAN = 100
+
+
+def tile_list_passacaglia_variation_surprise_kernel(
+    tc, tab_words, tab_scales, offs, pos1, pos2, w1_words, w1_scales, w2, phase, amp, mrg, out
+):
+    nc = tc.nc
+    with ExitStack() as ctx:
+        lists = ctx.enter_context(tc.tile_pool(name="lists", bufs=1))
+        keep = ctx.enter_context(tc.tile_pool(name="keep", bufs=1))
+        big = ctx.enter_context(tc.tile_pool(name="big", bufs=PASSES))
+        ring = ctx.enter_context(tc.tile_pool(name="ring", bufs=3))
+        psum = ctx.enter_context(tc.psum_pool(name="psum", bufs=1))
+
+        offs_sb = lists.tile([P, S // 16], U16, name="offs_sb")
+        pos1_sb = lists.tile([P, NP // 16], U16, name="pos1_sb")
+        pos2_sb = lists.tile([P, NP // 16], U16, name="pos2_sb")
+
+        tab_sc = big.tile([P, T], U8, name="tab_sc", tag="big", align_bytes=64)
+        picked_sc = keep.tile([P, S], U8, name="picked_sc", align_bytes=64)
+        v_sc = keep.tile([P, PASSES * S], U8, name="v_sc", align_bytes=64)
+        w1_raw = keep.tile([P, PASSES * H // 2], I32, name="w1_raw", align_bytes=64)
+        w1_codes = keep.tile([P, PASSES * H * 2], U8, name="w1_codes", align_bytes=64)
+        w1_sc_raw = keep.tile([P, PASSES * H // 4], I32, name="w1_sc_raw", align_bytes=64)
+        w1_sc = keep.tile([P, PASSES * H], U8, name="w1_sc", align_bytes=64)
+        vec_rows = keep.tile([P, 512], F32, name="vec_rows")
+        vec_ordered = keep.tile([P, 4, P], F32, name="vec_ordered")
+        vec = keep.tile([P, 4, 8], F32, name="vec")
+        ident = keep.tile([P, P], F32, name="ident")
+        warm = keep.tile([P, 8], F32, name="warm")
+
+        nc.gpsimd.memset(w1_sc_raw[:], 0)
+        nc.gpsimd.memset(vec_rows[:], 0.0)
+        nc.sync.dma_start(
+            out=w1_raw[:].rearrange("p (a c) -> p a c", a=PASSES),
+            in_=w1_words.rearrange("a p c -> p a c").bitcast(I32),
+        )
+        nc.sync.dma_start(offs_sb[:], offs)
+        for q in range(4):
+            queue = nc.sync if q < 2 else nc.scalar
+            queue.dma_start(
+                out=tab_sc[32 * q + ROW0 : 32 * q + 32, :].bitcast(I32),
+                in_=tab_scales[:, 4 * q : 4 * q + 4, :].bitcast(I32),
+            )
+        for q in range(4):
+            nc.scalar.dma_start(
+                out=w1_sc_raw[32 * q : 32 * q + 4, :].rearrange("p (a c) -> p a c", a=PASSES),
+                in_=w1_scales[:, 4 * q : 4 * q + 4, :].rearrange("a r n -> r a n").bitcast(I32),
+            )
+        nc.vector.memset(warm[:], 0.0)
+        nc.scalar.activation(out=warm[:, 0:1], in_=warm[:, 7:8], func=ACT.Sin)
+        tabs = []
+
+        def load_tab(a):
+            tab = big.tile([P, T], I32, name=f"tab{a}", tag="big", align_bytes=64)
+            nc.sync.dma_start(out=tab[:], in_=tab_words[a].rearrange("p t i -> p (t i)").bitcast(I32))
+            tabs.append(tab)
+
+        load_tab(0)
+        load_tab(1)
+        for v, vector in enumerate((phase, amp, mrg)):
+            nc.gpsimd.dma_start(
+                out=vec_rows[GROUPS * v : GROUPS * (v + 1), :], in_=vector.rearrange("(b c) -> b c", b=GROUPS)
+            )
+        nc.sync.dma_start(pos1_sb[:], pos1)
+        nc.sync.dma_start(pos2_sb[:], pos2)
+
+        for q in range(4):
+            nc.vector.memset(tab_sc[32 * q : 32 * q + ROW0, :].bitcast(I32), 0)
+        nc.vector.memset(v_sc[96:P, :].bitcast(I32), 0)
+        make_identity(nc, ident[:])
+
+        nc.vector.tensor_copy(
+            out=w1_codes[:].bitcast(I32).rearrange("p (b t g w) -> p b t g w", t=4, g=16, w=4),
+            in_=w1_raw[:].rearrange("p (b g t w) -> p b t g w", t=4, g=16, w=4),
+        )
+        nc.vector.tensor_copy(picked_sc[:], tab_sc[:].indirect(offs_sb[:]))
+        for a in range(PASSES):
+            first = ROW0 + 4 * a
+            nc.scalar.dma_start(
+                out=v_sc[0:SPAN, a * S : (a + 1) * S].bitcast(I32),
+                in_=picked_sc[first : first + SPAN, :].bitcast(I32),
+            )
+        load_tab(2)
+        v_codes = [big.tile([P, S], U32, name=f"v_codes{a}", tag="late", align_bytes=64) for a in range(PASSES)]
+
+        def pick_codes(a, half):
+            nc.vector.tensor_copy(
+                v_codes[a][:, half * BANK : (half + 1) * BANK], tabs[a][:].bitcast(U32).indirect(offs_sb[:, 32 * half : 32 * (half + 1)])
+            )
+
+        pick_codes(0, 0)
+        nc.vector.tensor_copy(
+            out=w1_sc[:].bitcast(I32).rearrange("p (b t g w) -> p b t g w", t=4, g=16, w=2),
+            in_=w1_sc_raw[:].rearrange("p (b g t w) -> p b t g w", t=4, g=16, w=2),
+        )
+        pick_codes(0, 1)
+        for half in range(2):
+            pick_codes(1, half)
+        nc.vector.tensor_copy(v_codes[2][:], tabs[2][:].bitcast(U32).indirect(offs_sb[:]))
+
+        nc.gpsimd.tensor_copy(
+            out=vec_ordered[:].rearrange("p t (g i) -> p t g i", i=8),
+            in_=vec_rows[:].rearrange("p (g t i) -> p t g i", t=4, i=8),
+        )
+        vec_ps = psum.tile([P, 4, P], F32, name="vec_ps", tag="bank7")
+        for t in range(4):
+            nc.tensor.transpose(vec_ps[:, t, :], vec_ordered[:, t, :], ident[:])
+        nc.scalar.copy(out=vec[:, :, 0:6], in_=vec_ps[:, :, 0:6])
+
+        def per_channel(v, j):
+            col = GROUPS * v + j // 4
+            return vec[:, j % 4, col : col + 1]
+
+        w2_view = w2.rearrange("(b g t i) (c n) -> b c t g i n", b=GROUPS, g=16, t=4, c=GROUPS)
+        chunks = [(b, c) for c in range(GROUPS) for b in range(GROUPS)]
+        w2_raw = {}
+
+        def load_w2(b, c):
+            raw = big.tile([P, 4, 512], F32, name=f"w2_raw{b}{c}", tag="big", align_bytes=64)
+            for t in range(4):
+                nc.sync.dma_start(out=raw[:, t, :], in_=w2_view[b, c, t])
+            w2_raw[(b, c)] = raw
+
+        for b, c in chunks[:PASSES]:
+            load_w2(b, c)
+
+        w2_codes, w2_sc, w2_grouped = {}, {}, {}
+
+        def quantize_w2(b, c):
+            if (b, c) == chunks[0]:
+                grouped = ring.tile([P, 4 * 512], BF16, name="w2_grouped00", tag="grouped", bufs=2, align_bytes=64)
+            else:
+                grouped = big.tile([P, 4 * 512], BF16, name=f"w2_grouped{b}{c}", tag="late", align_bytes=64)
+            dst = grouped[:].rearrange("p (u g e l t) -> p e g u t l", u=4, g=16, e=2, l=4)
+            src = w2_raw[(b, c)][:].rearrange("p t (g u e l) -> p e g u t l", u=4, g=16, e=2)
+            for e in range(2):
+                if (b, c) == chunks[0]:
+                    nc.vector.tensor_copy(out=dst[:, e], in_=src[:, e])
+                else:
+                    nc.scalar.copy(out=dst[:, e], in_=src[:, e])
+            codes = keep.tile([P, 512], U32, name=f"w2_codes{b}{c}", align_bytes=64)
+            scales = keep.tile([P, 512], U8, name=f"w2_sc{b}{c}", align_bytes=64)
+            nc.vector.quantize_mx(out=codes[:].bitcast(FP8X4), scales=scales[:], in_=grouped[:])
+            w2_codes[(b, c)] = codes
+            w2_sc[(b, c)] = scales
+            w2_grouped[(b, c)] = grouped
+
+        quantize_w2(*chunks[0])
+        load_w2(*chunks[3])
+
+        h = [keep.tile([P, S], F32, name=f"h{j}") for j in range(TILES)]
+        theme = [keep.tile([P, NP], F32, name=f"theme{j}") for j in range(TILES)]
+        sine = [keep.tile([P, NP], F32, name=f"sine{j}") for j in range(TILES)]
+        z_rows = [keep.tile([P, 4, NP], BF16, name=f"z_rows{b}", align_bytes=64) for b in range(GROUPS)]
+        z_codes = [keep.tile([P, NP], U32, name=f"z_codes{b}", align_bytes=64) for b in range(GROUPS)]
+        z_sc = [keep.tile([P, NP], U8, name=f"z_sc{b}", align_bytes=64) for b in range(GROUPS)]
+
+        def scale_by_amp(j):
+            nc.vector.tensor_scalar(
+                out=z_rows[j // 4][:, j % 4, :], in0=sine[j][:], scalar1=per_channel(1, j), scalar2=None, op0=ALU.mult
+            )
+
+        z_grouped = {}
+
+        def group_z(b):
+            grouped = ring.tile([P, 4 * NP], BF16, name=f"z_grouped{b}", tag="grouped", bufs=2, align_bytes=64)
+            nc.vector.tensor_copy(
+                out=grouped[:].rearrange("p (c i t) -> p c t i", i=4, t=4),
+                in_=z_rows[b][:].rearrange("p t (c i) -> p c t i", i=4),
+            )
+            z_grouped[b] = grouped
+
+        def quantize_z(b):
+            nc.vector.quantize_mx(out=z_codes[b][:].bitcast(FP8X4), scales=z_sc[b][:], in_=z_grouped[b][:])
+
+        def new_banks(j):
+            return [
+                psum.tile([P, BANK], F32, name=f"h_ps{j}_{half}", tag=f"bank{2 * (j % 4) + half}") for half in range(2)
+            ]
+
+        def first_stage_pass(bank, j, a, half):
+            nc.tensor.matmul_mx(
+                out=bank[:],
+                lhsT=w1_codes[:, 2 * (a * H + j * P) : 2 * (a * H + (j + 1) * P)].bitcast(FP4X4),
+                lhsT_scale=w1_sc[:, a * H + j * P : a * H + (j + 1) * P],
+                rhs=v_codes[a][:, half * BANK : (half + 1) * BANK].bitcast(FP8X4),
+                rhs_scale=v_sc[:, a * S + half * BANK : a * S + (half + 1) * BANK],
+                start=(a == 0),
+                stop=(a == PASSES - 1),
+            )
+
+        def pick_theme(j, banks):
+            for half in range(2):
+                if j == 0 and half == 1:
+                    nc.vector.tensor_copy(out=h[j][:, half * BANK : (half + 1) * BANK], in_=banks[half][:])
+                else:
+                    nc.scalar.copy(out=h[j][:, half * BANK : (half + 1) * BANK], in_=banks[half][:])
+            nc.vector.tensor_copy(theme[j][:], h[j][:].indirect(pos1_sb[:]))
+
+        early = [new_banks(j) for j in range(4)]
+        for a in range(PASSES):
+            for j in range(4):
+                for half in range(2):
+                    first_stage_pass(early[j][half], j, a, half)
+        for j in range(4):
+            pick_theme(j, early[j])
+        for j in range(4, TILES):
+            banks = new_banks(j)
+            for half in range(2):
+                for a in range(PASSES):
+                    first_stage_pass(banks[half], j, a, half)
+            pick_theme(j, banks)
+        for j in range(TILES):
+            nc.scalar.activation(out=sine[j][:], in_=theme[j][:], func=ACT.Sin, bias=per_channel(0, j))
+            scale_by_amp(j)
+            if j == 3:
+                group_z(0)
+                quantize_z(0)
+        group_z(1)
+        quantize_z(1)
+
+        for b, c in chunks[1:]:
+            quantize_w2(b, c)
+
+        out_view = out.rearrange("(b g t i) m -> b t g i m", b=GROUPS, g=16, t=4)
+        actual = [theme[6][:], theme[7][:], sine[6][:], w2_grouped[chunks[1]][:].bitcast(F32)[:, 0:NP]]
+        actual = actual + actual[:3] + [w2_grouped[chunks[3]][:].bitcast(F32)[:, 0:NP]]
+
+        def pick_actual(j):
+            nc.vector.tensor_copy(actual[j], h[j][:].indirect(pos2_sb[:]))
+
+        for j in range(4):
+            pick_actual(j)
+        for j in range(TILES):
+            c, u = j // 4, j % 4
+            y = psum.tile([P, NP], F32, name=f"y{j}", tag=f"bank{j}")
+            for b in range(GROUPS):
+                nc.tensor.matmul_mx(
+                    out=y[:],
+                    lhsT=w2_codes[(b, c)][:, u * P : (u + 1) * P].bitcast(FP8X4),
+                    lhsT_scale=w2_sc[(b, c)][:, u * P : (u + 1) * P],
+                    rhs=z_codes[b][:].bitcast(FP8X4),
+                    rhs_scale=z_sc[b][:],
+                    start=(b == 0),
+                    stop=(b == GROUPS - 1),
+                )
+            diff = ring.tile([P, NP], F32, name=f"diff{j}", tag="diff", bufs=5)
+            nc.vector.tensor_tensor(out=diff[:], in0=y[:], in1=actual[j], op=ALU.subtract)
+            if j + 4 < TILES:
+                pick_actual(j + 4)
+            mark = ring.tile([P, NP], F32, name=f"mark{j}", tag="mark", bufs=TILES)
+            if j < TILES - 1:
+                square = ring.tile([P, NP], F32, name=f"square{j}", tag="square")
+                nc.scalar.activation(out=square[:], in_=diff[:], func=ACT.Square)
+                nc.scalar.activation(out=mark[:], in_=square[:], func=ACT.Copy, scale=per_channel(2, j))
+            else:
+                nc.vector.scalar_tensor_tensor(
+                    out=mark[:], in0=diff[:], scalar=per_channel(2, j), in1=diff[:], op0=ALU.mult, op1=ALU.mult
+                )
+            nc.sync.dma_start(out=out_view[c, u], in_=mark[:])

@@ -67,10 +67,10 @@ def tile_list_passacaglia_variation_surprise_kernel(
                 out=tab_sc[32 * q + ROW0 : 32 * q + 32, :].bitcast(I32),
                 in_=tab_scales[:, 4 * q : 4 * q + 4, :].bitcast(I32),
             )
-        for q in range(4):
+        for r in range(4):
             nc.scalar.dma_start(
-                out=w1_sc_raw[32 * q : 32 * q + 4, :].rearrange("p (a c) -> p a c", a=PASSES),
-                in_=w1_scales[:, 4 * q : 4 * q + 4, :].rearrange("a r n -> r a n").bitcast(I32),
+                out=w1_sc_raw[r:P:32, :].rearrange("p (a c) -> p a c", a=PASSES),
+                in_=w1_scales[:, r:16:4, :].rearrange("a q n -> q a n").bitcast(I32),
             )
         nc.vector.memset(warm[:], 0.0)
         nc.scalar.activation(out=warm[:, 0:1], in_=warm[:, 7:8], func=ACT.Sin)
@@ -124,7 +124,7 @@ def tile_list_passacaglia_variation_surprise_kernel(
             pick_codes(1, half)
         nc.vector.tensor_copy(v_codes[2][:], tabs[2][:].bitcast(U32).indirect(offs_sb[:]))
 
-        nc.gpsimd.tensor_copy(
+        nc.scalar.copy(
             out=vec_ordered[:].rearrange("p t (g i) -> p t g i", i=8),
             in_=vec_rows[:].rearrange("p (g t i) -> p t g i", t=4, i=8),
         )
@@ -153,14 +153,14 @@ def tile_list_passacaglia_variation_surprise_kernel(
         w2_codes, w2_sc, w2_grouped = {}, {}, {}
 
         def quantize_w2(b, c):
-            if (b, c) == chunks[0]:
-                grouped = ring.tile([P, 4 * 512], BF16, name="w2_grouped00", tag="grouped", bufs=2, align_bytes=64)
+            if c == 0:
+                grouped = ring.tile([P, 4 * 512], BF16, name=f"w2_grouped{b}{c}", tag="grouped", bufs=3, align_bytes=64)
             else:
                 grouped = big.tile([P, 4 * 512], BF16, name=f"w2_grouped{b}{c}", tag="late", align_bytes=64)
             dst = grouped[:].rearrange("p (u g e l t) -> p e g u t l", u=4, g=16, e=2, l=4)
             src = w2_raw[(b, c)][:].rearrange("p t (g u e l) -> p e g u t l", u=4, g=16, e=2)
             for e in range(2):
-                if (b, c) == chunks[0]:
+                if c == 0:
                     nc.vector.tensor_copy(out=dst[:, e], in_=src[:, e])
                 else:
                     nc.scalar.copy(out=dst[:, e], in_=src[:, e])
@@ -182,14 +182,16 @@ def tile_list_passacaglia_variation_surprise_kernel(
         z_sc = [keep.tile([P, NP], U8, name=f"z_sc{b}", align_bytes=64) for b in range(GROUPS)]
 
         def scale_by_amp(j):
-            nc.vector.tensor_scalar(
-                out=z_rows[j // 4][:, j % 4, :], in0=sine[j][:], scalar1=per_channel(1, j), scalar2=None, op0=ALU.mult
-            )
+            row = z_rows[j // 4][:, j % 4, :]
+            if j < 4:
+                nc.scalar.activation(out=row, in_=sine[j][:], func=ACT.Copy, scale=per_channel(1, j))
+            else:
+                nc.vector.tensor_scalar(out=row, in0=sine[j][:], scalar1=per_channel(1, j), scalar2=None, op0=ALU.mult)
 
         z_grouped = {}
 
         def group_z(b):
-            grouped = ring.tile([P, 4 * NP], BF16, name=f"z_grouped{b}", tag="grouped", bufs=2, align_bytes=64)
+            grouped = ring.tile([P, 4 * NP], BF16, name=f"z_grouped{b}", tag="grouped", bufs=3, align_bytes=64)
             nc.vector.tensor_copy(
                 out=grouped[:].rearrange("p (c i t) -> p c t i", i=4, t=4),
                 in_=z_rows[b][:].rearrange("p t (c i) -> p c t i", i=4),
@@ -245,19 +247,9 @@ def tile_list_passacaglia_variation_surprise_kernel(
         group_z(1)
         quantize_z(1)
 
-        for b, c in chunks[1:]:
-            quantize_w2(b, c)
-
         out_view = out.rearrange("(b g t i) m -> b t g i m", b=GROUPS, g=16, t=4)
-        actual = [theme[6][:], theme[7][:], sine[6][:], w2_grouped[chunks[1]][:].bitcast(F32)[:, 0:NP]]
-        actual = actual + actual[:3] + [w2_grouped[chunks[3]][:].bitcast(F32)[:, 0:NP]]
 
-        def pick_actual(j):
-            nc.vector.tensor_copy(actual[j], h[j][:].indirect(pos2_sb[:]))
-
-        for j in range(4):
-            pick_actual(j)
-        for j in range(TILES):
+        def predict(j):
             c, u = j // 4, j % 4
             y = psum.tile([P, NP], F32, name=f"y{j}", tag=f"bank{j}")
             for b in range(GROUPS):
@@ -270,10 +262,18 @@ def tile_list_passacaglia_variation_surprise_kernel(
                     start=(b == 0),
                     stop=(b == GROUPS - 1),
                 )
+            nc.scalar.copy(out=theme[j][:], in_=y[:])
+
+        quantize_w2(*chunks[1])
+        quantize_w2(*chunks[2])
+        for j in range(4):
+            predict(j)
+        quantize_w2(*chunks[3])
+        for j in range(4, TILES):
+            predict(j)
+        for j in range(TILES):
             diff = ring.tile([P, NP], F32, name=f"diff{j}", tag="diff", bufs=5)
-            nc.vector.tensor_tensor(out=diff[:], in0=y[:], in1=actual[j], op=ALU.subtract)
-            if j + 4 < TILES:
-                pick_actual(j + 4)
+            nc.vector.tensor_tensor(out=diff[:], in0=h[j][:].indirect(pos2_sb[:]), in1=theme[j][:], op=ALU.subtract)
             mark = ring.tile([P, NP], F32, name=f"mark{j}", tag="mark", bufs=TILES)
             if j < TILES - 1:
                 square = ring.tile([P, NP], F32, name=f"square{j}", tag="square")
@@ -283,4 +283,4 @@ def tile_list_passacaglia_variation_surprise_kernel(
                 nc.vector.scalar_tensor_tensor(
                     out=mark[:], in0=diff[:], scalar=per_channel(2, j), in1=diff[:], op0=ALU.mult, op1=ALU.mult
                 )
-            nc.sync.dma_start(out=out_view[c, u], in_=mark[:])
+            nc.sync.dma_start(out=out_view[j // 4, j % 4], in_=mark[:])

@@ -22,8 +22,23 @@ PASSES = K // 512
 GROUPS = H // 512
 TILES = H // P
 BANK = 512
-ROW0 = 20
-SPAN = 100
+LAST0 = P - 16 * PASSES
+PAIR0 = LAST0 + 16
+AT_W2_01 = 0
+AT_TAB2 = 7680
+AT_TAB_SC = 15360
+AT_W1_REST_RAW = 16896
+AT_W2_10 = 20992
+AT_TAB1 = AT_W2_10 + 8192 - 64
+AT_V2 = AT_TAB1 + 5184
+AT_W2_00 = AT_V2 + 4096
+AT_TAB0 = AT_W2_00 + 8192 - 64
+AT_W1_SC = AT_TAB0 + 64
+AT_W1_PAIR = AT_TAB0 + 5184
+AT_SINE = [AT_W1_PAIR + 512 - 2048, AT_W1_PAIR + 512]
+AT_V1 = AT_SINE[1] + 4096
+AT_Z_GROUPED1 = AT_V1 + 4096
+VEC_ROWS = 3 * GROUPS
 
 
 def tile_list_passacaglia_variation_surprise_kernel(
@@ -32,174 +47,169 @@ def tile_list_passacaglia_variation_surprise_kernel(
     nc = tc.nc
     with ExitStack() as ctx:
         lists = ctx.enter_context(tc.tile_pool(name="lists", bufs=1))
-        keep = ctx.enter_context(tc.tile_pool(name="keep", bufs=1))
-        big = ctx.enter_context(tc.tile_pool(name="big", bufs=PASSES))
-        ring = ctx.enter_context(tc.tile_pool(name="ring", bufs=3))
+        sb = ctx.enter_context(tc.tile_pool(name="sb", bufs=1))
+        hand = ctx.enter_context(tc.tile_pool(name="hand", bufs=1))
         psum = ctx.enter_context(tc.psum_pool(name="psum", bufs=1))
+
+        def tile(shape, dtype, name, place=None):
+            if isinstance(place, int):
+                return hand.tile(shape, dtype, name=name, align_bytes=64, offset=place)
+            return sb.tile(shape, dtype, name=name, tag=place or name, align_bytes=64)
 
         offs_sb = lists.tile([P, S // 16], U16, name="offs_sb")
         pos1_sb = lists.tile([P, NP // 16], U16, name="pos1_sb")
         pos2_sb = lists.tile([P, NP // 16], U16, name="pos2_sb")
 
-        tab_sc = big.tile([P, T], U8, name="tab_sc", tag="big", align_bytes=64)
-        picked_sc = keep.tile([P, S], U8, name="picked_sc", align_bytes=64)
-        v_sc = keep.tile([P, PASSES * S], U8, name="v_sc", align_bytes=64)
-        w1_raw = keep.tile([P, PASSES * H // 2], I32, name="w1_raw", align_bytes=64)
-        w1_codes = keep.tile([P, PASSES * H * 2], U8, name="w1_codes", align_bytes=64)
-        w1_sc_raw = keep.tile([P, PASSES * H // 4], I32, name="w1_sc_raw", align_bytes=64)
-        w1_sc = keep.tile([P, PASSES * H], U8, name="w1_sc", align_bytes=64)
-        vec_rows = keep.tile([P, 512], F32, name="vec_rows")
-        vec_ordered = keep.tile([P, 4, P], F32, name="vec_ordered")
-        vec = keep.tile([P, 4, 8], F32, name="vec")
-        ident = keep.tile([P, P], F32, name="ident")
-        warm = keep.tile([P, 8], F32, name="warm")
-
-        nc.gpsimd.memset(w1_sc_raw[:], 0)
-        nc.gpsimd.memset(vec_rows[:], 0.0)
-        nc.sync.dma_start(
-            out=w1_raw[:].rearrange("p (a c) -> p a c", a=PASSES),
-            in_=w1_words.rearrange("a p c -> p a c").bitcast(I32),
-        )
-        nc.sync.dma_start(offs_sb[:], offs)
-        for q in range(4):
-            queue = nc.sync if q < 2 else nc.scalar
-            queue.dma_start(
-                out=tab_sc[32 * q + ROW0 : 32 * q + 32, :].bitcast(I32),
-                in_=tab_scales[:, 4 * q : 4 * q + 4, :].bitcast(I32),
-            )
-        for r in range(4):
-            nc.scalar.dma_start(
-                out=w1_sc_raw[r:P:32, :].rearrange("p (a c) -> p a c", a=PASSES),
-                in_=w1_scales[:, r:16:4, :].rearrange("a q n -> q a n").bitcast(I32),
-            )
-        nc.vector.memset(warm[:], 0.0)
-        nc.scalar.activation(out=warm[:, 0:1], in_=warm[:, 7:8], func=ACT.Sin)
+        tab_sc = tile([P, T], U8, "tab_sc", AT_TAB_SC)
+        w1_sc_raw = tile([P, PASSES * H // 4], I32, "w1_sc_raw", AT_V1)
+        v_sc = tile([P, PASSES * S], U8, "v_sc")
+        vec_ordered = tile([P, 4, P], F32, "vec_ordered")
+        ident = tile([P, P], F32, "ident")
+        zeros = tile([P, 16], F32, "zeros")
         tabs = []
 
-        def load_tab(a):
-            tab = big.tile([P, T], I32, name=f"tab{a}", tag="big", align_bytes=64)
-            nc.sync.dma_start(out=tab[:], in_=tab_words[a].rearrange("p t i -> p (t i)").bitcast(I32))
+        def load_tab(a, queue=nc.sync):
+            tab = tile([P, T], I32, f"tab{a}", (AT_TAB0, AT_TAB1, AT_TAB2)[a])
+            queue.dma_start(out=tab[:], in_=tab_words[a].rearrange("p t i -> p (t i)").bitcast(I32))
             tabs.append(tab)
 
-        load_tab(0)
-        load_tab(1)
+        nc.sync.dma_start(offs_sb[:], offs)
+        nc.sync.dma_start(out=tab_sc[LAST0:PAIR0, :].bitcast(I32), in_=tab_scales[2].bitcast(I32))
+        nc.sync.dma_start(
+            out=tab_sc[PAIR0:P, :].bitcast(I32), in_=tab_scales[0:2].rearrange("a q t -> q a t").bitcast(I32)
+        )
+        make_identity(nc, ident[:])
+        vec_rows = tile([P, 512], F32, "vec_rows")
         for v, vector in enumerate((phase, amp, mrg)):
             nc.gpsimd.dma_start(
                 out=vec_rows[GROUPS * v : GROUPS * (v + 1), :], in_=vector.rearrange("(b c) -> b c", b=GROUPS)
             )
         nc.sync.dma_start(pos1_sb[:], pos1)
         nc.sync.dma_start(pos2_sb[:], pos2)
+        load_tab(0)
+        w1_raw = []
 
-        for q in range(4):
-            nc.vector.memset(tab_sc[32 * q : 32 * q + ROW0, :].bitcast(I32), 0)
-        nc.vector.memset(v_sc[96:P, :].bitcast(I32), 0)
-        make_identity(nc, ident[:])
+        def load_w1(b, place):
+            raw = tile([P, PASSES, 256], I32, f"w1_raw{b}", place)
+            nc.sync.dma_start(out=raw[:], in_=w1_words.rearrange("a p (b c) -> b p a c", b=GROUPS)[b].bitcast(I32))
+            w1_raw.append(raw)
 
-        nc.vector.tensor_copy(
-            out=w1_codes[:].bitcast(I32).rearrange("p (b t g w) -> p b t g w", t=4, g=16, w=4),
-            in_=w1_raw[:].rearrange("p (b g t w) -> p b t g w", t=4, g=16, w=4),
-        )
+        load_w1(0, None)
+        nc.vector.memset(w1_sc_raw[:], 0)
+        nc.vector.memset(zeros[:], 0.0)
+        nc.vector.memset(tab_sc[0:64, :].bitcast(I32), 0)
+        nc.vector.memset(tab_sc[64:LAST0, :].bitcast(I32), 0)
+        nc.vector.memset(v_sc[:].bitcast(I32), 0)
+        for r in range(4):
+            nc.sync.dma_start(
+                out=w1_sc_raw[r:P:32, :].rearrange("p (a c) -> p a c", a=PASSES),
+                in_=w1_scales[:, r:16:4, :].rearrange("a q n -> q a n").bitcast(I32),
+            )
+        nc.scalar.activation(out=vec_ordered[:].rearrange("p t c -> p (t c)"), in_=zeros[:, 0:1].to_broadcast([P, 512]), func=ACT.Sin)
+        load_tab(1)
+
+        picked_sc = tile([P, S], U8, "picked_sc")
         nc.vector.tensor_copy(picked_sc[:], tab_sc[:].indirect(offs_sb[:]))
-        for a in range(PASSES):
-            first = ROW0 + 4 * a
-            nc.scalar.dma_start(
-                out=v_sc[0:SPAN, a * S : (a + 1) * S].bitcast(I32),
-                in_=picked_sc[first : first + SPAN, :].bitcast(I32),
+        for q in range(4):
+            nc.sync.dma_start(
+                out=v_sc[32 * q : 32 * q + 4, 0 : 2 * S].bitcast(I32),
+                in_=picked_sc[PAIR0 + 8 * q : PAIR0 + 8 * q + 8, :].bitcast(I32),
             )
         load_tab(2)
-        v_codes = [big.tile([P, S], U32, name=f"v_codes{a}", tag="late", align_bytes=64) for a in range(PASSES)]
-
-        def pick_codes(a, half):
-            nc.vector.tensor_copy(
-                v_codes[a][:, half * BANK : (half + 1) * BANK], tabs[a][:].bitcast(U32).indirect(offs_sb[:, 32 * half : 32 * (half + 1)])
+        for q in range(4):
+            nc.sync.dma_start(
+                out=v_sc[32 * q : 32 * q + 4, 2 * S :].bitcast(I32),
+                in_=picked_sc[LAST0 + 4 * q : LAST0 + 4 * q + 4, :].bitcast(I32),
             )
+        load_w1(1, AT_W1_REST_RAW)
 
-        pick_codes(0, 0)
+        v_codes = [tile([P, S], U32, f"v_codes{a}", (None, AT_V1, AT_V2)[a]) for a in range(PASSES)]
+
+        def pick_codes(a, pieces=1):
+            width = S // pieces
+            for piece in range(pieces):
+                first = piece * width
+                nc.vector.tensor_copy(
+                    v_codes[a][:, first : first + width],
+                    tabs[a][:].bitcast(U32).indirect(offs_sb[:, first // 16 : (first + width) // 16]),
+                )
+
+        pick_codes(0)
+        w1_sc = tile([P, PASSES * H], U8, "w1_sc", AT_W1_SC)
         nc.vector.tensor_copy(
             out=w1_sc[:].bitcast(I32).rearrange("p (b t g w) -> p b t g w", t=4, g=16, w=2),
             in_=w1_sc_raw[:].rearrange("p (b g t w) -> p b t g w", t=4, g=16, w=2),
         )
-        pick_codes(0, 1)
-        for half in range(2):
-            pick_codes(1, half)
-        nc.vector.tensor_copy(v_codes[2][:], tabs[2][:].bitcast(U32).indirect(offs_sb[:]))
+        w1_codes = {}
 
-        nc.scalar.copy(
-            out=vec_ordered[:].rearrange("p t (g i) -> p t g i", i=8),
-            in_=vec_rows[:].rearrange("p (g t i) -> p t g i", t=4, i=8),
-        )
-        vec_ps = psum.tile([P, 4, P], F32, name="vec_ps", tag="bank7")
-        for t in range(4):
-            nc.tensor.transpose(vec_ps[:, t, :], vec_ordered[:, t, :], ident[:])
-        nc.scalar.copy(out=vec[:, :, 0:6], in_=vec_ps[:, :, 0:6])
+        def order_w1(tiles, passes, place):
+            b, t0, count = tiles[0] // 4, tiles[0] % 4, len(tiles)
+            codes = tile([P, len(passes), count * P * 2], U8, f"w1_codes{tiles[0]}_{passes[0]}", place)
+            by_tile = w1_raw[b][:].rearrange("p a (g t w) -> p t a g w", t=4, w=4)
+            nc.vector.tensor_copy(
+                out=codes[:].bitcast(I32).rearrange("p a (t g w) -> p t a g w", t=count, w=4),
+                in_=by_tile[:, t0 : t0 + count, passes[0] : passes[-1] + 1],
+            )
+            for n, j in enumerate(tiles):
+                for m, a in enumerate(passes):
+                    w1_codes[(j, a)] = codes[:, m, 2 * n * P : 2 * (n + 1) * P]
+
+        order_w1([0, 1], [0, 1, 2], AT_W1_PAIR)
+        pick_codes(1)
+        pick_codes(2, pieces=2)
+        order_w1([2, 3], [0, 1, 2], AT_W1_PAIR)
+
+        vec = tile([P, 4, 8], F32, "vec")
+
+        def turn_vectors():
+            nc.scalar.copy(
+                out=vec_ordered[0:VEC_ROWS].rearrange("p t (g i) -> p t g i", i=8),
+                in_=vec_rows[0:VEC_ROWS].rearrange("p (g t i) -> p t g i", t=4, i=8),
+            )
+            vec_ps = psum.tile([P, 4, P], F32, name="vec_ps", tag="bank0")
+            for t in range(4):
+                nc.tensor.transpose(vec_ps[:, t, :], vec_ordered[:, t, :], ident[:])
+            nc.scalar.copy(out=vec[:, :, 0:VEC_ROWS], in_=vec_ps[:, :, 0:VEC_ROWS])
 
         def per_channel(v, j):
             col = GROUPS * v + j // 4
             return vec[:, j % 4, col : col + 1]
 
         w2_view = w2.rearrange("(b g t i) (c n) -> b c t g i n", b=GROUPS, g=16, t=4, c=GROUPS)
-        chunks = [(b, c) for c in range(GROUPS) for b in range(GROUPS)]
-        w2_raw = {}
+        w2_raw, w2_codes, w2_sc = {}, {}, {}
 
-        def load_w2(b, c):
-            raw = big.tile([P, 4, 512], F32, name=f"w2_raw{b}{c}", tag="big", align_bytes=64)
+        def load_w2(b, c, place, queue=nc.sync):
+            raw = tile([P, 4, 512], F32, f"w2_raw{b}{c}", place)
             for t in range(4):
-                nc.sync.dma_start(out=raw[:, t, :], in_=w2_view[b, c, t])
+                queue.dma_start(out=raw[:, t, :], in_=w2_view[b, c, t])
             w2_raw[(b, c)] = raw
 
-        for b, c in chunks[:PASSES]:
-            load_w2(b, c)
+        w2_grouped = {}
 
-        w2_codes, w2_sc, w2_grouped = {}, {}, {}
-
-        def quantize_w2(b, c):
-            if c == 0:
-                grouped = ring.tile([P, 4 * 512], BF16, name=f"w2_grouped{b}{c}", tag="grouped", bufs=3, align_bytes=64)
-            else:
-                grouped = big.tile([P, 4 * 512], BF16, name=f"w2_grouped{b}{c}", tag="late", align_bytes=64)
+        def group_w2(b, c, place, copy):
+            grouped = tile([P, 4 * 512], BF16, f"w2_grouped{b}{c}", place)
             dst = grouped[:].rearrange("p (u g e l t) -> p e g u t l", u=4, g=16, e=2, l=4)
             src = w2_raw[(b, c)][:].rearrange("p t (g u e l) -> p e g u t l", u=4, g=16, e=2)
             for e in range(2):
-                if c == 0:
-                    nc.vector.tensor_copy(out=dst[:, e], in_=src[:, e])
-                else:
-                    nc.scalar.copy(out=dst[:, e], in_=src[:, e])
-            codes = keep.tile([P, 512], U32, name=f"w2_codes{b}{c}", align_bytes=64)
-            scales = keep.tile([P, 512], U8, name=f"w2_sc{b}{c}", align_bytes=64)
-            nc.vector.quantize_mx(out=codes[:].bitcast(FP8X4), scales=scales[:], in_=grouped[:])
-            w2_codes[(b, c)] = codes
-            w2_sc[(b, c)] = scales
+                copy(out=dst[:, e], in_=src[:, e])
             w2_grouped[(b, c)] = grouped
 
-        quantize_w2(*chunks[0])
-        load_w2(*chunks[3])
+        def quantize_w2(b, c, place):
+            codes = tile([P, 512], U32, f"w2_codes{b}{c}", place)
+            scales = tile([P, 512], U8, f"w2_sc{b}{c}")
+            nc.vector.quantize_mx(out=codes[:].bitcast(FP8X4), scales=scales[:], in_=w2_grouped[(b, c)][:])
+            w2_codes[(b, c)] = codes
+            w2_sc[(b, c)] = scales
 
-        h = [keep.tile([P, S], F32, name=f"h{j}") for j in range(TILES)]
-        theme = [keep.tile([P, NP], F32, name=f"theme{j}") for j in range(TILES)]
-        sine = [keep.tile([P, NP], F32, name=f"sine{j}") for j in range(TILES)]
-        z_rows = [keep.tile([P, 4, NP], BF16, name=f"z_rows{b}", align_bytes=64) for b in range(GROUPS)]
-        z_codes = [keep.tile([P, NP], U32, name=f"z_codes{b}", align_bytes=64) for b in range(GROUPS)]
-        z_sc = [keep.tile([P, NP], U8, name=f"z_sc{b}", align_bytes=64) for b in range(GROUPS)]
+        load_w2(0, 0, AT_W2_00)
+        load_w2(1, 0, AT_W2_10)
+        load_w2(0, 1, AT_W2_01)
+        group_w2(0, 0, None, nc.vector.tensor_copy)
+        order_w1([4, 5, 6, 7], [0, 1, 2], AT_TAB2 + 5120)
+        load_w2(1, 1, AT_W2_00)
 
-        def scale_by_amp(j):
-            row = z_rows[j // 4][:, j % 4, :]
-            if j < 4:
-                nc.scalar.activation(out=row, in_=sine[j][:], func=ACT.Copy, scale=per_channel(1, j))
-            else:
-                nc.vector.tensor_scalar(out=row, in0=sine[j][:], scalar1=per_channel(1, j), scalar2=None, op0=ALU.mult)
-
-        z_grouped = {}
-
-        def group_z(b):
-            grouped = ring.tile([P, 4 * NP], BF16, name=f"z_grouped{b}", tag="grouped", bufs=3, align_bytes=64)
-            nc.vector.tensor_copy(
-                out=grouped[:].rearrange("p (c i t) -> p c t i", i=4, t=4),
-                in_=z_rows[b][:].rearrange("p t (c i) -> p c t i", i=4),
-            )
-            z_grouped[b] = grouped
-
-        def quantize_z(b):
-            nc.vector.quantize_mx(out=z_codes[b][:].bitcast(FP8X4), scales=z_sc[b][:], in_=z_grouped[b][:])
+        h = [tile([P, S], F32, f"h{j}") for j in range(TILES)]
+        theme = [tile([P, NP], F32, f"theme{j}") for j in range(TILES)]
 
         def new_banks(j):
             return [
@@ -207,51 +217,83 @@ def tile_list_passacaglia_variation_surprise_kernel(
             ]
 
         def first_stage_pass(bank, j, a, half):
+            cols = slice(half * BANK, (half + 1) * BANK)
             nc.tensor.matmul_mx(
                 out=bank[:],
-                lhsT=w1_codes[:, 2 * (a * H + j * P) : 2 * (a * H + (j + 1) * P)].bitcast(FP4X4),
+                lhsT=w1_codes[(j, a)].bitcast(FP4X4),
                 lhsT_scale=w1_sc[:, a * H + j * P : a * H + (j + 1) * P],
-                rhs=v_codes[a][:, half * BANK : (half + 1) * BANK].bitcast(FP8X4),
+                rhs=v_codes[a][:, cols].bitcast(FP8X4),
                 rhs_scale=v_sc[:, a * S + half * BANK : a * S + (half + 1) * BANK],
                 start=(a == 0),
                 stop=(a == PASSES - 1),
             )
 
-        def pick_theme(j, banks):
-            for half in range(2):
-                if j == 0 and half == 1:
-                    nc.vector.tensor_copy(out=h[j][:, half * BANK : (half + 1) * BANK], in_=banks[half][:])
-                else:
-                    nc.scalar.copy(out=h[j][:, half * BANK : (half + 1) * BANK], in_=banks[half][:])
+        def empty_bank(j, banks, half):
+            nc.scalar.copy(out=h[j][:, half * BANK : (half + 1) * BANK], in_=banks[half][:])
+
+        def pick_theme(j):
             nc.vector.tensor_copy(theme[j][:], h[j][:].indirect(pos1_sb[:]))
 
-        early = [new_banks(j) for j in range(4)]
+        early = [new_banks(j) for j in range(2)]
         for a in range(PASSES):
-            for j in range(4):
-                for half in range(2):
+            for half in range(2):
+                for j in range(2):
                     first_stage_pass(early[j][half], j, a, half)
-        for j in range(4):
-            pick_theme(j, early[j])
-        for j in range(4, TILES):
+                    if a == PASSES - 1:
+                        empty_bank(j, early[j], half)
+        for j in range(2):
+            pick_theme(j)
+        turn_vectors()
+        for j in range(2, TILES):
             banks = new_banks(j)
             for half in range(2):
                 for a in range(PASSES):
                     first_stage_pass(banks[half], j, a, half)
-            pick_theme(j, banks)
+                empty_bank(j, banks, half)
+            pick_theme(j)
+
+        z_rows = [tile([P, 4, NP], BF16, f"z_rows{b}") for b in range(GROUPS)]
+        z_codes = [tile([P, NP], U32, f"z_codes{b}") for b in range(GROUPS)]
+        z_sc = [tile([P, NP], U8, f"z_sc{b}") for b in range(GROUPS)]
+
+        sines = {}
+
+        def take_sine(j):
+            sines[j] = tile([P, NP], F32, f"sine{j}", AT_SINE[j % 2])
+            nc.scalar.activation(out=sines[j][:], in_=theme[j][:], func=ACT.Sin, bias=per_channel(0, j))
+
+        def scale_by_amp(j):
+            nc.scalar.activation(out=z_rows[j // 4][:, j % 4, :], in_=sines[j][:], func=ACT.Copy, scale=per_channel(1, j))
+
+        def quantize_z(b):
+            grouped = tile([P, 4 * NP], BF16, f"z_grouped{b}", AT_Z_GROUPED1 if b else None)
+            nc.vector.tensor_copy(
+                out=grouped[:].rearrange("p (c i t) -> p c t i", i=4, t=4),
+                in_=z_rows[b][:].rearrange("p t (c i) -> p c t i", i=4),
+            )
+            quantize_w2(b, 0, f"z_rows{b}")
+            nc.vector.quantize_mx(out=z_codes[b][:].bitcast(FP8X4), scales=z_sc[b][:], in_=grouped[:])
+
+        take_sine(0)
         for j in range(TILES):
-            nc.scalar.activation(out=sine[j][:], in_=theme[j][:], func=ACT.Sin, bias=per_channel(0, j))
+            if j + 1 < TILES:
+                take_sine(j + 1)
             scale_by_amp(j)
             if j == 3:
-                group_z(0)
                 quantize_z(0)
-        group_z(1)
+        group_w2(1, 0, "theme1", nc.vector.tensor_copy)
+        group_w2(0, 1, "theme3", nc.vector.tensor_copy)
+        quantize_w2(0, 1, "z_grouped0")
         quantize_z(1)
+        group_w2(1, 1, AT_SINE[1], nc.scalar.copy)
 
         out_view = out.rearrange("(b g t i) m -> b t g i m", b=GROUPS, g=16, t=4)
+        y_place = [None, "y1", "y2", "y3", "diff1", "y5", "diff2", "diff3"]
+        y_of = {}
 
         def predict(j):
             c, u = j // 4, j % 4
-            y = psum.tile([P, NP], F32, name=f"y{j}", tag=f"bank{j}")
+            y = psum.tile([P, NP], F32, name=f"y{j}", tag=f"bank{(j + 4) % TILES}")
             for b in range(GROUPS):
                 nc.tensor.matmul_mx(
                     out=y[:],
@@ -262,25 +304,66 @@ def tile_list_passacaglia_variation_surprise_kernel(
                     start=(b == 0),
                     stop=(b == GROUPS - 1),
                 )
-            nc.scalar.copy(out=theme[j][:], in_=y[:])
+            y_of[j] = y
+            if j > 0:
+                y_of[j] = tile([P, NP], F32, f"y_sb{j}", y_place[j])
+                nc.scalar.copy(out=y_of[j][:], in_=y[:])
 
-        quantize_w2(*chunks[1])
-        quantize_w2(*chunks[2])
+        diffs = {}
+
+        def subtract(j, cols=slice(0, NP)):
+            if j not in diffs:
+                diffs[j] = tile([P, NP], F32, f"diff{j}")
+            picks = pos2_sb[:, cols.start // 16 : cols.stop // 16]
+            nc.vector.tensor_tensor(
+                out=diffs[j][:, cols], in0=h[j][:].indirect(picks), in1=y_of[j][:, cols], op=ALU.subtract
+            )
+
+        squares = {}
+
+        def square_on_scalar(j):
+            squares[j] = tile([P, NP], F32, f"square{j}", f"square{j % 3}")
+            nc.scalar.activation(out=squares[j][:], in_=diffs[j][:], func=ACT.Square)
+
+        def weigh_on_scalar(j):
+            mark = tile([P, NP], F32, f"mark{j}")
+            nc.scalar.activation(out=mark[:], in_=squares[j][:], func=ACT.Copy, scale=per_channel(2, j))
+            nc.sync.dma_start(out=out_view[j // 4, j % 4], in_=mark[:])
+
+        def finish_on_vector(j, cols=slice(0, NP), queue=nc.sync):
+            mark = tile([P, cols.stop - cols.start], F32, f"mark{j}_{cols.start}")
+            diff = diffs[j][:, cols]
+            nc.vector.scalar_tensor_tensor(
+                out=mark[:], in0=diff, scalar=per_channel(2, j), in1=diff, op0=ALU.mult, op1=ALU.mult
+            )
+            queue.dma_start(out=out_view[j // 4, j % 4][:, :, cols], in_=mark[:])
+
         for j in range(4):
             predict(j)
-        quantize_w2(*chunks[3])
-        for j in range(4, TILES):
+        actual = tile([P, NP], F32, "actual0", AT_Z_GROUPED1)
+        nc.vector.tensor_copy(actual[:], h[0][:].indirect(pos2_sb[:]))
+        quantize_w2(1, 1, AT_Z_GROUPED1 + 2048)
+        diffs[0] = tile([P, NP], F32, "diff0")
+        nc.vector.tensor_tensor(out=diffs[0][:], in0=actual[:], in1=y_of[0][:], op=ALU.subtract)
+        square_on_scalar(0)
+        subtract(1)
+        square_on_scalar(1)
+        weigh_on_scalar(0)
+        for j in range(4, 6):
             predict(j)
-        for j in range(TILES):
-            diff = ring.tile([P, NP], F32, name=f"diff{j}", tag="diff", bufs=5)
-            nc.vector.tensor_tensor(out=diff[:], in0=h[j][:].indirect(pos2_sb[:]), in1=theme[j][:], op=ALU.subtract)
-            mark = ring.tile([P, NP], F32, name=f"mark{j}", tag="mark", bufs=TILES)
-            if j < TILES - 1:
-                square = ring.tile([P, NP], F32, name=f"square{j}", tag="square")
-                nc.scalar.activation(out=square[:], in_=diff[:], func=ACT.Square)
-                nc.scalar.activation(out=mark[:], in_=square[:], func=ACT.Copy, scale=per_channel(2, j))
-            else:
-                nc.vector.scalar_tensor_tensor(
-                    out=mark[:], in0=diff[:], scalar=per_channel(2, j), in1=diff[:], op0=ALU.mult, op1=ALU.mult
-                )
-            nc.sync.dma_start(out=out_view[j // 4, j % 4], in_=mark[:])
+        for j in range(2, 5):
+            subtract(j)
+            square_on_scalar(j)
+            weigh_on_scalar(j - 1)
+            if j < 4:
+                predict(j + 4)
+        weigh_on_scalar(4)
+        halves = [slice(0, 3 * NP // 4), slice(3 * NP // 4, NP)]
+        subtract(5)
+        subtract(6)
+        finish_on_vector(5)
+        subtract(7, halves[0])
+        finish_on_vector(6)
+        subtract(7, halves[1])
+        finish_on_vector(7, halves[0])
+        finish_on_vector(7, halves[1], nc.scalar)

@@ -74,8 +74,8 @@ def tile_list_passacaglia_variation_surprise_kernel(
             tabs.append(tab)
 
         nc.sync.dma_start(offs_sb[:], offs)
-        nc.sync.dma_start(out=tab_sc[LAST0:PAIR0, :].bitcast(I32), in_=tab_scales[2].bitcast(I32))
-        nc.sync.dma_start(
+        nc.scalar.dma_start(out=tab_sc[LAST0:PAIR0, :].bitcast(I32), in_=tab_scales[2].bitcast(I32))
+        nc.scalar.dma_start(
             out=tab_sc[PAIR0:P, :].bitcast(I32), in_=tab_scales[0:2].rearrange("a q t -> q a t").bitcast(I32)
         )
         make_identity(nc, ident[:])
@@ -97,8 +97,7 @@ def tile_list_passacaglia_variation_surprise_kernel(
         load_w1(0, None)
         nc.vector.memset(w1_sc_raw[:], 0)
         nc.vector.memset(zeros[:], 0.0)
-        nc.vector.memset(tab_sc[0:64, :].bitcast(I32), 0)
-        nc.vector.memset(tab_sc[64:LAST0, :].bitcast(I32), 0)
+        nc.vector.memset(tab_sc[0:LAST0, :].bitcast(I32), 0)
         nc.vector.memset(v_sc[:].bitcast(I32), 0)
         for r in range(4):
             nc.sync.dma_start(
@@ -204,9 +203,7 @@ def tile_list_passacaglia_variation_surprise_kernel(
         load_w2(0, 0, AT_W2_00)
         load_w2(1, 0, AT_W2_10)
         load_w2(0, 1, AT_W2_01)
-        group_w2(0, 0, None, nc.vector.tensor_copy)
         order_w1([4, 5, 6, 7], [0, 1, 2], AT_TAB2 + 5120)
-        load_w2(1, 1, AT_W2_00)
 
         h = [tile([P, S], F32, f"h{j}") for j in range(TILES)]
         theme = [tile([P, NP], F32, f"theme{j}") for j in range(TILES)]
@@ -275,14 +272,16 @@ def tile_list_passacaglia_variation_surprise_kernel(
             nc.vector.quantize_mx(out=z_codes[b][:].bitcast(FP8X4), scales=z_sc[b][:], in_=grouped[:])
 
         take_sine(0)
+        group_w2(0, 0, "theme0", nc.vector.tensor_copy)
+        load_w2(1, 1, AT_W2_00)
         for j in range(TILES):
             if j + 1 < TILES:
                 take_sine(j + 1)
             scale_by_amp(j)
             if j == 3:
                 quantize_z(0)
-        group_w2(1, 0, "theme1", nc.vector.tensor_copy)
-        group_w2(0, 1, "theme3", nc.vector.tensor_copy)
+        group_w2(1, 0, "theme2", nc.vector.tensor_copy)
+        group_w2(0, 1, "theme4", nc.vector.tensor_copy)
         quantize_w2(0, 1, "z_grouped0")
         quantize_z(1)
         group_w2(1, 1, AT_SINE[1], nc.scalar.copy)

@@ -37,7 +37,6 @@ AT_W1_SC = AT_TAB0 + 64
 AT_W1_PAIR = AT_TAB0 + 5184
 AT_SINE = [AT_W1_PAIR + 512 - 2048, AT_W1_PAIR + 512]
 AT_V1 = AT_SINE[1] + 4096
-AT_Z_GROUPED1 = AT_V1 + 4096
 VEC_ROWS = 3 * GROUPS
 
 
@@ -187,10 +186,10 @@ def tile_list_passacaglia_variation_surprise_kernel(
 
         def group_w2(b, c, place, copy):
             grouped = tile([P, 4 * 512], BF16, f"w2_grouped{b}{c}", place)
-            dst = grouped[:].rearrange("p (u g e l t) -> p e g u t l", u=4, g=16, e=2, l=4)
-            src = w2_raw[(b, c)][:].rearrange("p t (g u e l) -> p e g u t l", u=4, g=16, e=2)
-            for e in range(2):
-                copy(out=dst[:, e], in_=src[:, e])
+            dst = grouped[:].rearrange("p (u g e l t) -> p u g e t l", u=4, g=16, e=2, l=4)
+            src = w2_raw[(b, c)][:].rearrange("p t (g u e l) -> p u g e t l", u=4, g=16, e=2)
+            for u in range(4):
+                copy(out=dst[:, u], in_=src[:, u])
             w2_grouped[(b, c)] = grouped
 
         def quantize_w2(b, c, place):
@@ -203,7 +202,7 @@ def tile_list_passacaglia_variation_surprise_kernel(
         load_w2(0, 0, AT_W2_00)
         load_w2(1, 0, AT_W2_10)
         load_w2(0, 1, AT_W2_01)
-        order_w1([4, 5, 6, 7], [0, 1, 2], AT_TAB2 + 5120)
+        order_w1([4, 5, 6, 7], [0, 1, 2], AT_TAB1 + 1024)
 
         h = [tile([P, S], F32, f"h{j}") for j in range(TILES)]
         theme = [tile([P, NP], F32, f"theme{j}") for j in range(TILES)]
@@ -263,13 +262,20 @@ def tile_list_passacaglia_variation_surprise_kernel(
             nc.scalar.activation(out=z_rows[j // 4][:, j % 4, :], in_=sines[j][:], func=ACT.Copy, scale=per_channel(1, j))
 
         def quantize_z(b):
-            grouped = tile([P, 4 * NP], BF16, f"z_grouped{b}", AT_Z_GROUPED1 if b else None)
-            nc.vector.tensor_copy(
-                out=grouped[:].rearrange("p (c i t) -> p c t i", i=4, t=4),
-                in_=z_rows[b][:].rearrange("p t (c i) -> p c t i", i=4),
-            )
-            quantize_w2(b, 0, f"z_rows{b}")
-            nc.vector.quantize_mx(out=z_codes[b][:].bitcast(FP8X4), scales=z_sc[b][:], in_=grouped[:])
+            width = NP // 2
+            grouped = []
+            for half in range(2):
+                part = tile([P, 4 * width], BF16, f"z_grouped{b}_{half}")
+                nc.vector.tensor_copy(
+                    out=part[:].rearrange("p (c i t) -> p c t i", i=4, t=4),
+                    in_=z_rows[b][:, :, half * width : (half + 1) * width].rearrange("p t (c i) -> p c t i", i=4),
+                )
+                grouped.append(part)
+            for half in range(2):
+                cols = slice(half * width, (half + 1) * width)
+                nc.vector.quantize_mx(
+                    out=z_codes[b][:, cols].bitcast(FP8X4), scales=z_sc[b][:, cols], in_=grouped[half][:]
+                )
 
         take_sine(0)
         group_w2(0, 0, "theme0", nc.vector.tensor_copy)
@@ -280,9 +286,11 @@ def tile_list_passacaglia_variation_surprise_kernel(
             scale_by_amp(j)
             if j == 3:
                 quantize_z(0)
+                quantize_w2(0, 0, "z_grouped0_0")
         group_w2(1, 0, "theme2", nc.vector.tensor_copy)
         group_w2(0, 1, "theme4", nc.vector.tensor_copy)
-        quantize_w2(0, 1, "z_grouped0")
+        quantize_w2(1, 0, "theme7")
+        quantize_w2(0, 1, "theme6")
         quantize_z(1)
         group_w2(1, 1, AT_SINE[1], nc.scalar.copy)
 
@@ -339,9 +347,9 @@ def tile_list_passacaglia_variation_surprise_kernel(
 
         for j in range(4):
             predict(j)
-        actual = tile([P, NP], F32, "actual0", AT_Z_GROUPED1)
+        actual = tile([P, NP], F32, "actual0", "z_grouped1_0")
         nc.vector.tensor_copy(actual[:], h[0][:].indirect(pos2_sb[:]))
-        quantize_w2(1, 1, AT_Z_GROUPED1 + 2048)
+        quantize_w2(1, 1, "z_grouped1_1")
         diffs[0] = tile([P, NP], F32, "diff0")
         nc.vector.tensor_tensor(out=diffs[0][:], in0=actual[:], in1=y_of[0][:], op=ALU.subtract)
         square_on_scalar(0)

@@ -24,20 +24,28 @@ TILES = H // P
 BANK = 512
 LAST0 = P - 16 * PASSES
 PAIR0 = LAST0 + 16
-AT_W2_01 = 0
-AT_TAB2 = 7680
-AT_TAB_SC = 15360
-AT_W1_REST_RAW = 16896
-AT_W2_10 = 20992
-AT_TAB1 = AT_W2_10 + 8192 - 64
-AT_V2 = AT_TAB1 + 5184
-AT_W2_00 = AT_V2 + 4096
-AT_TAB0 = AT_W2_00 + 8192 - 64
-AT_W1_SC = AT_TAB0 + 64
-AT_W1_PAIR = AT_TAB0 + 5184
-AT_SINE = [AT_W1_PAIR + 512 - 2048, AT_W1_PAIR + 512]
-AT_V1 = AT_SINE[1] + 4096
 VEC_ROWS = 3 * GROUPS
+VEC0 = 96
+LAP = 64
+CODE_BYTES = PASSES * 2 * P
+AT_TAB0 = 0
+AT_TAB1 = 8192
+AT_TAB2 = 16384
+AT_TAB_SC = AT_TAB2 + 8192 - LAP
+CHAIN0 = AT_TAB_SC + 2048 + 3072
+STEP = 2048 + CODE_BYTES + 4096
+
+
+def at_codes(j):
+    return CHAIN0 + (j - 2) * STEP + 2048 - LAP
+
+
+def at_sine(j):
+    return CHAIN0 + j * STEP
+
+
+def after_codes(j):
+    return at_codes(j) + CODE_BYTES - LAP
 
 
 def tile_list_passacaglia_variation_surprise_kernel(
@@ -60,16 +68,14 @@ def tile_list_passacaglia_variation_surprise_kernel(
         pos2_sb = lists.tile([P, NP // 16], U16, name="pos2_sb")
 
         tab_sc = tile([P, T], U8, "tab_sc", AT_TAB_SC)
-        w1_sc_raw = tile([P, PASSES * H // 4], I32, "w1_sc_raw", AT_V1)
         v_sc = tile([P, PASSES * S], U8, "v_sc")
-        vec_ordered = tile([P, 4, P], F32, "vec_ordered")
         ident = tile([P, P], F32, "ident")
         zeros = tile([P, 16], F32, "zeros")
         tabs = []
 
-        def load_tab(a, queue=nc.sync):
+        def load_tab(a):
             tab = tile([P, T], I32, f"tab{a}", (AT_TAB0, AT_TAB1, AT_TAB2)[a])
-            queue.dma_start(out=tab[:], in_=tab_words[a].rearrange("p t i -> p (t i)").bitcast(I32))
+            nc.sync.dma_start(out=tab[:], in_=tab_words[a].rearrange("p t i -> p (t i)").bitcast(I32))
             tabs.append(tab)
 
         nc.sync.dma_start(offs_sb[:], offs)
@@ -77,33 +83,38 @@ def tile_list_passacaglia_variation_surprise_kernel(
         nc.scalar.dma_start(
             out=tab_sc[PAIR0:P, :].bitcast(I32), in_=tab_scales[0:2].rearrange("a q t -> q a t").bitcast(I32)
         )
-        make_identity(nc, ident[:])
         vec_rows = tile([P, 512], F32, "vec_rows")
+        nc.gpsimd.memset(vec_rows[VEC0:P, :], 0.0)
         for v, vector in enumerate((phase, amp, mrg)):
             nc.gpsimd.dma_start(
-                out=vec_rows[GROUPS * v : GROUPS * (v + 1), :], in_=vector.rearrange("(b c) -> b c", b=GROUPS)
+                out=vec_rows[VEC0 + GROUPS * v : VEC0 + GROUPS * (v + 1), :], in_=vector.rearrange("(b c) -> b c", b=GROUPS)
             )
+        make_identity(nc, ident[:])
         nc.sync.dma_start(pos1_sb[:], pos1)
-        nc.sync.dma_start(pos2_sb[:], pos2)
         load_tab(0)
+        nc.sync.dma_start(pos2_sb[:], pos2)
         w1_raw = []
+        w1_sc_raw = tile([P, PASSES * 128], I32, "w1_sc_raw")
 
         def load_w1(b, place):
             raw = tile([P, PASSES, 256], I32, f"w1_raw{b}", place)
             nc.sync.dma_start(out=raw[:], in_=w1_words.rearrange("a p (b c) -> b p a c", b=GROUPS)[b].bitcast(I32))
             w1_raw.append(raw)
 
+        def load_w1_scales(b):
+            for r in range(4):
+                nc.sync.dma_start(
+                    out=w1_sc_raw[r:P:32, :].rearrange("p (a c) -> p a c", a=PASSES),
+                    in_=w1_scales[:, r:16:4, b * 512 : (b + 1) * 512].rearrange("a q n -> q a n").bitcast(I32),
+                )
+
         load_w1(0, None)
         nc.vector.memset(w1_sc_raw[:], 0)
+        load_w1_scales(0)
         nc.vector.memset(zeros[:], 0.0)
         nc.vector.memset(tab_sc[0:LAST0, :].bitcast(I32), 0)
         nc.vector.memset(v_sc[:].bitcast(I32), 0)
-        for r in range(4):
-            nc.sync.dma_start(
-                out=w1_sc_raw[r:P:32, :].rearrange("p (a c) -> p a c", a=PASSES),
-                in_=w1_scales[:, r:16:4, :].rearrange("a q n -> q a n").bitcast(I32),
-            )
-        nc.scalar.activation(out=vec_ordered[:].rearrange("p t c -> p (t c)"), in_=zeros[:, 0:1].to_broadcast([P, 512]), func=ACT.Sin)
+        nc.scalar.activation(out=vec_rows[0:VEC0, :], in_=zeros[0:VEC0, 0:1].to_broadcast([VEC0, 512]), func=ACT.Sin)
         load_tab(1)
 
         picked_sc = tile([P, S], U8, "picked_sc")
@@ -119,9 +130,9 @@ def tile_list_passacaglia_variation_surprise_kernel(
                 out=v_sc[32 * q : 32 * q + 4, 2 * S :].bitcast(I32),
                 in_=picked_sc[LAST0 + 4 * q : LAST0 + 4 * q + 4, :].bitcast(I32),
             )
-        load_w1(1, AT_W1_REST_RAW)
+        load_w1(1, AT_TAB_SC + 2048 - LAP)
 
-        v_codes = [tile([P, S], U32, f"v_codes{a}", (None, AT_V1, AT_V2)[a]) for a in range(PASSES)]
+        v_codes = [tile([P, S], U32, f"v_codes{a}") for a in range(PASSES)]
 
         def pick_codes(a, pieces=1):
             width = S // pieces
@@ -133,56 +144,56 @@ def tile_list_passacaglia_variation_surprise_kernel(
                 )
 
         pick_codes(0)
-        w1_sc = tile([P, PASSES * H], U8, "w1_sc", AT_W1_SC)
-        nc.vector.tensor_copy(
-            out=w1_sc[:].bitcast(I32).rearrange("p (b t g w) -> p b t g w", t=4, g=16, w=2),
-            in_=w1_sc_raw[:].rearrange("p (b g t w) -> p b t g w", t=4, g=16, w=2),
-        )
-        w1_codes = {}
-
-        def order_w1(tiles, passes, place):
-            b, t0, count = tiles[0] // 4, tiles[0] % 4, len(tiles)
-            codes = tile([P, len(passes), count * P * 2], U8, f"w1_codes{tiles[0]}_{passes[0]}", place)
-            by_tile = w1_raw[b][:].rearrange("p a (g t w) -> p t a g w", t=4, w=4)
-            nc.vector.tensor_copy(
-                out=codes[:].bitcast(I32).rearrange("p a (t g w) -> p t a g w", t=count, w=4),
-                in_=by_tile[:, t0 : t0 + count, passes[0] : passes[-1] + 1],
-            )
-            for n, j in enumerate(tiles):
-                for m, a in enumerate(passes):
-                    w1_codes[(j, a)] = codes[:, m, 2 * n * P : 2 * (n + 1) * P]
-
-        order_w1([0, 1], [0, 1, 2], AT_W1_PAIR)
         pick_codes(1)
         pick_codes(2, pieces=2)
-        order_w1([2, 3], [0, 1, 2], AT_W1_PAIR)
 
-        vec = tile([P, 4, 8], F32, "vec")
+        w1_codes, w1_sc = {}, []
 
-        def turn_vectors():
-            nc.scalar.copy(
-                out=vec_ordered[0:VEC_ROWS].rearrange("p t (g i) -> p t g i", i=8),
-                in_=vec_rows[0:VEC_ROWS].rearrange("p (g t i) -> p t g i", t=4, i=8),
+        def order_scales(b, copy, view):
+            sc = tile([P, PASSES * 512], U8, f"w1_sc{b}", AT_TAB_SC + LAP if b == 0 else None)
+            copy(
+                out=sc[:].bitcast(view).rearrange("p (a t g w) -> p a t g w", t=4, g=16, w=2),
+                in_=w1_sc_raw[:].bitcast(view).rearrange("p (a g t w) -> p a t g w", t=4, g=16, w=2),
             )
-            vec_ps = psum.tile([P, 4, P], F32, name="vec_ps", tag="bank0")
-            for t in range(4):
-                nc.tensor.transpose(vec_ps[:, t, :], vec_ordered[:, t, :], ident[:])
-            nc.scalar.copy(out=vec[:, :, 0:VEC_ROWS], in_=vec_ps[:, :, 0:VEC_ROWS])
+            w1_sc.append(sc)
+
+        def order_codes(j, copy, view):
+            codes = tile([P, CODE_BYTES], U8, f"w1_codes{j}", at_codes(j) if j >= 2 else None)
+            by_tile = w1_raw[j // 4][:].bitcast(view).rearrange("p a (g t w) -> p t a g w", t=4, w=4)
+            copy(out=codes[:].bitcast(view).rearrange("p (a g w) -> p a g w", a=PASSES, w=4), in_=by_tile[:, j % 4])
+            w1_codes[j] = codes
+
+        for j in range(4):
+            order_codes(j, nc.scalar.copy, U32)
+        vec = tile([P, 4, 8], F32, "vec")
+        vec_ordered = tile([P, 4, P], F32, "vec_ordered", "w1_raw0")
+        nc.scalar.copy(
+            out=vec_ordered[:].rearrange("p t (g i) -> p t g i", i=8),
+            in_=vec_rows[:].rearrange("p (g t i) -> p t g i", t=4, i=8),
+        )
+        vec_ps = psum.tile([P, 4, P], F32, name="vec_ps", tag="bank4")
+        for t in range(4):
+            nc.tensor.transpose(vec_ps[:, t, :], vec_ordered[:, t, :], ident[:])
+        order_scales(0, nc.scalar.copy, U32)
+        load_w1_scales(1)
+        nc.scalar.copy(out=vec[:, :, 0:VEC_ROWS], in_=vec_ps[:, :, VEC0 : VEC0 + VEC_ROWS])
 
         def per_channel(v, j):
             col = GROUPS * v + j // 4
             return vec[:, j % 4, col : col + 1]
 
-        w2_view = w2.rearrange("(b g t i) (c n) -> b c t g i n", b=GROUPS, g=16, t=4, c=GROUPS)
-        w2_raw, w2_codes, w2_sc = {}, {}, {}
+        for j in range(4, TILES):
+            order_codes(j, nc.vector.tensor_copy, I32)
+        order_scales(1, nc.vector.tensor_copy, I32)
 
-        def load_w2(b, c, place, queue=nc.sync):
+        w2_view = w2.rearrange("(b g t i) (c n) -> b c t g i n", b=GROUPS, g=16, t=4, c=GROUPS)
+        w2_raw, w2_grouped, w2_codes, w2_sc = {}, {}, {}, {}
+
+        def load_w2(b, c, place):
             raw = tile([P, 4, 512], F32, f"w2_raw{b}{c}", place)
             for t in range(4):
-                queue.dma_start(out=raw[:, t, :], in_=w2_view[b, c, t])
+                nc.sync.dma_start(out=raw[:, t, :], in_=w2_view[b, c, t])
             w2_raw[(b, c)] = raw
-
-        w2_grouped = {}
 
         def group_w2(b, c, place, copy):
             grouped = tile([P, 4 * 512], BF16, f"w2_grouped{b}{c}", place)
@@ -199,104 +210,115 @@ def tile_list_passacaglia_variation_surprise_kernel(
             w2_codes[(b, c)] = codes
             w2_sc[(b, c)] = scales
 
-        load_w2(0, 0, AT_W2_00)
-        load_w2(1, 0, AT_W2_10)
-        load_w2(0, 1, AT_W2_01)
-        order_w1([4, 5, 6, 7], [0, 1, 2], AT_TAB1 + 1024)
+        load_w2(0, 0, AT_TAB0)
+        load_w2(1, 0, AT_TAB1)
+        load_w2(0, 1, AT_TAB2)
 
         h = [tile([P, S], F32, f"h{j}") for j in range(TILES)]
-        theme = [tile([P, NP], F32, f"theme{j}") for j in range(TILES)]
+        theme, sines, banks = {}, {}, {}
+        z_rows = [tile([P, 4, NP], BF16, f"z_rows{b}") for b in range(GROUPS)]
+        z_codes = [tile([P, NP], U32, f"z_codes{b}") for b in range(GROUPS)]
+        z_sc = [tile([P, NP], U8, f"z_sc{b}") for b in range(GROUPS)]
 
-        def new_banks(j):
-            return [
-                psum.tile([P, BANK], F32, name=f"h_ps{j}_{half}", tag=f"bank{2 * (j % 4) + half}") for half in range(2)
-            ]
-
-        def first_stage_pass(bank, j, a, half):
-            cols = slice(half * BANK, (half + 1) * BANK)
+        def first_stage_pass(j, half, a):
+            if a == 0:
+                slot = 2 * half + j if j < 2 else (2 * j + half) % 4
+                banks[(j, half)] = psum.tile([P, BANK], F32, name=f"h_ps{j}_{half}", tag=f"bank{slot}")
+            at = a * 512 + (j % 4) * P
             nc.tensor.matmul_mx(
-                out=bank[:],
-                lhsT=w1_codes[(j, a)].bitcast(FP4X4),
-                lhsT_scale=w1_sc[:, a * H + j * P : a * H + (j + 1) * P],
-                rhs=v_codes[a][:, cols].bitcast(FP8X4),
+                out=banks[(j, half)][:],
+                lhsT=w1_codes[j][:, 2 * a * P : 2 * (a + 1) * P].bitcast(FP4X4),
+                lhsT_scale=w1_sc[j // 4][:, at : at + P],
+                rhs=v_codes[a][:, half * BANK : (half + 1) * BANK].bitcast(FP8X4),
                 rhs_scale=v_sc[:, a * S + half * BANK : a * S + (half + 1) * BANK],
                 start=(a == 0),
                 stop=(a == PASSES - 1),
             )
 
-        def empty_bank(j, banks, half):
-            nc.scalar.copy(out=h[j][:, half * BANK : (half + 1) * BANK], in_=banks[half][:])
+        def empty_bank(j, half):
+            nc.scalar.copy(out=h[j][:, half * BANK : (half + 1) * BANK], in_=banks[(j, half)][:])
+
+        def fill_bank(j, half):
+            for a in range(PASSES):
+                first_stage_pass(j, half, a)
+            empty_bank(j, half)
 
         def pick_theme(j):
+            theme[j] = tile([P, NP], F32, f"theme{j}")
             nc.vector.tensor_copy(theme[j][:], h[j][:].indirect(pos1_sb[:]))
 
-        early = [new_banks(j) for j in range(2)]
-        for a in range(PASSES):
-            for half in range(2):
-                for j in range(2):
-                    first_stage_pass(early[j][half], j, a, half)
-                    if a == PASSES - 1:
-                        empty_bank(j, early[j], half)
-        for j in range(2):
-            pick_theme(j)
-        turn_vectors()
-        for j in range(2, TILES):
-            banks = new_banks(j)
-            for half in range(2):
-                for a in range(PASSES):
-                    first_stage_pass(banks[half], j, a, half)
-                empty_bank(j, banks, half)
-            pick_theme(j)
-
-        z_rows = [tile([P, 4, NP], BF16, f"z_rows{b}") for b in range(GROUPS)]
-        z_codes = [tile([P, NP], U32, f"z_codes{b}") for b in range(GROUPS)]
-        z_sc = [tile([P, NP], U8, f"z_sc{b}") for b in range(GROUPS)]
-
-        sines = {}
-
         def take_sine(j):
-            sines[j] = tile([P, NP], F32, f"sine{j}", AT_SINE[j % 2])
+            sines[j] = tile([P, NP], F32, f"sine{j}", at_sine(j) if j + 2 < TILES else None)
             nc.scalar.activation(out=sines[j][:], in_=theme[j][:], func=ACT.Sin, bias=per_channel(0, j))
 
         def scale_by_amp(j):
             nc.scalar.activation(out=z_rows[j // 4][:, j % 4, :], in_=sines[j][:], func=ACT.Copy, scale=per_channel(1, j))
 
-        def quantize_z(b):
-            width = NP // 2
-            grouped = []
-            for half in range(2):
-                part = tile([P, 4 * width], BF16, f"z_grouped{b}_{half}")
-                nc.vector.tensor_copy(
-                    out=part[:].rearrange("p (c i t) -> p c t i", i=4, t=4),
-                    in_=z_rows[b][:, :, half * width : (half + 1) * width].rearrange("p t (c i) -> p c t i", i=4),
-                )
-                grouped.append(part)
-            for half in range(2):
-                cols = slice(half * width, (half + 1) * width)
-                nc.vector.quantize_mx(
-                    out=z_codes[b][:, cols].bitcast(FP8X4), scales=z_sc[b][:, cols], in_=grouped[half][:]
-                )
+        z_grouped = {}
+        HALF = NP // 2
 
-        take_sine(0)
-        group_w2(0, 0, "theme0", nc.vector.tensor_copy)
-        load_w2(1, 1, AT_W2_00)
-        for j in range(TILES):
-            if j + 1 < TILES:
-                take_sine(j + 1)
+        def group_z(b, half):
+            z_grouped[(b, half)] = tile([P, 4 * HALF], BF16, f"z_grouped{b}_{half}")
+            nc.vector.tensor_copy(
+                out=z_grouped[(b, half)][:].rearrange("p (c i t) -> p c t i", i=4, t=4),
+                in_=z_rows[b][:, :, half * HALF : (half + 1) * HALF].rearrange("p t (c i) -> p c t i", i=4),
+            )
+
+        def quantize_z(b, half):
+            cols = slice(half * HALF, (half + 1) * HALF)
+            nc.vector.quantize_mx(
+                out=z_codes[b][:, cols].bitcast(FP8X4), scales=z_sc[b][:, cols], in_=z_grouped[(b, half)][:]
+            )
+
+        for a in range(PASSES):
+            for half in range(2):
+                for j in range(2):
+                    first_stage_pass(j, half, a)
+                    if a == PASSES - 1:
+                        empty_bank(j, half)
+        pick_theme(0)
+        pick_theme(1)
+        fill_bank(2, 0)
+        fill_bank(2, 1)
+        group_w2(0, 0, after_codes(2), nc.vector.tensor_copy)
+        load_w2(1, 1, AT_TAB0)
+        pick_theme(2)
+        for j in range(TILES - 3):
+            take_sine(j)
+            fill_bank(j + 3, 0)
             scale_by_amp(j)
+            fill_bank(j + 3, 1)
+            if j == 0:
+                quantize_w2(0, 0, after_codes(3))
+            if j == 1:
+                group_w2(1, 0, after_codes(4), nc.vector.tensor_copy)
+            if j == 2:
+                quantize_w2(1, 0, after_codes(5))
             if j == 3:
-                quantize_z(0)
-                quantize_w2(0, 0, "z_grouped0_0")
-        group_w2(1, 0, "theme2", nc.vector.tensor_copy)
-        group_w2(0, 1, "theme4", nc.vector.tensor_copy)
-        quantize_w2(1, 0, "theme7")
-        quantize_w2(0, 1, "theme6")
-        quantize_z(1)
-        group_w2(1, 1, AT_SINE[1], nc.scalar.copy)
+                group_z(0, 0)
+                group_z(0, 1)
+            pick_theme(j + 3)
+            if j == 3:
+                quantize_z(0, 0)
+                quantize_z(0, 1)
+        take_sine(5)
+        group_w2(0, 1, "theme5", nc.vector.tensor_copy)
+        take_sine(6)
+        scale_by_amp(5)
+        scale_by_amp(6)
+        take_sine(7)
+        scale_by_amp(7)
+
+        group_z(1, 0)
+        group_z(1, 1)
+        quantize_z(1, 0)
+        quantize_z(1, 1)
+        group_w2(1, 1, "sine7", nc.scalar.copy)
+        quantize_w2(0, 1, "z_rows1")
+        quantize_w2(1, 1, "z_grouped1_0")
 
         out_view = out.rearrange("(b g t i) m -> b t g i m", b=GROUPS, g=16, t=4)
-        y_place = [None, "y1", "y2", "y3", "diff1", "y5", "diff2", "diff3"]
-        y_of = {}
+        y_of, y_sb, diffs, squares = {}, {}, {}, {}
 
         def predict(j):
             c, u = j // 4, j % 4
@@ -312,65 +334,60 @@ def tile_list_passacaglia_variation_surprise_kernel(
                     stop=(b == GROUPS - 1),
                 )
             y_of[j] = y
-            if j > 0:
-                y_of[j] = tile([P, NP], F32, f"y_sb{j}", y_place[j])
-                nc.scalar.copy(out=y_of[j][:], in_=y[:])
 
-        diffs = {}
+        def fetch_y(j, cols=slice(0, NP)):
+            y_sb[(j, cols.start)] = tile([P, cols.stop - cols.start], F32, f"y_sb{j}_{cols.start}")
+            nc.scalar.copy(out=y_sb[(j, cols.start)][:], in_=y_of[j][:, cols])
 
-        def subtract(j, cols=slice(0, NP)):
-            if j not in diffs:
-                diffs[j] = tile([P, NP], F32, f"diff{j}")
-            picks = pos2_sb[:, cols.start // 16 : cols.stop // 16]
-            nc.vector.tensor_tensor(
-                out=diffs[j][:, cols], in0=h[j][:].indirect(picks), in1=y_of[j][:, cols], op=ALU.subtract
-            )
-
-        squares = {}
+        def subtract(j, cols=slice(0, NP), place=None):
+            diff = tile([P, cols.stop - cols.start], F32, f"diff{j}_{cols.start}", place)
+            picked = h[j][:].indirect(pos2_sb[:, cols.start // 16 : cols.stop // 16])
+            nc.vector.tensor_tensor(out=diff[:], in0=picked, in1=y_sb[(j, cols.start)][:], op=ALU.subtract)
+            diffs[(j, cols.start)] = diff
 
         def square_on_scalar(j):
-            squares[j] = tile([P, NP], F32, f"square{j}", f"square{j % 3}")
-            nc.scalar.activation(out=squares[j][:], in_=diffs[j][:], func=ACT.Square)
+            squares[j] = tile([P, NP], F32, f"square{j}", f"theme{j}" if j else AT_TAB2 + 2048)
+            nc.scalar.activation(out=squares[j][:], in_=diffs[(j, 0)][:], func=ACT.Square)
 
-        def weigh_on_scalar(j):
-            mark = tile([P, NP], F32, f"mark{j}")
+        def weigh_on_scalar(j, queue=nc.sync):
+            mark = tile([P, NP], F32, f"mark{j}", AT_TAB1 + 2048 * j if j < 4 else None)
             nc.scalar.activation(out=mark[:], in_=squares[j][:], func=ACT.Copy, scale=per_channel(2, j))
-            nc.sync.dma_start(out=out_view[j // 4, j % 4], in_=mark[:])
+            queue.dma_start(out=out_view[j // 4, j % 4], in_=mark[:])
 
         def finish_on_vector(j, cols=slice(0, NP), queue=nc.sync):
             mark = tile([P, cols.stop - cols.start], F32, f"mark{j}_{cols.start}")
-            diff = diffs[j][:, cols]
+            diff = diffs[(j, cols.start)][:]
             nc.vector.scalar_tensor_tensor(
                 out=mark[:], in0=diff, scalar=per_channel(2, j), in1=diff, op0=ALU.mult, op1=ALU.mult
             )
             queue.dma_start(out=out_view[j // 4, j % 4][:, :, cols], in_=mark[:])
 
-        for j in range(4):
+        for j in range(TILES):
             predict(j)
-        actual = tile([P, NP], F32, "actual0", "z_grouped1_0")
-        nc.vector.tensor_copy(actual[:], h[0][:].indirect(pos2_sb[:]))
-        quantize_w2(1, 1, "z_grouped1_1")
-        diffs[0] = tile([P, NP], F32, "diff0")
-        nc.vector.tensor_tensor(out=diffs[0][:], in0=actual[:], in1=y_of[0][:], op=ALU.subtract)
+        parts = [slice(0, NP // 2), slice(NP // 2, 3 * NP // 4), slice(3 * NP // 4, NP)]
+        for j in range(3):
+            fetch_y(j)
+        subtract(0)
         square_on_scalar(0)
-        subtract(1)
-        square_on_scalar(1)
+        for j in range(3, 7):
+            fetch_y(j)
+        for part in parts:
+            fetch_y(7, part)
         weigh_on_scalar(0)
-        for j in range(4, 6):
-            predict(j)
-        for j in range(2, 5):
+        for j in range(1, 5):
             subtract(j)
+        square_on_scalar(1)
+        for j in range(2, 5):
             square_on_scalar(j)
             weigh_on_scalar(j - 1)
-            if j < 4:
-                predict(j + 4)
-        weigh_on_scalar(4)
-        halves = [slice(0, 3 * NP // 4), slice(3 * NP // 4, NP)]
-        subtract(5)
-        subtract(6)
+        weigh_on_scalar(4, nc.scalar)
+        subtract(5, place=AT_TAB2 + LAP)
+        subtract(6, place=AT_TAB2 + 4096 - LAP)
         finish_on_vector(5)
-        subtract(7, halves[0])
+        subtract(7, parts[0], "y_sb6_0")
         finish_on_vector(6)
-        subtract(7, halves[1])
-        finish_on_vector(7, halves[0])
-        finish_on_vector(7, halves[1], nc.scalar)
+        subtract(7, parts[1], "y_sb7_0")
+        finish_on_vector(7, parts[0])
+        subtract(7, parts[2], "y_sb7_256")
+        finish_on_vector(7, parts[1])
+        finish_on_vector(7, parts[2], nc.scalar)

@@ -27,21 +27,35 @@ PAIR0 = LAST0 + 16
 VEC_ROWS = 3 * GROUPS
 VEC0 = 96
 LAP = 64
+AMP_ON_VECTOR = (6,)
+FILL_ORDER = [(0, 0), (0, 1), (1, 0), (1, 1)] + [(j, half) for j in range(2, TILES) for half in range(2)]
+BANK_OF = {key: (n % 3 if n < 6 else (n + 1) % 4) for n, key in enumerate(FILL_ORDER)}
 CODE_BYTES = PASSES * 2 * P
-AT_TAB0 = 0
-AT_TAB1 = 8192
-AT_TAB2 = 16384
-AT_TAB_SC = AT_TAB2 + 8192 - LAP
-CHAIN0 = AT_TAB_SC + 2048 + 3072
+AT_TAB0 = 3072
+AT_TAB1 = AT_TAB0 + 8192
+AT_SINE0 = AT_TAB1 + 8192
+AT_VEC_ROWS = AT_SINE0 + 2048 - LAP
+AT_LATER_CODES = [AT_VEC_ROWS + 1024, AT_VEC_ROWS]
+AT_CODES3 = AT_VEC_ROWS + 2048 - LAP
+AT_W2_00 = AT_CODES3 + CODE_BYTES - LAP
+AT_TAB_SC = AT_W2_00 + 8192 - LAP
+AT_TAB2 = AT_TAB_SC + 2048 - LAP
+CHAIN0 = AT_TAB2 + 8192
 STEP = 2048 + CODE_BYTES + 4096
 
 
 def at_codes(j):
-    return CHAIN0 + (j - 2) * STEP + 2048 - LAP
+    return at_sine(j - 2) + 2048 - LAP
 
 
 def at_sine(j):
-    return CHAIN0 + j * STEP
+    return AT_VEC_ROWS if j == 1 else CHAIN0 + j * STEP
+
+
+def sine_place(j):
+    if j == 0:
+        return AT_SINE0
+    return at_sine(j) if j < 6 else None
 
 
 def after_codes(j):
@@ -83,7 +97,7 @@ def tile_list_passacaglia_variation_surprise_kernel(
         nc.scalar.dma_start(
             out=tab_sc[PAIR0:P, :].bitcast(I32), in_=tab_scales[0:2].rearrange("a q t -> q a t").bitcast(I32)
         )
-        vec_rows = tile([P, 512], F32, "vec_rows")
+        vec_rows = tile([P, 512], F32, "vec_rows", AT_VEC_ROWS)
         nc.gpsimd.memset(vec_rows[VEC0:P, :], 0.0)
         for v, vector in enumerate((phase, amp, mrg)):
             nc.gpsimd.dma_start(
@@ -94,23 +108,23 @@ def tile_list_passacaglia_variation_surprise_kernel(
         load_tab(0)
         nc.sync.dma_start(pos2_sb[:], pos2)
         w1_raw = []
-        w1_sc_raw = tile([P, PASSES * 128], I32, "w1_sc_raw")
+        w1_sc_raw = tile([P, PASSES * 256], I32, "w1_sc_raw")
 
         def load_w1(b, place):
             raw = tile([P, PASSES, 256], I32, f"w1_raw{b}", place)
             nc.sync.dma_start(out=raw[:], in_=w1_words.rearrange("a p (b c) -> b p a c", b=GROUPS)[b].bitcast(I32))
             w1_raw.append(raw)
 
-        def load_w1_scales(b):
+        def load_w1_scales():
             for r in range(4):
                 nc.sync.dma_start(
                     out=w1_sc_raw[r:P:32, :].rearrange("p (a c) -> p a c", a=PASSES),
-                    in_=w1_scales[:, r:16:4, b * 512 : (b + 1) * 512].rearrange("a q n -> q a n").bitcast(I32),
+                    in_=w1_scales[:, r:16:4, :].rearrange("a q n -> q a n").bitcast(I32),
                 )
 
         load_w1(0, None)
         nc.vector.memset(w1_sc_raw[:], 0)
-        load_w1_scales(0)
+        load_w1_scales()
         nc.vector.memset(zeros[:], 0.0)
         nc.vector.memset(tab_sc[0:LAST0, :].bitcast(I32), 0)
         nc.vector.memset(v_sc[:].bitcast(I32), 0)
@@ -130,7 +144,6 @@ def tile_list_passacaglia_variation_surprise_kernel(
                 out=v_sc[32 * q : 32 * q + 4, 2 * S :].bitcast(I32),
                 in_=picked_sc[LAST0 + 4 * q : LAST0 + 4 * q + 4, :].bitcast(I32),
             )
-        load_w1(1, AT_TAB_SC + 2048 - LAP)
 
         v_codes = [tile([P, S], U32, f"v_codes{a}") for a in range(PASSES)]
 
@@ -150,41 +163,47 @@ def tile_list_passacaglia_variation_surprise_kernel(
         w1_codes, w1_sc = {}, []
 
         def order_scales(b, copy, view):
-            sc = tile([P, PASSES * 512], U8, f"w1_sc{b}", AT_TAB_SC + LAP if b == 0 else None)
+            sc = tile([P, PASSES * 512], U8, f"w1_sc{b}")
             copy(
                 out=sc[:].bitcast(view).rearrange("p (a t g w) -> p a t g w", t=4, g=16, w=2),
-                in_=w1_sc_raw[:].bitcast(view).rearrange("p (a g t w) -> p a t g w", t=4, g=16, w=2),
+                in_=w1_sc_raw[:].bitcast(view).rearrange("p (a b g t w) -> p b a t g w", b=2, t=4, g=16, w=2)[:, b],
             )
             w1_sc.append(sc)
 
-        def order_codes(j, copy, view):
-            codes = tile([P, CODE_BYTES], U8, f"w1_codes{j}", at_codes(j) if j >= 2 else None)
+        def order_codes(j, copy, view, first=0, count=PASSES, place=None):
+            codes = tile([P, count * 2 * P], U8, f"w1_codes{j}_{first}", at_codes(j) if j >= 2 else place)
             by_tile = w1_raw[j // 4][:].bitcast(view).rearrange("p a (g t w) -> p t a g w", t=4, w=4)
-            copy(out=codes[:].bitcast(view).rearrange("p (a g w) -> p a g w", a=PASSES, w=4), in_=by_tile[:, j % 4])
-            w1_codes[j] = codes
+            copy(
+                out=codes[:].bitcast(view).rearrange("p (a g w) -> p a g w", a=count, w=4),
+                in_=by_tile[:, j % 4, first : first + count],
+            )
+            for n in range(count):
+                w1_codes[(j, first + n)] = codes[:, 2 * n * P : 2 * (n + 1) * P]
 
-        for j in range(4):
-            order_codes(j, nc.scalar.copy, U32)
-        vec = tile([P, 4, 8], F32, "vec")
-        vec_ordered = tile([P, 4, P], F32, "vec_ordered", "w1_raw0")
-        nc.scalar.copy(
-            out=vec_ordered[:].rearrange("p t (g i) -> p t g i", i=8),
-            in_=vec_rows[:].rearrange("p (g t i) -> p t g i", t=4, i=8),
-        )
-        vec_ps = psum.tile([P, 4, P], F32, name="vec_ps", tag="bank4")
-        for t in range(4):
-            nc.tensor.transpose(vec_ps[:, t, :], vec_ordered[:, t, :], ident[:])
+        for j in range(2):
+            order_codes(j, nc.scalar.copy, U32, 0, 1)
+        order_codes(2, nc.scalar.copy, U32)
         order_scales(0, nc.scalar.copy, U32)
-        load_w1_scales(1)
-        nc.scalar.copy(out=vec[:, :, 0:VEC_ROWS], in_=vec_ps[:, :, VEC0 : VEC0 + VEC_ROWS])
+        order_scales(1, nc.scalar.copy, U32)
+        vec = tile([P, 4, 8], F32, "vec")
+        vec_ordered = tile([P, 4, P], F32, "vec_ordered", "w1_codes0_0")
+
+        def order_vectors():
+            nc.scalar.copy(
+                out=vec_ordered[:].rearrange("p t (g i) -> p t g i", i=8),
+                in_=vec_rows[:].rearrange("p (g t i) -> p t g i", t=4, i=8),
+            )
+
+        def turn_vectors():
+            vec_ps = psum.tile([P, 4, P], F32, name="vec_ps", tag="bank3")
+            for t in range(4):
+                nc.tensor.transpose(vec_ps[:, t, :], vec_ordered[:, t, :], ident[:])
+            nc.scalar.copy(out=vec[:, :, 0:VEC_ROWS], in_=vec_ps[:, :, VEC0 : VEC0 + VEC_ROWS])
 
         def per_channel(v, j):
             col = GROUPS * v + j // 4
             return vec[:, j % 4, col : col + 1]
 
-        for j in range(4, TILES):
-            order_codes(j, nc.vector.tensor_copy, I32)
-        order_scales(1, nc.vector.tensor_copy, I32)
 
         w2_view = w2.rearrange("(b g t i) (c n) -> b c t g i n", b=GROUPS, g=16, t=4, c=GROUPS)
         w2_raw, w2_grouped, w2_codes, w2_sc = {}, {}, {}, {}
@@ -210,7 +229,8 @@ def tile_list_passacaglia_variation_surprise_kernel(
             w2_codes[(b, c)] = codes
             w2_sc[(b, c)] = scales
 
-        load_w2(0, 0, AT_TAB0)
+        load_w2(0, 0, AT_W2_00)
+        load_w1(1, AT_TAB0 - 3072 + LAP)
         load_w2(1, 0, AT_TAB1)
         load_w2(0, 1, AT_TAB2)
 
@@ -222,12 +242,12 @@ def tile_list_passacaglia_variation_surprise_kernel(
 
         def first_stage_pass(j, half, a):
             if a == 0:
-                slot = 2 * half + j if j < 2 else (2 * j + half) % 4
+                slot = BANK_OF[(j, half)]
                 banks[(j, half)] = psum.tile([P, BANK], F32, name=f"h_ps{j}_{half}", tag=f"bank{slot}")
             at = a * 512 + (j % 4) * P
             nc.tensor.matmul_mx(
                 out=banks[(j, half)][:],
-                lhsT=w1_codes[j][:, 2 * a * P : 2 * (a + 1) * P].bitcast(FP4X4),
+                lhsT=w1_codes[(j, a)].bitcast(FP4X4),
                 lhsT_scale=w1_sc[j // 4][:, at : at + P],
                 rhs=v_codes[a][:, half * BANK : (half + 1) * BANK].bitcast(FP8X4),
                 rhs_scale=v_sc[:, a * S + half * BANK : a * S + (half + 1) * BANK],
@@ -244,15 +264,19 @@ def tile_list_passacaglia_variation_surprise_kernel(
             empty_bank(j, half)
 
         def pick_theme(j):
-            theme[j] = tile([P, NP], F32, f"theme{j}")
+            theme[j] = tile([P, NP], F32, f"theme{j}", AT_W2_00 + LAP + 2048 * j if j < 2 else None)
             nc.vector.tensor_copy(theme[j][:], h[j][:].indirect(pos1_sb[:]))
 
         def take_sine(j):
-            sines[j] = tile([P, NP], F32, f"sine{j}", at_sine(j) if j + 2 < TILES else None)
+            sines[j] = tile([P, NP], F32, f"sine{j}", sine_place(j))
             nc.scalar.activation(out=sines[j][:], in_=theme[j][:], func=ACT.Sin, bias=per_channel(0, j))
 
         def scale_by_amp(j):
-            nc.scalar.activation(out=z_rows[j // 4][:, j % 4, :], in_=sines[j][:], func=ACT.Copy, scale=per_channel(1, j))
+            rows = z_rows[j // 4][:, j % 4, :]
+            if j in AMP_ON_VECTOR:
+                nc.vector.tensor_scalar(out=rows, in0=sines[j][:], scalar1=per_channel(1, j), scalar2=None, op0=ALU.mult)
+            else:
+                nc.scalar.activation(out=rows, in_=sines[j][:], func=ACT.Copy, scale=per_channel(1, j))
 
         z_grouped = {}
         HALF = NP // 2
@@ -270,26 +294,42 @@ def tile_list_passacaglia_variation_surprise_kernel(
                 out=z_codes[b][:, cols].bitcast(FP8X4), scales=z_sc[b][:, cols], in_=z_grouped[(b, half)][:]
             )
 
-        for a in range(PASSES):
+        for j, half in ((0, 0), (0, 1), (1, 0)):
+            first_stage_pass(j, half, 0)
+        order_vectors()
+        for j in range(2):
+            order_codes(j, nc.scalar.copy, U32, 1, 2, AT_LATER_CODES[j])
+        turn_vectors()
+        for a in (1, 2):
             for half in range(2):
-                for j in range(2):
-                    first_stage_pass(j, half, a)
-                    if a == PASSES - 1:
-                        empty_bank(j, half)
+                first_stage_pass(0, half, a)
+                if a == 2:
+                    empty_bank(0, half)
+        first_stage_pass(1, 0, 1)
+        first_stage_pass(1, 0, 2)
+        empty_bank(1, 0)
+        group_w2(0, 0, None, nc.vector.tensor_copy)
         pick_theme(0)
+        fill_bank(1, 1)
+        for j in range(3, TILES):
+            order_codes(j, nc.vector.tensor_copy, I32)
         pick_theme(1)
         fill_bank(2, 0)
+        take_sine(0)
         fill_bank(2, 1)
-        group_w2(0, 0, after_codes(2), nc.vector.tensor_copy)
-        load_w2(1, 1, AT_TAB0)
+        scale_by_amp(0)
+        quantize_w2(0, 0, after_codes(2))
         pick_theme(2)
-        for j in range(TILES - 3):
+        fill_bank(3, 0)
+        fill_bank(3, 1)
+        pick_theme(3)
+        for j in range(1, TILES - 3):
             take_sine(j)
+            if j == 1:
+                load_w2(1, 1, AT_W2_00)
             fill_bank(j + 3, 0)
             scale_by_amp(j)
             fill_bank(j + 3, 1)
-            if j == 0:
-                quantize_w2(0, 0, after_codes(3))
             if j == 1:
                 group_w2(1, 0, after_codes(4), nc.vector.tensor_copy)
             if j == 2:
@@ -322,7 +362,7 @@ def tile_list_passacaglia_variation_surprise_kernel(
 
         def predict(j):
             c, u = j // 4, j % 4
-            y = psum.tile([P, NP], F32, name=f"y{j}", tag=f"bank{(j + 4) % TILES}")
+            y = psum.tile([P, NP], F32, name=f"y{j}", tag=f"bank{j + 4 if j < 4 else (j + 1) % 4}")
             for b in range(GROUPS):
                 nc.tensor.matmul_mx(
                     out=y[:],
@@ -346,7 +386,7 @@ def tile_list_passacaglia_variation_surprise_kernel(
             diffs[(j, cols.start)] = diff
 
         def square_on_scalar(j):
-            squares[j] = tile([P, NP], F32, f"square{j}", f"theme{j}" if j else AT_TAB2 + 2048)
+            squares[j] = tile([P, NP], F32, f"square{j}", AT_TAB2 + 2048 if j == 4 else f"square{j % 2}")
             nc.scalar.activation(out=squares[j][:], in_=diffs[(j, 0)][:], func=ACT.Square)
 
         def weigh_on_scalar(j, queue=nc.sync):
@@ -354,8 +394,8 @@ def tile_list_passacaglia_variation_surprise_kernel(
             nc.scalar.activation(out=mark[:], in_=squares[j][:], func=ACT.Copy, scale=per_channel(2, j))
             queue.dma_start(out=out_view[j // 4, j % 4], in_=mark[:])
 
-        def finish_on_vector(j, cols=slice(0, NP), queue=nc.sync):
-            mark = tile([P, cols.stop - cols.start], F32, f"mark{j}_{cols.start}")
+        def finish_on_vector(j, cols=slice(0, NP), queue=nc.sync, place=None):
+            mark = tile([P, cols.stop - cols.start], F32, f"mark{j}_{cols.start}", place)
             diff = diffs[(j, cols.start)][:]
             nc.vector.scalar_tensor_tensor(
                 out=mark[:], in0=diff, scalar=per_channel(2, j), in1=diff, op0=ALU.mult, op1=ALU.mult
@@ -364,30 +404,22 @@ def tile_list_passacaglia_variation_surprise_kernel(
 
         for j in range(TILES):
             predict(j)
-        parts = [slice(0, NP // 2), slice(NP // 2, 3 * NP // 4), slice(3 * NP // 4, NP)]
-        for j in range(3):
-            fetch_y(j)
-        subtract(0)
-        square_on_scalar(0)
-        for j in range(3, 7):
+        parts = [slice(0, 3 * NP // 4), slice(3 * NP // 4, NP)]
+        for j in range(TILES - 1):
             fetch_y(j)
         for part in parts:
             fetch_y(7, part)
-        weigh_on_scalar(0)
-        for j in range(1, 5):
+        for j in range(3):
+            subtract(j)
+        finish_on_vector(0, place="z_codes1")
+        for j in range(3, 7):
             subtract(j)
         square_on_scalar(1)
-        for j in range(2, 5):
+        for j in range(2, 7):
             square_on_scalar(j)
-            weigh_on_scalar(j - 1)
-        weigh_on_scalar(4, nc.scalar)
-        subtract(5, place=AT_TAB2 + LAP)
-        subtract(6, place=AT_TAB2 + 4096 - LAP)
-        finish_on_vector(5)
-        subtract(7, parts[0], "y_sb6_0")
-        finish_on_vector(6)
-        subtract(7, parts[1], "y_sb7_0")
+            weigh_on_scalar(j - 1, nc.scalar)
+        weigh_on_scalar(6, nc.scalar)
+        subtract(7, parts[0])
+        subtract(7, parts[1])
         finish_on_vector(7, parts[0])
-        subtract(7, parts[2], "y_sb7_256")
         finish_on_vector(7, parts[1])
-        finish_on_vector(7, parts[2], nc.scalar)

@@ -386,7 +386,7 @@ def tile_list_passacaglia_variation_surprise_kernel(
             diffs[(j, cols.start)] = diff
 
         def square_on_scalar(j):
-            squares[j] = tile([P, NP], F32, f"square{j}", AT_TAB2 + 2048 if j == 4 else f"square{j % 2}")
+            squares[j] = tile([P, NP], F32, f"square{j}", AT_TAB2 + 2048 if j == 5 else f"square{j % 2}")
             nc.scalar.activation(out=squares[j][:], in_=diffs[(j, 0)][:], func=ACT.Square)
 
         def weigh_on_scalar(j, queue=nc.sync):
@@ -417,9 +417,9 @@ def tile_list_passacaglia_variation_surprise_kernel(
         square_on_scalar(1)
         for j in range(2, 7):
             square_on_scalar(j)
-            weigh_on_scalar(j - 1, nc.scalar)
+            weigh_on_scalar(j - 1)
         weigh_on_scalar(6, nc.scalar)
         subtract(7, parts[0])
         subtract(7, parts[1])
-        finish_on_vector(7, parts[0])
-        finish_on_vector(7, parts[1])
+        finish_on_vector(7, parts[0], place=AT_TAB2 + 512 + LAP)
+        finish_on_vector(7, parts[1], place=AT_TAB2 + 4096 - LAP)

@@ -27,35 +27,29 @@ PAIR0 = LAST0 + 16
 VEC_ROWS = 3 * GROUPS
 VEC0 = 96
 LAP = 64
-AMP_ON_VECTOR = (6,)
+SPARE_BANK = 5
+AMP_ON_VECTOR = ()
 FILL_ORDER = [(0, 0), (0, 1), (1, 0), (1, 1)] + [(j, half) for j in range(2, TILES) for half in range(2)]
-BANK_OF = {key: (n % 3 if n < 6 else (n + 1) % 4) for n, key in enumerate(FILL_ORDER)}
+BANK_OF = {key: (n if n < 5 else (n - 4) % 5 if n < 8 else (0, 4, 1, 2, 3)[(n - 8) % 5]) for n, key in enumerate(FILL_ORDER)}
 CODE_BYTES = PASSES * 2 * P
-AT_TAB0 = 3072
+AT_W1_GROUP1 = 0
+AT_TAB0 = AT_W1_GROUP1 + 3072 - LAP
 AT_TAB1 = AT_TAB0 + 8192
-AT_SINE0 = AT_TAB1 + 8192
-AT_VEC_ROWS = AT_SINE0 + 2048 - LAP
-AT_LATER_CODES = [AT_VEC_ROWS + 1024, AT_VEC_ROWS]
-AT_CODES3 = AT_VEC_ROWS + 2048 - LAP
-AT_W2_00 = AT_CODES3 + CODE_BYTES - LAP
-AT_TAB_SC = AT_W2_00 + 8192 - LAP
+AT_W1_LATER = AT_TAB1 + 8192 + LAP
+AT_TAB_SC = AT_W1_LATER + 2048 - LAP
 AT_TAB2 = AT_TAB_SC + 2048 - LAP
 CHAIN0 = AT_TAB2 + 8192
 STEP = 2048 + CODE_BYTES + 4096
 
 
 def at_codes(j):
-    return at_sine(j - 2) + 2048 - LAP
-
-
-def at_sine(j):
-    return AT_VEC_ROWS if j == 1 else CHAIN0 + j * STEP
+    return CHAIN0 + (j - 1) * STEP + 2048 - LAP
 
 
 def sine_place(j):
-    if j == 0:
-        return AT_SINE0
-    return at_sine(j) if j < 6 else None
+    if j >= TILES - 2:
+        return None
+    return at_codes(j + 2 if j else 1) - 2048 + LAP
 
 
 def after_codes(j):
@@ -97,34 +91,37 @@ def tile_list_passacaglia_variation_surprise_kernel(
         nc.scalar.dma_start(
             out=tab_sc[PAIR0:P, :].bitcast(I32), in_=tab_scales[0:2].rearrange("a q t -> q a t").bitcast(I32)
         )
-        vec_rows = tile([P, 512], F32, "vec_rows", AT_VEC_ROWS)
-        nc.gpsimd.memset(vec_rows[VEC0:P, :], 0.0)
-        for v, vector in enumerate((phase, amp, mrg)):
-            nc.gpsimd.dma_start(
-                out=vec_rows[VEC0 + GROUPS * v : VEC0 + GROUPS * (v + 1), :], in_=vector.rearrange("(b c) -> b c", b=GROUPS)
-            )
+        vec_rows = tile([P, 512], F32, "vec_rows")
         make_identity(nc, ident[:])
+        nc.vector.memset(vec_rows[VEC0:P, :], 0.0)
+        for v, vector in enumerate((phase, amp, mrg)):
+            first = VEC0 + GROUPS * v
+            nc.gpsimd.dma_start(
+                out=vec_rows[first : first + GROUPS, :], in_=vector.rearrange("(b c) -> b c", b=GROUPS)
+            )
         nc.sync.dma_start(pos1_sb[:], pos1)
         load_tab(0)
         nc.sync.dma_start(pos2_sb[:], pos2)
-        w1_raw = []
-        w1_sc_raw = tile([P, PASSES * 256], I32, "w1_sc_raw")
+        w1_raw = {}
+        w1_sc_raw = tile([P, PASSES * 128], I32, "w1_sc_raw")
+        w1_view = w1_words.rearrange("a p (b c) -> b p a c", b=GROUPS)
 
-        def load_w1(b, place):
-            raw = tile([P, PASSES, 256], I32, f"w1_raw{b}", place)
-            nc.sync.dma_start(out=raw[:], in_=w1_words.rearrange("a p (b c) -> b p a c", b=GROUPS)[b].bitcast(I32))
-            w1_raw.append(raw)
+        def load_w1(b, first, count, place):
+            raw = tile([P, count, 256], I32, f"w1_raw{b}_{first}", place)
+            nc.sync.dma_start(out=raw[:], in_=w1_view[b, :, first : first + count].bitcast(I32))
+            for n in range(count):
+                w1_raw[(b, first + n)] = raw[:, n:count]
 
-        def load_w1_scales():
+        def load_w1_scales(b):
             for r in range(4):
                 nc.sync.dma_start(
                     out=w1_sc_raw[r:P:32, :].rearrange("p (a c) -> p a c", a=PASSES),
-                    in_=w1_scales[:, r:16:4, :].rearrange("a q n -> q a n").bitcast(I32),
+                    in_=w1_scales[:, r:16:4, b * 512 : (b + 1) * 512].rearrange("a q n -> q a n").bitcast(I32),
                 )
 
-        load_w1(0, None)
+        load_w1(0, 0, 2, None)
         nc.vector.memset(w1_sc_raw[:], 0)
-        load_w1_scales()
+        load_w1_scales(0)
         nc.vector.memset(zeros[:], 0.0)
         nc.vector.memset(tab_sc[0:LAST0, :].bitcast(I32), 0)
         nc.vector.memset(v_sc[:].bitcast(I32), 0)
@@ -145,57 +142,68 @@ def tile_list_passacaglia_variation_surprise_kernel(
                 in_=picked_sc[LAST0 + 4 * q : LAST0 + 4 * q + 4, :].bitcast(I32),
             )
 
+        load_w1(0, 2, 1, AT_W1_LATER + 1024)
+        load_w1(1, 0, PASSES, AT_W1_GROUP1)
+
         v_codes = [tile([P, S], U32, f"v_codes{a}") for a in range(PASSES)]
 
-        def pick_codes(a, pieces=1):
-            width = S // pieces
-            for piece in range(pieces):
-                first = piece * width
-                nc.vector.tensor_copy(
-                    v_codes[a][:, first : first + width],
-                    tabs[a][:].bitcast(U32).indirect(offs_sb[:, first // 16 : (first + width) // 16]),
-                )
+        def pick_codes(a, first=0, width=S):
+            nc.vector.tensor_copy(
+                v_codes[a][:, first : first + width],
+                tabs[a][:].bitcast(U32).indirect(offs_sb[:, first // 16 : (first + width) // 16]),
+            )
 
         pick_codes(0)
         pick_codes(1)
-        pick_codes(2, pieces=2)
+        pick_codes(2, 0, BANK)
+        pick_codes(2, BANK, BANK // 2)
+        pick_codes(2, BANK + BANK // 2, BANK // 2)
 
         w1_codes, w1_sc = {}, []
 
         def order_scales(b, copy, view):
-            sc = tile([P, PASSES * 512], U8, f"w1_sc{b}")
+            sc = tile([P, PASSES * 512], U8, f"w1_sc{b}", None if b else AT_TAB_SC + LAP)
             copy(
-                out=sc[:].bitcast(view).rearrange("p (a t g w) -> p a t g w", t=4, g=16, w=2),
-                in_=w1_sc_raw[:].bitcast(view).rearrange("p (a b g t w) -> p b a t g w", b=2, t=4, g=16, w=2)[:, b],
+                out=sc[:].bitcast(view).rearrange("p (a t o) -> p a t o", t=4, o=32),
+                in_=w1_sc_raw[:].bitcast(view).rearrange("p (a o t) -> p a t o", t=4, o=32),
             )
             w1_sc.append(sc)
 
-        def order_codes(j, copy, view, first=0, count=PASSES, place=None):
-            codes = tile([P, count * 2 * P], U8, f"w1_codes{j}_{first}", at_codes(j) if j >= 2 else place)
-            by_tile = w1_raw[j // 4][:].bitcast(view).rearrange("p a (g t w) -> p t a g w", t=4, w=4)
+        code_tiles = {}
+        APART = {(0, 0): None, (0, 1): None, (0, 2): at_codes(2) + LAP, (1, 1): AT_W1_LATER + 1024, (2, 2): None}
+
+        def order_codes(j, copy, view, first, count):
+            if (j, first) in APART:
+                codes = tile([P, count * 2 * P], U8, f"w1_codes{j}_{first}", APART[(j, first)])[:]
+            else:
+                if j not in code_tiles:
+                    code_tiles[j] = tile([P, CODE_BYTES], U8, f"w1_codes{j}", at_codes(j))
+                codes = code_tiles[j][:, first * 2 * P : (first + count) * 2 * P]
+            by_tile = w1_raw[(j // 4, first)].bitcast(view).rearrange("p a (o t w) -> p t a o w", t=4, w=2)
             copy(
-                out=codes[:].bitcast(view).rearrange("p (a g w) -> p a g w", a=count, w=4),
-                in_=by_tile[:, j % 4, first : first + count],
+                out=codes.bitcast(view).rearrange("p (a o w) -> p a o w", a=count, w=2),
+                in_=by_tile[:, j % 4, 0:count],
             )
             for n in range(count):
                 w1_codes[(j, first + n)] = codes[:, 2 * n * P : 2 * (n + 1) * P]
 
-        for j in range(2):
-            order_codes(j, nc.scalar.copy, U32, 0, 1)
-        order_codes(2, nc.scalar.copy, U32)
+        for j in (0, 1, 3):
+            order_codes(j, nc.scalar.copy, U32, 0, 2 if j == 3 else 1)
+        order_codes(0, nc.scalar.copy, U32, 1, 1)
         order_scales(0, nc.scalar.copy, U32)
-        order_scales(1, nc.scalar.copy, U32)
+        load_w1_scales(1)
         vec = tile([P, 4, 8], F32, "vec")
+
         vec_ordered = tile([P, 4, P], F32, "vec_ordered", "w1_codes0_0")
 
         def order_vectors():
             nc.scalar.copy(
-                out=vec_ordered[:].rearrange("p t (g i) -> p t g i", i=8),
-                in_=vec_rows[:].rearrange("p (g t i) -> p t g i", t=4, i=8),
+                out=vec_ordered[:].rearrange("p t (o i) -> p t o i", i=4),
+                in_=vec_rows[:].rearrange("p (o t i) -> p t o i", t=4, i=4),
             )
 
         def turn_vectors():
-            vec_ps = psum.tile([P, 4, P], F32, name="vec_ps", tag="bank3")
+            vec_ps = psum.tile([P, 4, P], F32, name="vec_ps", tag="bank0")
             for t in range(4):
                 nc.tensor.transpose(vec_ps[:, t, :], vec_ordered[:, t, :], ident[:])
             nc.scalar.copy(out=vec[:, :, 0:VEC_ROWS], in_=vec_ps[:, :, VEC0 : VEC0 + VEC_ROWS])
@@ -205,7 +213,7 @@ def tile_list_passacaglia_variation_surprise_kernel(
             return vec[:, j % 4, col : col + 1]
 
 
-        w2_view = w2.rearrange("(b g t i) (c n) -> b c t g i n", b=GROUPS, g=16, t=4, c=GROUPS)
+        w2_view = w2.rearrange("(b o t i) (c n) -> b c t o i n", b=GROUPS, o=32, t=4, c=GROUPS)
         w2_raw, w2_grouped, w2_codes, w2_sc = {}, {}, {}, {}
 
         def load_w2(b, c, place):
@@ -214,211 +222,238 @@ def tile_list_passacaglia_variation_surprise_kernel(
                 nc.sync.dma_start(out=raw[:, t, :], in_=w2_view[b, c, t])
             w2_raw[(b, c)] = raw
 
-        def group_w2(b, c, place, copy):
-            grouped = tile([P, 4 * 512], BF16, f"w2_grouped{b}{c}", place)
-            dst = grouped[:].rearrange("p (u g e l t) -> p u g e t l", u=4, g=16, e=2, l=4)
-            src = w2_raw[(b, c)][:].rearrange("p t (g u e l) -> p u g e t l", u=4, g=16, e=2)
-            for u in range(4):
-                copy(out=dst[:, u], in_=src[:, u])
-            w2_grouped[(b, c)] = grouped
+        def group_w2(b, c, place, copy, quarters=range(4)):
+            if (b, c) not in w2_grouped:
+                w2_grouped[(b, c)] = tile([P, 4 * 512], BF16, f"w2_grouped{b}{c}", place)
+            dst = w2_grouped[(b, c)][:].rearrange("p (u o l t) -> p u o t l", u=4, o=32, l=4)
+            src = w2_raw[(b, c)][:].rearrange("p t (o u l) -> p u o t l", u=4, o=32)
+            copy(out=dst[:, quarters[0] : quarters[-1] + 1], in_=src[:, quarters[0] : quarters[-1] + 1])
 
-        def quantize_w2(b, c, place):
-            codes = tile([P, 512], U32, f"w2_codes{b}{c}", place)
-            scales = tile([P, 512], U8, f"w2_sc{b}{c}")
-            nc.vector.quantize_mx(out=codes[:].bitcast(FP8X4), scales=scales[:], in_=w2_grouped[(b, c)][:])
-            w2_codes[(b, c)] = codes
-            w2_sc[(b, c)] = scales
+        def quantize_w2(b, c, place, scale_place=None, tiles=range(4)):
+            first, count = tiles[0] * P, len(tiles) * P
+            codes = tile([P, count], U32, f"w2_codes{b}{c}_{first}", place)
+            scales = tile([P, count], U8, f"w2_sc{b}{c}_{first}", scale_place)
+            grouped = w2_grouped[(b, c)][:, 4 * first : 4 * (first + count)]
+            nc.vector.quantize_mx(out=codes[:].bitcast(FP8X4), scales=scales[:], in_=grouped)
+            for n, u in enumerate(tiles):
+                w2_codes[(b, c, u)] = codes[:, n * P : (n + 1) * P]
+                w2_sc[(b, c, u)] = scales[:, n * P : (n + 1) * P]
 
-        load_w2(0, 0, AT_W2_00)
-        load_w1(1, AT_TAB0 - 3072 + LAP)
-        load_w2(1, 0, AT_TAB1)
+        load_w2(0, 0, AT_TAB0 + LAP)
+        load_w2(1, 0, AT_TAB1 + LAP)
         load_w2(0, 1, AT_TAB2)
 
         h = [tile([P, S], F32, f"h{j}") for j in range(TILES)]
         theme, sines, banks = {}, {}, {}
         z_rows = [tile([P, 4, NP], BF16, f"z_rows{b}") for b in range(GROUPS)]
         z_codes = [tile([P, NP], U32, f"z_codes{b}") for b in range(GROUPS)]
-        z_sc = [tile([P, NP], U8, f"z_sc{b}") for b in range(GROUPS)]
+        z_sc = [tile([P, NP], U8, f"z_sc{b}", None if b else after_codes(7)) for b in range(GROUPS)]
 
-        def first_stage_pass(j, half, a):
+        def first_stage_pass(j, half, a, first=0, width=BANK):
             if a == 0:
-                slot = BANK_OF[(j, half)]
-                banks[(j, half)] = psum.tile([P, BANK], F32, name=f"h_ps{j}_{half}", tag=f"bank{slot}")
+                slot = SPARE_BANK if first else BANK_OF[(j, half)]
+                banks[(j, half, first)] = psum.tile([P, width], F32, name=f"h_ps{j}_{half}_{first}", tag=f"bank{slot}")
             at = a * 512 + (j % 4) * P
+            col = half * BANK + first
             nc.tensor.matmul_mx(
-                out=banks[(j, half)][:],
+                out=banks[(j, half, first)][:],
                 lhsT=w1_codes[(j, a)].bitcast(FP4X4),
                 lhsT_scale=w1_sc[j // 4][:, at : at + P],
-                rhs=v_codes[a][:, half * BANK : (half + 1) * BANK].bitcast(FP8X4),
-                rhs_scale=v_sc[:, a * S + half * BANK : a * S + (half + 1) * BANK],
+                rhs=v_codes[a][:, col : col + width].bitcast(FP8X4),
+                rhs_scale=v_sc[:, a * S + col : a * S + col + width],
                 start=(a == 0),
                 stop=(a == PASSES - 1),
             )
 
-        def empty_bank(j, half):
-            nc.scalar.copy(out=h[j][:, half * BANK : (half + 1) * BANK], in_=banks[(j, half)][:])
+        def empty_bank(j, half, first=0, width=BANK):
+            col = half * BANK + first
+            nc.scalar.copy(out=h[j][:, col : col + width], in_=banks[(j, half, first)][:])
 
         def fill_bank(j, half):
             for a in range(PASSES):
                 first_stage_pass(j, half, a)
             empty_bank(j, half)
 
-        def pick_theme(j):
-            theme[j] = tile([P, NP], F32, f"theme{j}", AT_W2_00 + LAP + 2048 * j if j < 2 else None)
-            nc.vector.tensor_copy(theme[j][:], h[j][:].indirect(pos1_sb[:]))
+        WHOLE = slice(0, NP)
+        HALVES = [slice(0, NP // 2), slice(NP // 2, NP)]
 
-        def take_sine(j):
-            sines[j] = tile([P, NP], F32, f"sine{j}", sine_place(j))
-            nc.scalar.activation(out=sines[j][:], in_=theme[j][:], func=ACT.Sin, bias=per_channel(0, j))
+        def pick_theme(j, cols=WHOLE):
+            if cols.start == 0:
+                theme[j] = tile([P, NP], F32, f"theme{j}")
+            picks = pos1_sb[:, cols.start // 16 : cols.stop // 16]
+            nc.vector.tensor_copy(theme[j][:, cols], h[j][:].indirect(picks))
 
-        def scale_by_amp(j):
-            rows = z_rows[j // 4][:, j % 4, :]
+        def take_sine(j, cols=WHOLE):
+            if cols.start == 0:
+                sines[j] = tile([P, NP], F32, f"sine{j}", sine_place(j))
+            nc.scalar.activation(out=sines[j][:, cols], in_=theme[j][:, cols], func=ACT.Sin, bias=per_channel(0, j))
+
+        def scale_by_amp(j, cols=WHOLE):
+            rows = z_rows[j // 4][:, j % 4, cols]
             if j in AMP_ON_VECTOR:
-                nc.vector.tensor_scalar(out=rows, in0=sines[j][:], scalar1=per_channel(1, j), scalar2=None, op0=ALU.mult)
+                nc.vector.tensor_scalar(
+                    out=rows, in0=sines[j][:, cols], scalar1=per_channel(1, j), scalar2=None, op0=ALU.mult
+                )
             else:
-                nc.scalar.activation(out=rows, in_=sines[j][:], func=ACT.Copy, scale=per_channel(1, j))
+                nc.scalar.activation(out=rows, in_=sines[j][:, cols], func=ACT.Copy, scale=per_channel(1, j))
 
         z_grouped = {}
-        HALF = NP // 2
 
-        def group_z(b, half):
-            z_grouped[(b, half)] = tile([P, 4 * HALF], BF16, f"z_grouped{b}_{half}")
+        def group_z(b, cols):
+            grouped = tile([P, 4 * (cols.stop - cols.start)], BF16, f"z_grouped{b}_{cols.start}")
             nc.vector.tensor_copy(
-                out=z_grouped[(b, half)][:].rearrange("p (c i t) -> p c t i", i=4, t=4),
-                in_=z_rows[b][:, :, half * HALF : (half + 1) * HALF].rearrange("p t (c i) -> p c t i", i=4),
+                out=grouped[:].rearrange("p (c i t) -> p c t i", i=4, t=4),
+                in_=z_rows[b][:, :, cols].rearrange("p t (c i) -> p c t i", i=4),
             )
+            z_grouped[(b, cols.start)] = grouped
 
-        def quantize_z(b, half):
-            cols = slice(half * HALF, (half + 1) * HALF)
+        def quantize_z(b, cols):
             nc.vector.quantize_mx(
-                out=z_codes[b][:, cols].bitcast(FP8X4), scales=z_sc[b][:, cols], in_=z_grouped[(b, half)][:]
+                out=z_codes[b][:, cols].bitcast(FP8X4), scales=z_sc[b][:, cols], in_=z_grouped[(b, cols.start)][:]
             )
 
-        for j, half in ((0, 0), (0, 1), (1, 0)):
-            first_stage_pass(j, half, 0)
+        EARLY = [(0, 0, 0, BANK), (0, 1, 0, BANK // 2), (0, 1, BANK // 2, BANK // 2), (1, 0, 0, BANK), (1, 1, 0, BANK)]
+        for j, half, first, width in EARLY:
+            first_stage_pass(j, half, 0, first, width)
         order_vectors()
-        for j in range(2):
-            order_codes(j, nc.scalar.copy, U32, 1, 2, AT_LATER_CODES[j])
-        turn_vectors()
-        for a in (1, 2):
-            for half in range(2):
-                first_stage_pass(0, half, a)
-                if a == 2:
-                    empty_bank(0, half)
-        first_stage_pass(1, 0, 1)
-        first_stage_pass(1, 0, 2)
-        empty_bank(1, 0)
-        group_w2(0, 0, None, nc.vector.tensor_copy)
+        for j, half, first, width in EARLY[:3]:
+            first_stage_pass(j, half, 1, first, width)
+        for j in range(4):
+            order_codes(j, nc.scalar.copy, U32, 2, 1)
+        order_codes(1, nc.scalar.copy, U32, 1, 1)
+        for j, half, first, width in EARLY[:3]:
+            first_stage_pass(j, half, 2, first, width)
+            empty_bank(j, half, first, width)
+        for half in range(2):
+            first_stage_pass(1, half, 1)
+            first_stage_pass(1, half, 2)
+            empty_bank(1, half)
+        for j in range(4, TILES):
+            order_codes(j, nc.vector.tensor_copy, I32, 0, PASSES)
+        order_codes(2, nc.vector.tensor_copy, I32, 0, 2)
+        order_scales(1, nc.vector.tensor_copy, I32)
         pick_theme(0)
-        fill_bank(1, 1)
-        for j in range(3, TILES):
-            order_codes(j, nc.vector.tensor_copy, I32)
         pick_theme(1)
         fill_bank(2, 0)
+        turn_vectors()
         take_sine(0)
         fill_bank(2, 1)
         scale_by_amp(0)
-        quantize_w2(0, 0, after_codes(2))
         pick_theme(2)
         fill_bank(3, 0)
         fill_bank(3, 1)
+        group_w2(0, 0, after_codes(3), nc.vector.tensor_copy)
+        load_w2(1, 1, AT_TAB0 + LAP)
         pick_theme(3)
         for j in range(1, TILES - 3):
             take_sine(j)
-            if j == 1:
-                load_w2(1, 1, AT_W2_00)
             fill_bank(j + 3, 0)
             scale_by_amp(j)
             fill_bank(j + 3, 1)
             if j == 1:
+                quantize_w2(0, 0, None, at_codes(4) + LAP, range(2))
                 group_w2(1, 0, after_codes(4), nc.vector.tensor_copy)
             if j == 2:
                 quantize_w2(1, 0, after_codes(5))
             if j == 3:
-                group_z(0, 0)
-                group_z(0, 1)
-            pick_theme(j + 3)
+                group_z(0, WHOLE)
+            for cols in HALVES if j + 3 == TILES - 1 else [WHOLE]:
+                pick_theme(j + 3, cols)
             if j == 3:
-                quantize_z(0, 0)
-                quantize_z(0, 1)
+                quantize_z(0, WHOLE)
         take_sine(5)
         group_w2(0, 1, "theme5", nc.vector.tensor_copy)
         take_sine(6)
+        quantize_w2(0, 0, "theme6", None, range(2, 4))
         scale_by_amp(5)
         scale_by_amp(6)
-        take_sine(7)
-        scale_by_amp(7)
+        for cols in HALVES:
+            take_sine(7, cols)
+        for cols in HALVES:
+            scale_by_amp(7, cols)
 
-        group_z(1, 0)
-        group_z(1, 1)
-        quantize_z(1, 0)
-        quantize_z(1, 1)
-        group_w2(1, 1, "sine7", nc.scalar.copy)
+        for cols in HALVES:
+            group_z(1, cols)
+        for cols in HALVES:
+            quantize_z(1, cols)
+        group_w2(1, 1, "sine7", nc.scalar.copy, range(3))
+        group_w2(1, 1, "sine7", nc.vector.tensor_copy, [3])
         quantize_w2(0, 1, "z_rows1")
         quantize_w2(1, 1, "z_grouped1_0")
 
-        out_view = out.rearrange("(b g t i) m -> b t g i m", b=GROUPS, g=16, t=4)
+        out_view = out.rearrange("(b o t i) m -> b t o i m", b=GROUPS, o=32, t=4)
         y_of, y_sb, diffs, squares = {}, {}, {}, {}
 
-        def predict(j):
+        def predict(j, bank, cols=WHOLE):
             c, u = j // 4, j % 4
-            y = psum.tile([P, NP], F32, name=f"y{j}", tag=f"bank{j + 4 if j < 4 else (j + 1) % 4}")
+            y = psum.tile([P, cols.stop - cols.start], F32, name=f"y{j}_{cols.start}", tag=f"bank{bank}")
             for b in range(GROUPS):
                 nc.tensor.matmul_mx(
                     out=y[:],
-                    lhsT=w2_codes[(b, c)][:, u * P : (u + 1) * P].bitcast(FP8X4),
-                    lhsT_scale=w2_sc[(b, c)][:, u * P : (u + 1) * P],
-                    rhs=z_codes[b][:].bitcast(FP8X4),
-                    rhs_scale=z_sc[b][:],
+                    lhsT=w2_codes[(b, c, u)].bitcast(FP8X4),
+                    lhsT_scale=w2_sc[(b, c, u)],
+                    rhs=z_codes[b][:, cols].bitcast(FP8X4),
+                    rhs_scale=z_sc[b][:, cols],
                     start=(b == 0),
                     stop=(b == GROUPS - 1),
                 )
-            y_of[j] = y
+            y_of[(j, cols.start)] = y
 
-        def fetch_y(j, cols=slice(0, NP)):
-            y_sb[(j, cols.start)] = tile([P, cols.stop - cols.start], F32, f"y_sb{j}_{cols.start}")
-            nc.scalar.copy(out=y_sb[(j, cols.start)][:], in_=y_of[j][:, cols])
+        def fetch_y(j, cols=WHOLE):
+            if cols.start == 0:
+                y_sb[j] = tile([P, NP], F32, f"y_sb{j}")
+            nc.scalar.copy(out=y_sb[j][:, cols], in_=y_of[(j, cols.start)][:])
 
-        def subtract(j, cols=slice(0, NP), place=None):
-            diff = tile([P, cols.stop - cols.start], F32, f"diff{j}_{cols.start}", place)
+        def subtract(j, cols=WHOLE):
+            if cols.start == 0:
+                diffs[j] = tile([P, NP], F32, f"diff{j}")
             picked = h[j][:].indirect(pos2_sb[:, cols.start // 16 : cols.stop // 16])
-            nc.vector.tensor_tensor(out=diff[:], in0=picked, in1=y_sb[(j, cols.start)][:], op=ALU.subtract)
-            diffs[(j, cols.start)] = diff
+            nc.vector.tensor_tensor(out=diffs[j][:, cols], in0=picked, in1=y_sb[j][:, cols], op=ALU.subtract)
 
-        def square_on_scalar(j):
-            squares[j] = tile([P, NP], F32, f"square{j}", AT_TAB2 + 2048 if j == 5 else f"square{j % 2}")
-            nc.scalar.activation(out=squares[j][:], in_=diffs[(j, 0)][:], func=ACT.Square)
+        def square_on_scalar(j, cols=WHOLE):
+            if j not in squares:
+                squares[j] = tile([P, NP], F32, f"square{j}", AT_TAB2 + 2048 if j == 5 else f"square{j % 2}")
+            nc.scalar.activation(out=squares[j][:, cols], in_=diffs[j][:, cols], func=ACT.Square)
 
-        def weigh_on_scalar(j, queue=nc.sync):
-            mark = tile([P, NP], F32, f"mark{j}", AT_TAB1 + 2048 * j if j < 4 else None)
-            nc.scalar.activation(out=mark[:], in_=squares[j][:], func=ACT.Copy, scale=per_channel(2, j))
-            queue.dma_start(out=out_view[j // 4, j % 4], in_=mark[:])
+        def weigh_on_scalar(j, cols=WHOLE, queue=nc.sync):
+            place = AT_TAB1 + LAP + 2048 * j if j < 4 else None
+            mark = tile([P, cols.stop - cols.start], F32, f"mark{j}_{cols.start}", place)
+            nc.scalar.activation(out=mark[:], in_=squares[j][:, cols], func=ACT.Copy, scale=per_channel(2, j))
+            queue.dma_start(out=out_view[j // 4, j % 4][:, :, cols], in_=mark[:])
 
         def finish_on_vector(j, cols=slice(0, NP), queue=nc.sync, place=None):
             mark = tile([P, cols.stop - cols.start], F32, f"mark{j}_{cols.start}", place)
-            diff = diffs[(j, cols.start)][:]
+            diff = diffs[j][:, cols]
             nc.vector.scalar_tensor_tensor(
                 out=mark[:], in0=diff, scalar=per_channel(2, j), in1=diff, op0=ALU.mult, op1=ALU.mult
             )
             queue.dma_start(out=out_view[j // 4, j % 4][:, :, cols], in_=mark[:])
 
-        for j in range(TILES):
-            predict(j)
+        for n, cols in enumerate(HALVES):
+            predict(0, 5 + n, cols)
+        for j in range(1, TILES):
+            predict(j, (7, 2, 3, 0, 4, 1, 5)[j - 1])
         parts = [slice(0, 3 * NP // 4), slice(3 * NP // 4, NP)]
-        for j in range(TILES - 1):
+        for cols in HALVES:
+            fetch_y(0, cols)
+        for j in range(1, TILES):
             fetch_y(j)
-        for part in parts:
-            fetch_y(7, part)
-        for j in range(3):
+        for cols in HALVES:
+            subtract(0, cols)
+        for j in range(1, 3):
             subtract(j)
         finish_on_vector(0, place="z_codes1")
         for j in range(3, 7):
             subtract(j)
         square_on_scalar(1)
-        for j in range(2, 7):
+        for j in range(2, 6):
             square_on_scalar(j)
             weigh_on_scalar(j - 1)
-        weigh_on_scalar(6, nc.scalar)
+        weigh_on_scalar(5)
+        for cols in HALVES:
+            square_on_scalar(6, cols)
+        for cols in HALVES:
+            weigh_on_scalar(6, cols, nc.scalar)
         subtract(7, parts[0])
         subtract(7, parts[1])
         finish_on_vector(7, parts[0], place=AT_TAB2 + 512 + LAP)

@@ -25,10 +25,11 @@ BANK = 512
 LAST0 = P - 16 * PASSES
 PAIR0 = LAST0 + 16
 VEC_ROWS = 3 * GROUPS
-VEC0 = 96
+VEC0 = P - VEC_ROWS
+SPARE0 = 96
 LAP = 64
 SPARE_BANK = 5
-AMP_ON_VECTOR = ()
+AMP_ON_VECTOR = (5,)
 FILL_ORDER = [(0, 0), (0, 1), (1, 0), (1, 1)] + [(j, half) for j in range(2, TILES) for half in range(2)]
 BANK_OF = {key: (n if n < 5 else (n - 4) % 5 if n < 8 else (0, 4, 1, 2, 3)[(n - 8) % 5]) for n, key in enumerate(FILL_ORDER)}
 CODE_BYTES = PASSES * 2 * P
@@ -92,13 +93,13 @@ def tile_list_passacaglia_variation_surprise_kernel(
             out=tab_sc[PAIR0:P, :].bitcast(I32), in_=tab_scales[0:2].rearrange("a q t -> q a t").bitcast(I32)
         )
         vec_rows = tile([P, 512], F32, "vec_rows")
-        make_identity(nc, ident[:])
-        nc.vector.memset(vec_rows[VEC0:P, :], 0.0)
+        nc.vector.memset(vec_rows[SPARE0:VEC0, :], 0.0)
         for v, vector in enumerate((phase, amp, mrg)):
             first = VEC0 + GROUPS * v
             nc.gpsimd.dma_start(
                 out=vec_rows[first : first + GROUPS, :], in_=vector.rearrange("(b c) -> b c", b=GROUPS)
             )
+        make_identity(nc, ident[:])
         nc.sync.dma_start(pos1_sb[:], pos1)
         load_tab(0)
         nc.sync.dma_start(pos2_sb[:], pos2)
@@ -125,7 +126,9 @@ def tile_list_passacaglia_variation_surprise_kernel(
         nc.vector.memset(zeros[:], 0.0)
         nc.vector.memset(tab_sc[0:LAST0, :].bitcast(I32), 0)
         nc.vector.memset(v_sc[:].bitcast(I32), 0)
-        nc.scalar.activation(out=vec_rows[0:VEC0, :], in_=zeros[0:VEC0, 0:1].to_broadcast([VEC0, 512]), func=ACT.Sin)
+        nc.scalar.activation(
+            out=vec_rows[0:SPARE0, :], in_=zeros[0:SPARE0, 0:1].to_broadcast([SPARE0, 512]), func=ACT.Sin
+        )
         load_tab(1)
 
         picked_sc = tile([P, S], U8, "picked_sc")
@@ -247,7 +250,7 @@ def tile_list_passacaglia_variation_surprise_kernel(
         theme, sines, banks = {}, {}, {}
         z_rows = [tile([P, 4, NP], BF16, f"z_rows{b}") for b in range(GROUPS)]
         z_codes = [tile([P, NP], U32, f"z_codes{b}") for b in range(GROUPS)]
-        z_sc = [tile([P, NP], U8, f"z_sc{b}", None if b else after_codes(7)) for b in range(GROUPS)]
+        z_sc = [tile([P, NP], U8, f"z_sc{b}", None if b else sine_place(4)) for b in range(GROUPS)]
 
         def first_stage_pass(j, half, a, first=0, width=BANK):
             if a == 0:
@@ -332,43 +335,40 @@ def tile_list_passacaglia_variation_surprise_kernel(
             order_codes(j, nc.vector.tensor_copy, I32, 0, PASSES)
         order_codes(2, nc.vector.tensor_copy, I32, 0, 2)
         order_scales(1, nc.vector.tensor_copy, I32)
+        for j in range(2, TILES):
+            fill_bank(j, 0)
+            if j == 2:
+                turn_vectors()
+            fill_bank(j, 1)
         pick_theme(0)
         pick_theme(1)
-        fill_bank(2, 0)
-        turn_vectors()
-        take_sine(0)
-        fill_bank(2, 1)
-        scale_by_amp(0)
-        pick_theme(2)
-        fill_bank(3, 0)
-        fill_bank(3, 1)
-        group_w2(0, 0, after_codes(3), nc.vector.tensor_copy)
+        group_w2(0, 0, "w1_codes0_0", nc.vector.tensor_copy)
         load_w2(1, 1, AT_TAB0 + LAP)
+        pick_theme(2)
+        quantize_w2(0, 0, None, after_codes(3), range(2))
         pick_theme(3)
-        for j in range(1, TILES - 3):
+        group_w2(1, 0, after_codes(4), nc.vector.tensor_copy)
+        pick_theme(4)
+        group_w2(0, 1, after_codes(5), nc.vector.tensor_copy)
+        pick_theme(5)
+        pick_theme(6)
+        pick_theme(7)
+        for j in range(3):
             take_sine(j)
-            fill_bank(j + 3, 0)
             scale_by_amp(j)
-            fill_bank(j + 3, 1)
-            if j == 1:
-                quantize_w2(0, 0, None, at_codes(4) + LAP, range(2))
-                group_w2(1, 0, after_codes(4), nc.vector.tensor_copy)
-            if j == 2:
-                quantize_w2(1, 0, after_codes(5))
-            if j == 3:
-                group_z(0, WHOLE)
-            for cols in HALVES if j + 3 == TILES - 1 else [WHOLE]:
-                pick_theme(j + 3, cols)
-            if j == 3:
-                quantize_z(0, WHOLE)
+        take_sine(3)
+        take_sine(4)
+        scale_by_amp(3)
+        group_z(0, WHOLE)
         take_sine(5)
-        group_w2(0, 1, "theme5", nc.vector.tensor_copy)
-        take_sine(6)
-        quantize_w2(0, 0, "theme6", None, range(2, 4))
+        scale_by_amp(4)
         scale_by_amp(5)
+        quantize_z(0, WHOLE)
+        take_sine(6)
+        quantize_w2(1, 0, "theme6")
+        take_sine(7, HALVES[0])
         scale_by_amp(6)
-        for cols in HALVES:
-            take_sine(7, cols)
+        take_sine(7, HALVES[1])
         for cols in HALVES:
             scale_by_amp(7, cols)
 
@@ -376,13 +376,13 @@ def tile_list_passacaglia_variation_surprise_kernel(
             group_z(1, cols)
         for cols in HALVES:
             quantize_z(1, cols)
-        group_w2(1, 1, "sine7", nc.scalar.copy, range(3))
-        group_w2(1, 1, "sine7", nc.vector.tensor_copy, [3])
+        group_w2(1, 1, "sine7", nc.scalar.copy)
+        quantize_w2(0, 0, "z_grouped1_0", None, range(2, 4))
         quantize_w2(0, 1, "z_rows1")
-        quantize_w2(1, 1, "z_grouped1_0")
+        quantize_w2(1, 1, None)
 
         out_view = out.rearrange("(b o t i) m -> b t o i m", b=GROUPS, o=32, t=4)
-        y_of, y_sb, diffs, squares = {}, {}, {}, {}
+        y_of, y_sb, diffs, diff_of, squares = {}, {}, {}, {}, {}
 
         def predict(j, bank, cols=WHOLE):
             c, u = j // 4, j % 4
@@ -404,26 +404,36 @@ def tile_list_passacaglia_variation_surprise_kernel(
                 y_sb[j] = tile([P, NP], F32, f"y_sb{j}")
             nc.scalar.copy(out=y_sb[j][:, cols], in_=y_of[(j, cols.start)][:])
 
-        def subtract(j, cols=WHOLE):
-            if cols.start == 0:
-                diffs[j] = tile([P, NP], F32, f"diff{j}")
+        def subtract(j, cols=WHOLE, place=None):
+            if place is not None:
+                diff = tile([P, cols.stop - cols.start], F32, f"diff{j}_{cols.start}", place)[:]
+            else:
+                if cols.start == 0:
+                    diffs[j] = tile([P, NP], F32, f"diff{j}")
+                diff = diffs[j][:, cols]
+            diff_of[(j, cols.start)] = diff
             picked = h[j][:].indirect(pos2_sb[:, cols.start // 16 : cols.stop // 16])
-            nc.vector.tensor_tensor(out=diffs[j][:, cols], in0=picked, in1=y_sb[j][:, cols], op=ALU.subtract)
+            nc.vector.tensor_tensor(out=diff, in0=picked, in1=y_sb[j][:, cols], op=ALU.subtract)
 
         def square_on_scalar(j, cols=WHOLE):
             if j not in squares:
-                squares[j] = tile([P, NP], F32, f"square{j}", AT_TAB2 + 2048 if j == 5 else f"square{j % 2}")
+                squares[j] = tile([P, NP], F32, f"square{j}", AT_TAB2 + 2048 if j == 3 else f"square{j % 3}")
             nc.scalar.activation(out=squares[j][:, cols], in_=diffs[j][:, cols], func=ACT.Square)
 
-        def weigh_on_scalar(j, cols=WHOLE, queue=nc.sync):
+        marks = {}
+
+        def store(j, cols=WHOLE, queue=nc.sync):
+            queue.dma_start(out=out_view[j // 4, j % 4][:, :, cols], in_=marks[(j, cols.start)][:])
+
+        def weigh_on_scalar(j, cols=WHOLE):
             place = AT_TAB1 + LAP + 2048 * j if j < 4 else None
             mark = tile([P, cols.stop - cols.start], F32, f"mark{j}_{cols.start}", place)
             nc.scalar.activation(out=mark[:], in_=squares[j][:, cols], func=ACT.Copy, scale=per_channel(2, j))
-            queue.dma_start(out=out_view[j // 4, j % 4][:, :, cols], in_=mark[:])
+            marks[(j, cols.start)] = mark
 
         def finish_on_vector(j, cols=slice(0, NP), queue=nc.sync, place=None):
             mark = tile([P, cols.stop - cols.start], F32, f"mark{j}_{cols.start}", place)
-            diff = diffs[j][:, cols]
+            diff = diff_of[(j, cols.start)]
             nc.vector.scalar_tensor_tensor(
                 out=mark[:], in0=diff, scalar=per_channel(2, j), in1=diff, op0=ALU.mult, op1=ALU.mult
             )
@@ -433,7 +443,7 @@ def tile_list_passacaglia_variation_surprise_kernel(
             predict(0, 5 + n, cols)
         for j in range(1, TILES):
             predict(j, (7, 2, 3, 0, 4, 1, 5)[j - 1])
-        parts = [slice(0, 3 * NP // 4), slice(3 * NP // 4, NP)]
+        parts = HALVES
         for cols in HALVES:
             fetch_y(0, cols)
         for j in range(1, TILES):
@@ -442,19 +452,23 @@ def tile_list_passacaglia_variation_surprise_kernel(
             subtract(0, cols)
         for j in range(1, 3):
             subtract(j)
-        finish_on_vector(0, place="z_codes1")
         for j in range(3, 7):
             subtract(j)
-        square_on_scalar(1)
-        for j in range(2, 6):
+        subtract(7, parts[0])
+        square_on_scalar(0)
+        for j in range(1, 6):
             square_on_scalar(j)
             weigh_on_scalar(j - 1)
+            if j < 5:
+                store(j - 1)
+        square_on_scalar(6, HALVES[0])
+        store(4, WHOLE, nc.scalar)
         weigh_on_scalar(5)
-        for cols in HALVES:
-            square_on_scalar(6, cols)
-        for cols in HALVES:
-            weigh_on_scalar(6, cols, nc.scalar)
-        subtract(7, parts[0])
-        subtract(7, parts[1])
-        finish_on_vector(7, parts[0], place=AT_TAB2 + 512 + LAP)
-        finish_on_vector(7, parts[1], place=AT_TAB2 + 4096 - LAP)
+        weigh_on_scalar(6, HALVES[0])
+        store(5, WHOLE, nc.scalar)
+        store(6, HALVES[0], nc.scalar)
+        diff_of[(6, HALVES[1].start)] = diffs[6][:, HALVES[1]]
+        finish_on_vector(6, HALVES[1], place=AT_TAB2 + 1024 + LAP)
+        subtract(7, parts[1], AT_TAB2 + 2048 + LAP + 1024)
+        finish_on_vector(7, parts[0], place=AT_TAB2 + 2048 + LAP)
+        finish_on_vector(7, parts[1], nc.scalar, place="diff5")

@@ -1,7 +1,6 @@
 from contextlib import ExitStack
 
 import concourse.mybir as mybir
-from concourse.masks import make_identity
 
 K, T, S, NP, H = 1536, 2048, 1024, 512, 1024
 FLOPS = 2 * K * S * H + 2 * H * H * NP
@@ -24,37 +23,35 @@ TILES = H // P
 BANK = 512
 LAST0 = P - 16 * PASSES
 PAIR0 = LAST0 + 16
-VEC_ROWS = 3 * GROUPS
-VEC0 = P - VEC_ROWS
-SPARE0 = 96
 LAP = 64
-SPARE_BANK = 5
-AMP_ON_VECTOR = (5,)
-FILL_ORDER = [(0, 0), (0, 1), (1, 0), (1, 1)] + [(j, half) for j in range(2, TILES) for half in range(2)]
-BANK_OF = {key: (n if n < 5 else (n - 4) % 5 if n < 8 else (0, 4, 1, 2, 3)[(n - 8) % 5]) for n, key in enumerate(FILL_ORDER)}
+SINE_LAG = 3
+AMP_ON_VECTOR = (0, 1, 2, 3, 4, 5)
 CODE_BYTES = PASSES * 2 * P
-AT_W1_GROUP1 = 0
+AT_FIRST_GROUPED = 0
+AT_W1_GROUP1 = AT_FIRST_GROUPED + 4096 - LAP
 AT_TAB0 = AT_W1_GROUP1 + 3072 - LAP
-AT_TAB1 = AT_TAB0 + 8192
+AT_W1_FIRST = AT_TAB0 + 8192
+AT_TAB1 = AT_W1_FIRST + 2048
 AT_W1_LATER = AT_TAB1 + 8192 + LAP
 AT_TAB_SC = AT_W1_LATER + 2048 - LAP
 AT_TAB2 = AT_TAB_SC + 2048 - LAP
 CHAIN0 = AT_TAB2 + 8192
-STEP = 2048 + CODE_BYTES + 4096
+STEP = 2048 + CODE_BYTES
 
 
 def at_codes(j):
     return CHAIN0 + (j - 1) * STEP + 2048 - LAP
 
 
+AT_Z_ROWS = at_codes(TILES - 1) + CODE_BYTES - LAP
+AT_THIRD_CHUNK = AT_Z_ROWS + 4096 - LAP
+AT_SECOND_PASS = AT_THIRD_CHUNK + 8192 - LAP
+
+
 def sine_place(j):
-    if j >= TILES - 2:
+    if j + SINE_LAG >= TILES:
         return None
-    return at_codes(j + 2 if j else 1) - 2048 + LAP
-
-
-def after_codes(j):
-    return at_codes(j) + CODE_BYTES - LAP
+    return at_codes(j + SINE_LAG) - 2048 + LAP
 
 
 def tile_list_passacaglia_variation_surprise_kernel(
@@ -78,7 +75,6 @@ def tile_list_passacaglia_variation_surprise_kernel(
 
         tab_sc = tile([P, T], U8, "tab_sc", AT_TAB_SC)
         v_sc = tile([P, PASSES * S], U8, "v_sc")
-        ident = tile([P, P], F32, "ident")
         zeros = tile([P, 16], F32, "zeros")
         tabs = []
 
@@ -92,19 +88,16 @@ def tile_list_passacaglia_variation_surprise_kernel(
         nc.scalar.dma_start(
             out=tab_sc[PAIR0:P, :].bitcast(I32), in_=tab_scales[0:2].rearrange("a q t -> q a t").bitcast(I32)
         )
-        vec_rows = tile([P, 512], F32, "vec_rows")
-        nc.vector.memset(vec_rows[SPARE0:VEC0, :], 0.0)
+        vec_rows = tile([P, P], F32, "vec_rows")
+        nc.vector.memset(zeros[:], 0.0)
+        nc.scalar.activation(out=vec_rows[:], in_=zeros[:, 0:1].to_broadcast([P, P]), func=ACT.Sin)
         for v, vector in enumerate((phase, amp, mrg)):
-            first = VEC0 + GROUPS * v
-            nc.gpsimd.dma_start(
-                out=vec_rows[first : first + GROUPS, :], in_=vector.rearrange("(b c) -> b c", b=GROUPS)
-            )
-        make_identity(nc, ident[:])
+            nc.gpsimd.dma_start(out=vec_rows[v:P:16, :], in_=vector.rearrange("(b q c) -> q b c", b=GROUPS, q=4))
         nc.sync.dma_start(pos1_sb[:], pos1)
         load_tab(0)
         nc.sync.dma_start(pos2_sb[:], pos2)
         w1_raw = {}
-        w1_sc_raw = tile([P, PASSES * 128], I32, "w1_sc_raw")
+        w1_sc_raw = tile([P, PASSES, 256], I32, "w1_sc_raw")
         w1_view = w1_words.rearrange("a p (b c) -> b p a c", b=GROUPS)
 
         def load_w1(b, first, count, place):
@@ -113,22 +106,18 @@ def tile_list_passacaglia_variation_surprise_kernel(
             for n in range(count):
                 w1_raw[(b, first + n)] = raw[:, n:count]
 
-        def load_w1_scales(b):
+        def load_w1_scales():
             for r in range(4):
                 nc.sync.dma_start(
-                    out=w1_sc_raw[r:P:32, :].rearrange("p (a c) -> p a c", a=PASSES),
-                    in_=w1_scales[:, r:16:4, b * 512 : (b + 1) * 512].rearrange("a q n -> q a n").bitcast(I32),
+                    out=w1_sc_raw[r:P:32],
+                    in_=w1_scales[:, r:16:4, :].rearrange("a q n -> q a n").bitcast(I32),
                 )
 
-        load_w1(0, 0, 2, None)
+        load_w1(0, 0, 2, AT_W1_FIRST)
         nc.vector.memset(w1_sc_raw[:], 0)
-        load_w1_scales(0)
-        nc.vector.memset(zeros[:], 0.0)
+        load_w1_scales()
         nc.vector.memset(tab_sc[0:LAST0, :].bitcast(I32), 0)
         nc.vector.memset(v_sc[:].bitcast(I32), 0)
-        nc.scalar.activation(
-            out=vec_rows[0:SPARE0, :], in_=zeros[0:SPARE0, 0:1].to_broadcast([SPARE0, 512]), func=ACT.Sin
-        )
         load_tab(1)
 
         picked_sc = tile([P, S], U8, "picked_sc")
@@ -159,8 +148,7 @@ def tile_list_passacaglia_variation_surprise_kernel(
         pick_codes(0)
         pick_codes(1)
         pick_codes(2, 0, BANK)
-        pick_codes(2, BANK, BANK // 2)
-        pick_codes(2, BANK + BANK // 2, BANK // 2)
+        pick_codes(2, BANK, BANK)
 
         w1_codes, w1_sc = {}, []
 
@@ -168,12 +156,12 @@ def tile_list_passacaglia_variation_surprise_kernel(
             sc = tile([P, PASSES * 512], U8, f"w1_sc{b}", None if b else AT_TAB_SC + LAP)
             copy(
                 out=sc[:].bitcast(view).rearrange("p (a t o) -> p a t o", t=4, o=32),
-                in_=w1_sc_raw[:].bitcast(view).rearrange("p (a o t) -> p a t o", t=4, o=32),
+                in_=w1_sc_raw[:, :, 128 * b : 128 * (b + 1)].bitcast(view).rearrange("p a (o t) -> p a t o", t=4),
             )
             w1_sc.append(sc)
 
         code_tiles = {}
-        APART = {(0, 0): None, (0, 1): None, (0, 2): at_codes(2) + LAP, (1, 1): AT_W1_LATER + 1024, (2, 2): None}
+        APART = {(0, 0): None, (0, 1): AT_SECOND_PASS, (0, 2): None}
 
         def order_codes(j, copy, view, first, count):
             if (j, first) in APART:
@@ -190,31 +178,25 @@ def tile_list_passacaglia_variation_surprise_kernel(
             for n in range(count):
                 w1_codes[(j, first + n)] = codes[:, 2 * n * P : 2 * (n + 1) * P]
 
-        for j in (0, 1, 3):
-            order_codes(j, nc.scalar.copy, U32, 0, 2 if j == 3 else 1)
-        order_codes(0, nc.scalar.copy, U32, 1, 1)
+        order_codes(0, nc.scalar.copy, U32, 0, 1)
+        for j in range(1, 4):
+            order_codes(j, nc.scalar.copy, U32, 0, 2)
         order_scales(0, nc.scalar.copy, U32)
-        load_w1_scales(1)
-        vec = tile([P, 4, 8], F32, "vec")
+        order_codes(0, nc.scalar.copy, U32, 1, 1)
+        order_scales(1, nc.scalar.copy, U32)
+        vec = tile([P, 4, 32], F32, "vec")
+        vec_ordered = tile([P, 4, 32], F32, "vec_ordered", "w1_codes0_0")
 
-        vec_ordered = tile([P, 4, P], F32, "vec_ordered", "w1_codes0_0")
-
-        def order_vectors():
+        def turn_vectors():
             nc.scalar.copy(
                 out=vec_ordered[:].rearrange("p t (o i) -> p t o i", i=4),
                 in_=vec_rows[:].rearrange("p (o t i) -> p t o i", t=4, i=4),
             )
-
-        def turn_vectors():
-            vec_ps = psum.tile([P, 4, P], F32, name="vec_ps", tag="bank0")
-            for t in range(4):
-                nc.tensor.transpose(vec_ps[:, t, :], vec_ordered[:, t, :], ident[:])
-            nc.scalar.copy(out=vec[:, :, 0:VEC_ROWS], in_=vec_ps[:, :, VEC0 : VEC0 + VEC_ROWS])
+            nc.vector.transpose(vec[:].rearrange("p t r -> p (t r)"), vec_ordered[:].rearrange("p t c -> p (t c)"))
 
         def per_channel(v, j):
-            col = GROUPS * v + j // 4
+            col = 16 * (j // 4) + v
             return vec[:, j % 4, col : col + 1]
-
 
         w2_view = w2.rearrange("(b o t i) (c n) -> b c t o i n", b=GROUPS, o=32, t=4, c=GROUPS)
         w2_raw, w2_grouped, w2_codes, w2_sc = {}, {}, {}, {}
@@ -232,6 +214,16 @@ def tile_list_passacaglia_variation_surprise_kernel(
             src = w2_raw[(b, c)][:].rearrange("p t (o u l) -> p u o t l", u=4, o=32)
             copy(out=dst[:, quarters[0] : quarters[-1] + 1], in_=src[:, quarters[0] : quarters[-1] + 1])
 
+        def group_w2_on_gpsimd(b, c, place):
+            grouped = tile([P, 4 * 512], BF16, f"w2_grouped{b}{c}", place)
+            dst = grouped[:].rearrange("p (u o l t) -> p u o l t", u=4, o=32, l=4)
+            src = w2_raw[(b, c)][:].rearrange("p t (o u l) -> p u o l t", u=4, o=32)
+            for u in range(4):
+                nc.gpsimd.tensor_scalar(
+                    out=dst[:, u], in0=src[:, u], scalar1=1.0, scalar2=0.0, op0=ALU.mult, op1=ALU.add
+                )
+            w2_grouped[(b, c)] = grouped
+
         def quantize_w2(b, c, place, scale_place=None, tiles=range(4)):
             first, count = tiles[0] * P, len(tiles) * P
             codes = tile([P, count], U32, f"w2_codes{b}{c}_{first}", place)
@@ -243,18 +235,18 @@ def tile_list_passacaglia_variation_surprise_kernel(
                 w2_sc[(b, c, u)] = scales[:, n * P : (n + 1) * P]
 
         load_w2(0, 0, AT_TAB0 + LAP)
-        load_w2(1, 0, AT_TAB1 + LAP)
-        load_w2(0, 1, AT_TAB2)
+        load_w2(1, 0, AT_TAB1 - LAP)
+        load_w2(0, 1, AT_THIRD_CHUNK)
 
         h = [tile([P, S], F32, f"h{j}") for j in range(TILES)]
         theme, sines, banks = {}, {}, {}
-        z_rows = [tile([P, 4, NP], BF16, f"z_rows{b}") for b in range(GROUPS)]
+        z_rows = [tile([P, 4, NP], BF16, f"z_rows{b}", None if b else AT_Z_ROWS) for b in range(GROUPS)]
         z_codes = [tile([P, NP], U32, f"z_codes{b}") for b in range(GROUPS)]
-        z_sc = [tile([P, NP], U8, f"z_sc{b}", None if b else sine_place(4)) for b in range(GROUPS)]
+        z_sc = [tile([P, NP], U8, f"z_sc{b}") for b in range(GROUPS)]
 
         def first_stage_pass(j, half, a, first=0, width=BANK):
             if a == 0:
-                slot = SPARE_BANK if first else BANK_OF[(j, half)]
+                slot = (2 * j + half) % 8
                 banks[(j, half, first)] = psum.tile([P, width], F32, name=f"h_ps{j}_{half}_{first}", tag=f"bank{slot}")
             at = a * 512 + (j % 4) * P
             col = half * BANK + first
@@ -315,69 +307,49 @@ def tile_list_passacaglia_variation_surprise_kernel(
                 out=z_codes[b][:, cols].bitcast(FP8X4), scales=z_sc[b][:, cols], in_=z_grouped[(b, cols.start)][:]
             )
 
-        EARLY = [(0, 0, 0, BANK), (0, 1, 0, BANK // 2), (0, 1, BANK // 2, BANK // 2), (1, 0, 0, BANK), (1, 1, 0, BANK)]
-        for j, half, first, width in EARLY:
-            first_stage_pass(j, half, 0, first, width)
-        order_vectors()
-        for j, half, first, width in EARLY[:3]:
-            first_stage_pass(j, half, 1, first, width)
+        for half in range(2):
+            first_stage_pass(0, half, 0)
+        turn_vectors()
+        for j in range(1, 4):
+            for half in range(2):
+                first_stage_pass(j, half, 0)
         for j in range(4):
             order_codes(j, nc.scalar.copy, U32, 2, 1)
-        order_codes(1, nc.scalar.copy, U32, 1, 1)
-        for j, half, first, width in EARLY[:3]:
-            first_stage_pass(j, half, 2, first, width)
-            empty_bank(j, half, first, width)
-        for half in range(2):
-            first_stage_pass(1, half, 1)
-            first_stage_pass(1, half, 2)
-            empty_bank(1, half)
+        for j, half in ((0, 0), (1, 0), (0, 1), (1, 1), (2, 0), (2, 1), (3, 0), (3, 1)):
+            first_stage_pass(j, half, 1)
+            first_stage_pass(j, half, 2)
+            empty_bank(j, half)
         for j in range(4, TILES):
             order_codes(j, nc.vector.tensor_copy, I32, 0, PASSES)
-        order_codes(2, nc.vector.tensor_copy, I32, 0, 2)
-        order_scales(1, nc.vector.tensor_copy, I32)
-        for j in range(2, TILES):
+        for j in range(4, TILES):
             fill_bank(j, 0)
-            if j == 2:
-                turn_vectors()
             fill_bank(j, 1)
-        pick_theme(0)
-        pick_theme(1)
-        group_w2(0, 0, "w1_codes0_0", nc.vector.tensor_copy)
+        group_w2_on_gpsimd(0, 0, AT_FIRST_GROUPED)
         load_w2(1, 1, AT_TAB0 + LAP)
-        pick_theme(2)
-        quantize_w2(0, 0, None, after_codes(3), range(2))
-        pick_theme(3)
-        group_w2(1, 0, after_codes(4), nc.vector.tensor_copy)
-        pick_theme(4)
-        group_w2(0, 1, after_codes(5), nc.vector.tensor_copy)
-        pick_theme(5)
-        pick_theme(6)
-        pick_theme(7)
-        for j in range(3):
+        group_w2_on_gpsimd(1, 0, None)
+        group_w2_on_gpsimd(0, 1, None)
+        for j in range(TILES):
+            pick_theme(j)
+        for j in range(TILES - 1):
             take_sine(j)
+        for j in range(4):
             scale_by_amp(j)
-        take_sine(3)
-        take_sine(4)
-        scale_by_amp(3)
+        quantize_w2(0, 0, sine_place(1))
         group_z(0, WHOLE)
-        take_sine(5)
-        scale_by_amp(4)
-        scale_by_amp(5)
+        quantize_w2(1, 0, sine_place(3))
         quantize_z(0, WHOLE)
-        take_sine(6)
-        quantize_w2(1, 0, "theme6")
         take_sine(7, HALVES[0])
         scale_by_amp(6)
         take_sine(7, HALVES[1])
+        scale_by_amp(4)
+        scale_by_amp(5)
         for cols in HALVES:
             scale_by_amp(7, cols)
-
         for cols in HALVES:
             group_z(1, cols)
         for cols in HALVES:
             quantize_z(1, cols)
         group_w2(1, 1, "sine7", nc.scalar.copy)
-        quantize_w2(0, 0, "z_grouped1_0", None, range(2, 4))
         quantize_w2(0, 1, "z_rows1")
         quantize_w2(1, 1, None)
 
@@ -440,9 +412,9 @@ def tile_list_passacaglia_variation_surprise_kernel(
             queue.dma_start(out=out_view[j // 4, j % 4][:, :, cols], in_=mark[:])
 
         for n, cols in enumerate(HALVES):
-            predict(0, 5 + n, cols)
+            predict(0, n, cols)
         for j in range(1, TILES):
-            predict(j, (7, 2, 3, 0, 4, 1, 5)[j - 1])
+            predict(j, (j + 1) % 8)
         parts = HALVES
         for cols in HALVES:
             fetch_y(0, cols)

@@ -24,34 +24,38 @@ BANK = 512
 LAST0 = P - 16 * PASSES
 PAIR0 = LAST0 + 16
 LAP = 64
-SINE_LAG = 3
-AMP_ON_VECTOR = (0, 1, 2, 3, 4, 5)
+BANK_OF = (0, 1, 2, 3, 4, 0, 1, 2, 5, 6, 7, 3, 4, 0, 1, 2)
+SINE_LAG = 2
+AMP_ON_VECTOR = (0, 1, 2, 3)
+EARLY_PICKS = (1, 3, 5)
 CODE_BYTES = PASSES * 2 * P
 AT_FIRST_GROUPED = 0
 AT_W1_GROUP1 = AT_FIRST_GROUPED + 4096 - LAP
 AT_TAB0 = AT_W1_GROUP1 + 3072 - LAP
-AT_W1_FIRST = AT_TAB0 + 8192
-AT_TAB1 = AT_W1_FIRST + 2048
-AT_W1_LATER = AT_TAB1 + 8192 + LAP
-AT_TAB_SC = AT_W1_LATER + 2048 - LAP
+AT_TAB1 = AT_TAB0 + 8192 + LAP
+AT_LAST_PASS = AT_TAB1 + 8192 + LAP
+AT_TAB_SC = AT_LAST_PASS + 768
 AT_TAB2 = AT_TAB_SC + 2048 - LAP
 CHAIN0 = AT_TAB2 + 8192
 STEP = 2048 + CODE_BYTES
 
 
 def at_codes(j):
-    return CHAIN0 + (j - 1) * STEP + 2048 - LAP
+    return CHAIN0 + (j - 4) % 8 * STEP + 2048 - LAP
 
 
-AT_Z_ROWS = at_codes(TILES - 1) + CODE_BYTES - LAP
-AT_THIRD_CHUNK = AT_Z_ROWS + 4096 - LAP
-AT_SECOND_PASS = AT_THIRD_CHUNK + 8192 - LAP
+AT_GATE = at_codes(3) + CODE_BYTES
+AT_LAST_CHUNK = AT_GATE + LAP
+AT_SECOND_PASS = AT_LAST_CHUNK + 8192 - LAP
+
+
+AT_LATE_Z = AT_TAB0 + LAP
 
 
 def sine_place(j):
-    if j + SINE_LAG >= TILES:
-        return None
-    return at_codes(j + SINE_LAG) - 2048 + LAP
+    if j + SINE_LAG < TILES:
+        return at_codes(j + SINE_LAG) - 2048 + LAP
+    return f"theme{j - 1}"
 
 
 def tile_list_passacaglia_variation_surprise_kernel(
@@ -79,8 +83,8 @@ def tile_list_passacaglia_variation_surprise_kernel(
         tabs = []
 
         def load_tab(a):
-            tab = tile([P, T], I32, f"tab{a}", (AT_TAB0, AT_TAB1, AT_TAB2)[a])
-            nc.sync.dma_start(out=tab[:], in_=tab_words[a].rearrange("p t i -> p (t i)").bitcast(I32))
+            tab = tile([P, T + (STEP if a == 2 else 0)], I32, f"tab{a}", (AT_TAB0, AT_TAB1, AT_TAB2)[a])[:, 0:T]
+            nc.sync.dma_start(out=tab, in_=tab_words[a].rearrange("p t i -> p (t i)").bitcast(I32))
             tabs.append(tab)
 
         nc.sync.dma_start(offs_sb[:], offs)
@@ -89,8 +93,9 @@ def tile_list_passacaglia_variation_surprise_kernel(
             out=tab_sc[PAIR0:P, :].bitcast(I32), in_=tab_scales[0:2].rearrange("a q t -> q a t").bitcast(I32)
         )
         vec_rows = tile([P, P], F32, "vec_rows")
-        nc.vector.memset(zeros[:], 0.0)
-        nc.scalar.activation(out=vec_rows[:], in_=zeros[:, 0:1].to_broadcast([P, P]), func=ACT.Sin)
+        nc.gpsimd.memset(vec_rows[:], 0.0)
+        nc.vector.memset(zeros[:, 0:1], 0.0)
+        nc.scalar.activation(out=zeros[:, 8:9], in_=zeros[:, 0:1], func=ACT.Sin)
         for v, vector in enumerate((phase, amp, mrg)):
             nc.gpsimd.dma_start(out=vec_rows[v:P:16, :], in_=vector.rearrange("(b q c) -> q b c", b=GROUPS, q=4))
         nc.sync.dma_start(pos1_sb[:], pos1)
@@ -113,7 +118,7 @@ def tile_list_passacaglia_variation_surprise_kernel(
                     in_=w1_scales[:, r:16:4, :].rearrange("a q n -> q a n").bitcast(I32),
                 )
 
-        load_w1(0, 0, 2, AT_W1_FIRST)
+        load_w1(0, 0, PASSES, None)
         nc.vector.memset(w1_sc_raw[:], 0)
         load_w1_scales()
         nc.vector.memset(tab_sc[0:LAST0, :].bitcast(I32), 0)
@@ -134,7 +139,6 @@ def tile_list_passacaglia_variation_surprise_kernel(
                 in_=picked_sc[LAST0 + 4 * q : LAST0 + 4 * q + 4, :].bitcast(I32),
             )
 
-        load_w1(0, 2, 1, AT_W1_LATER + 1024)
         load_w1(1, 0, PASSES, AT_W1_GROUP1)
 
         v_codes = [tile([P, S], U32, f"v_codes{a}") for a in range(PASSES)]
@@ -142,7 +146,7 @@ def tile_list_passacaglia_variation_surprise_kernel(
         def pick_codes(a, first=0, width=S):
             nc.vector.tensor_copy(
                 v_codes[a][:, first : first + width],
-                tabs[a][:].bitcast(U32).indirect(offs_sb[:, first // 16 : (first + width) // 16]),
+                tabs[a].bitcast(U32).indirect(offs_sb[:, first // 16 : (first + width) // 16]),
             )
 
         pick_codes(0)
@@ -161,11 +165,13 @@ def tile_list_passacaglia_variation_surprise_kernel(
             w1_sc.append(sc)
 
         code_tiles = {}
-        APART = {(0, 0): None, (0, 1): AT_SECOND_PASS, (0, 2): None}
+        APART = {(0, 0): None, (0, 1): AT_SECOND_PASS, (0, 2): AT_LAST_PASS}
+        APART.update({(j, 2): AT_LAST_PASS + 256 * j for j in (1, 2)})
 
         def order_codes(j, copy, view, first, count):
             if (j, first) in APART:
-                codes = tile([P, count * 2 * P], U8, f"w1_codes{j}_{first}", APART[(j, first)])[:]
+                width = CODE_BYTES if (j, first) == (0, 2) else count * 2 * P
+                codes = tile([P, width], U8, f"w1_codes{j}_{first}", APART[(j, first)])[:, 0 : count * 2 * P]
             else:
                 if j not in code_tiles:
                     code_tiles[j] = tile([P, CODE_BYTES], U8, f"w1_codes{j}", at_codes(j))
@@ -180,19 +186,20 @@ def tile_list_passacaglia_variation_surprise_kernel(
 
         order_codes(0, nc.scalar.copy, U32, 0, 1)
         for j in range(1, 4):
-            order_codes(j, nc.scalar.copy, U32, 0, 2)
+            order_codes(j, nc.scalar.copy, U32, 0, PASSES if j == 3 else 2)
         order_scales(0, nc.scalar.copy, U32)
         order_codes(0, nc.scalar.copy, U32, 1, 1)
+        order_codes(0, nc.scalar.copy, U32, 2, 1)
         order_scales(1, nc.scalar.copy, U32)
         vec = tile([P, 4, 32], F32, "vec")
-        vec_ordered = tile([P, 4, 32], F32, "vec_ordered", "w1_codes0_0")
+        vec_ordered = tile([P, P], F32, "vec_ordered", "w1_codes0_0")[:]
 
         def turn_vectors():
             nc.scalar.copy(
-                out=vec_ordered[:].rearrange("p t (o i) -> p t o i", i=4),
+                out=vec_ordered.rearrange("p (t o i) -> p t o i", t=4, i=4),
                 in_=vec_rows[:].rearrange("p (o t i) -> p t o i", t=4, i=4),
             )
-            nc.vector.transpose(vec[:].rearrange("p t r -> p (t r)"), vec_ordered[:].rearrange("p t c -> p (t c)"))
+            nc.vector.transpose(vec[:].rearrange("p t r -> p (t r)"), vec_ordered)
 
         def per_channel(v, j):
             col = 16 * (j // 4) + v
@@ -206,13 +213,6 @@ def tile_list_passacaglia_variation_surprise_kernel(
             for t in range(4):
                 nc.sync.dma_start(out=raw[:, t, :], in_=w2_view[b, c, t])
             w2_raw[(b, c)] = raw
-
-        def group_w2(b, c, place, copy, quarters=range(4)):
-            if (b, c) not in w2_grouped:
-                w2_grouped[(b, c)] = tile([P, 4 * 512], BF16, f"w2_grouped{b}{c}", place)
-            dst = w2_grouped[(b, c)][:].rearrange("p (u o l t) -> p u o t l", u=4, o=32, l=4)
-            src = w2_raw[(b, c)][:].rearrange("p t (o u l) -> p u o t l", u=4, o=32)
-            copy(out=dst[:, quarters[0] : quarters[-1] + 1], in_=src[:, quarters[0] : quarters[-1] + 1])
 
         def group_w2_on_gpsimd(b, c, place):
             grouped = tile([P, 4 * 512], BF16, f"w2_grouped{b}{c}", place)
@@ -235,18 +235,19 @@ def tile_list_passacaglia_variation_surprise_kernel(
                 w2_sc[(b, c, u)] = scales[:, n * P : (n + 1) * P]
 
         load_w2(0, 0, AT_TAB0 + LAP)
-        load_w2(1, 0, AT_TAB1 - LAP)
-        load_w2(0, 1, AT_THIRD_CHUNK)
+        load_w2(1, 0, AT_TAB1)
+        load_w2(0, 1, AT_TAB2)
+        load_w2(1, 1, AT_LAST_CHUNK)
 
         h = [tile([P, S], F32, f"h{j}") for j in range(TILES)]
         theme, sines, banks = {}, {}, {}
-        z_rows = [tile([P, 4, NP], BF16, f"z_rows{b}", None if b else AT_Z_ROWS) for b in range(GROUPS)]
-        z_codes = [tile([P, NP], U32, f"z_codes{b}") for b in range(GROUPS)]
+        z_rows = [tile([P, 4, NP], BF16, f"z_rows{b}", None if b else AT_LAST_CHUNK) for b in range(GROUPS)]
+        z_codes = [tile([P, NP], U32, "z_codes0")]
         z_sc = [tile([P, NP], U8, f"z_sc{b}") for b in range(GROUPS)]
 
         def first_stage_pass(j, half, a, first=0, width=BANK):
             if a == 0:
-                slot = (2 * j + half) % 8
+                slot = BANK_OF[2 * j + half]
                 banks[(j, half, first)] = psum.tile([P, width], F32, name=f"h_ps{j}_{half}_{first}", tag=f"bank{slot}")
             at = a * 512 + (j % 4) * P
             col = half * BANK + first
@@ -274,9 +275,15 @@ def tile_list_passacaglia_variation_surprise_kernel(
 
         def pick_theme(j, cols=WHOLE):
             if cols.start == 0:
-                theme[j] = tile([P, NP], F32, f"theme{j}")
+                theme[j] = tile([P, NP], F32, f"theme{j}", None if j else AT_W1_GROUP1 + LAP)
             picks = pos1_sb[:, cols.start // 16 : cols.stop // 16]
             nc.vector.tensor_copy(theme[j][:, cols], h[j][:].indirect(picks))
+
+        actual = {}
+
+        def pick_actual(j):
+            actual[j] = tile([P, NP], F32, f"actual{j}")
+            nc.vector.tensor_copy(actual[j][:], h[j][:].indirect(pos2_sb[:]))
 
         def take_sine(j, cols=WHOLE):
             if cols.start == 0:
@@ -294,9 +301,10 @@ def tile_list_passacaglia_variation_surprise_kernel(
 
         z_grouped = {}
 
-        def group_z(b, cols):
-            grouped = tile([P, 4 * (cols.stop - cols.start)], BF16, f"z_grouped{b}_{cols.start}")
-            nc.vector.tensor_copy(
+        def group_z(b, cols, copy):
+            place = AT_LATE_Z if cols.start else None
+            grouped = tile([P, 4 * (cols.stop - cols.start)], BF16, f"z_grouped{b}_{cols.start}", place)
+            copy(
                 out=grouped[:].rearrange("p (c i t) -> p c t i", i=4, t=4),
                 in_=z_rows[b][:, :, cols].rearrange("p t (c i) -> p c t i", i=4),
             )
@@ -310,48 +318,53 @@ def tile_list_passacaglia_variation_surprise_kernel(
         for half in range(2):
             first_stage_pass(0, half, 0)
         turn_vectors()
-        for j in range(1, 4):
-            for half in range(2):
-                first_stage_pass(j, half, 0)
-        for j in range(4):
-            order_codes(j, nc.scalar.copy, U32, 2, 1)
-        for j, half in ((0, 0), (1, 0), (0, 1), (1, 1), (2, 0), (2, 1), (3, 0), (3, 1)):
+        for j, half in ((1, 0), (1, 1), (2, 0)):
+            first_stage_pass(j, half, 0)
+        early = ((0, 0), (0, 1), (1, 0), (1, 1), (2, 0))
+        for j, half in early:
             first_stage_pass(j, half, 1)
+        for j, half in early:
+            if j and not half:
+                order_codes(j, nc.vector.tensor_copy, I32, 2, 1)
             first_stage_pass(j, half, 2)
             empty_bank(j, half)
+        fill_bank(2, 1)
         for j in range(4, TILES):
             order_codes(j, nc.vector.tensor_copy, I32, 0, PASSES)
-        for j in range(4, TILES):
+        for j in range(3, TILES):
             fill_bank(j, 0)
             fill_bank(j, 1)
         group_w2_on_gpsimd(0, 0, AT_FIRST_GROUPED)
-        load_w2(1, 1, AT_TAB0 + LAP)
         group_w2_on_gpsimd(1, 0, None)
         group_w2_on_gpsimd(0, 1, None)
+        group_w2_on_gpsimd(1, 1, None)
         for j in range(TILES):
             pick_theme(j)
+        for j in EARLY_PICKS:
+            pick_actual(j)
         for j in range(TILES - 1):
             take_sine(j)
-        for j in range(4):
+            if j not in AMP_ON_VECTOR:
+                scale_by_amp(j)
+        for j in AMP_ON_VECTOR:
             scale_by_amp(j)
-        quantize_w2(0, 0, sine_place(1))
-        group_z(0, WHOLE)
-        quantize_w2(1, 0, sine_place(3))
+        quantize_w2(0, 0, None, AT_LAST_CHUNK + 4096, range(2))
+        group_z(0, WHOLE, nc.vector.tensor_copy)
+        quantize_w2(1, 0, None, AT_LAST_CHUNK + 4096 + 256, range(2))
         quantize_z(0, WHOLE)
-        take_sine(7, HALVES[0])
-        scale_by_amp(6)
-        take_sine(7, HALVES[1])
-        scale_by_amp(4)
-        scale_by_amp(5)
+        z_codes.append(tile([P, NP], U32, "z_codes1", "z_grouped0_0"))
+        for cols in HALVES:
+            take_sine(7, cols)
         for cols in HALVES:
             scale_by_amp(7, cols)
         for cols in HALVES:
-            group_z(1, cols)
+            group_z(1, cols, nc.scalar.copy)
         for cols in HALVES:
             quantize_z(1, cols)
-        group_w2(1, 1, "sine7", nc.scalar.copy)
-        quantize_w2(0, 1, "z_rows1")
-        quantize_w2(1, 1, None)
+        quantize_w2(0, 0, None, AT_LATE_Z, range(2, 4))
+        quantize_w2(1, 0, None, AT_LATE_Z + 256, range(2, 4))
+        quantize_w2(0, 1, None, AT_LATE_Z + 512)
+        quantize_w2(1, 1, None, AT_LATE_Z + 1024)
 
         out_view = out.rearrange("(b o t i) m -> b t o i m", b=GROUPS, o=32, t=4)
         y_of, y_sb, diffs, diff_of, squares = {}, {}, {}, {}, {}
@@ -384,6 +397,9 @@ def tile_list_passacaglia_variation_surprise_kernel(
                     diffs[j] = tile([P, NP], F32, f"diff{j}")
                 diff = diffs[j][:, cols]
             diff_of[(j, cols.start)] = diff
+            if j in EARLY_PICKS:
+                nc.vector.tensor_tensor(out=diff, in0=actual[j][:], in1=y_of[(j, 0)][:], op=ALU.subtract)
+                return
             picked = h[j][:].indirect(pos2_sb[:, cols.start // 16 : cols.stop // 16])
             nc.vector.tensor_tensor(out=diff, in0=picked, in1=y_sb[j][:, cols], op=ALU.subtract)
 
@@ -411,28 +427,24 @@ def tile_list_passacaglia_variation_surprise_kernel(
             )
             queue.dma_start(out=out_view[j // 4, j % 4][:, :, cols], in_=mark[:])
 
-        for n, cols in enumerate(HALVES):
-            predict(0, n, cols)
-        for j in range(1, TILES):
-            predict(j, (j + 1) % 8)
-        parts = HALVES
-        for cols in HALVES:
-            fetch_y(0, cols)
-        for j in range(1, TILES):
-            fetch_y(j)
-        for cols in HALVES:
-            subtract(0, cols)
-        for j in range(1, 3):
+        for n, j in enumerate((1, 0, 2, 3, 4, 5, 6, 7)):
+            predict(j, n)
+        for j in range(TILES):
+            if j not in EARLY_PICKS:
+                fetch_y(j)
+        subtract(1)
+        subtract(0)
+        finish_on_vector(1)
+        for j in range(2, 7):
             subtract(j)
-        for j in range(3, 7):
-            subtract(j)
-        subtract(7, parts[0])
+        subtract(7, HALVES[0])
+        on_scalar = (0, 2, 3, 4, 5)
         square_on_scalar(0)
-        for j in range(1, 6):
+        for before, j in zip(on_scalar, on_scalar[1:]):
             square_on_scalar(j)
-            weigh_on_scalar(j - 1)
+            weigh_on_scalar(before)
             if j < 5:
-                store(j - 1)
+                store(before)
         square_on_scalar(6, HALVES[0])
         store(4, WHOLE, nc.scalar)
         weigh_on_scalar(5)
@@ -441,6 +453,6 @@ def tile_list_passacaglia_variation_surprise_kernel(
         store(6, HALVES[0], nc.scalar)
         diff_of[(6, HALVES[1].start)] = diffs[6][:, HALVES[1]]
         finish_on_vector(6, HALVES[1], place=AT_TAB2 + 1024 + LAP)
-        subtract(7, parts[1], AT_TAB2 + 2048 + LAP + 1024)
-        finish_on_vector(7, parts[0], place=AT_TAB2 + 2048 + LAP)
-        finish_on_vector(7, parts[1], nc.scalar, place="diff5")
+        subtract(7, HALVES[1], AT_TAB2 + 2048 + LAP + 1024)
+        finish_on_vector(7, HALVES[0], place=AT_TAB2 + 2048 + LAP)
+        finish_on_vector(7, HALVES[1], nc.scalar, place="diff5")

@@ -214,21 +214,30 @@ def tile_list_passacaglia_variation_surprise_kernel(
                 nc.sync.dma_start(out=raw[:, t, :], in_=w2_view[b, c, t])
             w2_raw[(b, c)] = raw
 
-        def group_w2_on_gpsimd(b, c, place):
-            grouped = tile([P, 4 * 512], BF16, f"w2_grouped{b}{c}", place)
-            dst = grouped[:].rearrange("p (u o l t) -> p u o l t", u=4, o=32, l=4)
+        def group_w2_on_gpsimd(b, c, place, tiles=range(4)):
+            grouped = tile([P, len(tiles) * 512], BF16, f"w2_grouped{b}{c}", place)
+            dst = grouped[:].rearrange("p (u o l t) -> p u o l t", o=32, l=4, t=4)
             src = w2_raw[(b, c)][:].rearrange("p t (o u l) -> p u o l t", u=4, o=32)
-            for u in range(4):
+            for u in tiles:
                 nc.gpsimd.tensor_scalar(
                     out=dst[:, u], in0=src[:, u], scalar1=1.0, scalar2=0.0, op0=ALU.mult, op1=ALU.add
                 )
-            w2_grouped[(b, c)] = grouped
+                w2_grouped[(b, c, u)] = grouped[:, u * 512 :]
+
+        def group_w2_on_scalar(b, c, place, tiles):
+            grouped = tile([P, len(tiles) * 512], BF16, f"w2_grouped{b}{c}_late", place)
+            src = w2_raw[(b, c)][:].rearrange("p t (o u l) -> p u o t l", u=4, o=32)
+            nc.scalar.copy(
+                out=grouped[:].rearrange("p (u o l t) -> p u o t l", o=32, l=4, t=4),
+                in_=src[:, tiles[0] : tiles[-1] + 1],
+            )
+            w2_grouped[(b, c, tiles[0])] = grouped[:]
 
         def quantize_w2(b, c, place, scale_place=None, tiles=range(4)):
             first, count = tiles[0] * P, len(tiles) * P
             codes = tile([P, count], U32, f"w2_codes{b}{c}_{first}", place)
             scales = tile([P, count], U8, f"w2_sc{b}{c}_{first}", scale_place)
-            grouped = w2_grouped[(b, c)][:, 4 * first : 4 * (first + count)]
+            grouped = w2_grouped[(b, c, tiles[0])][:, 0 : 4 * count]
             nc.vector.quantize_mx(out=codes[:].bitcast(FP8X4), scales=scales[:], in_=grouped)
             for n, u in enumerate(tiles):
                 w2_codes[(b, c, u)] = codes[:, n * P : (n + 1) * P]
@@ -236,8 +245,8 @@ def tile_list_passacaglia_variation_surprise_kernel(
 
         load_w2(0, 0, AT_TAB0 + LAP)
         load_w2(1, 0, AT_TAB1)
-        load_w2(0, 1, AT_TAB2)
-        load_w2(1, 1, AT_LAST_CHUNK)
+        load_w2(1, 1, AT_TAB2)
+        load_w2(0, 1, AT_LAST_CHUNK)
 
         h = [tile([P, S], F32, f"h{j}") for j in range(TILES)]
         theme, sines, banks = {}, {}, {}
@@ -336,8 +345,8 @@ def tile_list_passacaglia_variation_surprise_kernel(
             fill_bank(j, 1)
         group_w2_on_gpsimd(0, 0, AT_FIRST_GROUPED)
         group_w2_on_gpsimd(1, 0, None)
+        group_w2_on_gpsimd(1, 1, None, range(1))
         group_w2_on_gpsimd(0, 1, None)
-        group_w2_on_gpsimd(1, 1, None)
         for j in range(TILES):
             pick_theme(j)
         for j in EARLY_PICKS:
@@ -364,7 +373,9 @@ def tile_list_passacaglia_variation_surprise_kernel(
         quantize_w2(0, 0, None, AT_LATE_Z, range(2, 4))
         quantize_w2(1, 0, None, AT_LATE_Z + 256, range(2, 4))
         quantize_w2(0, 1, None, AT_LATE_Z + 512)
-        quantize_w2(1, 1, None, AT_LATE_Z + 1024)
+        group_w2_on_scalar(1, 1, "z_rows1", range(1, 4))
+        quantize_w2(1, 1, None, AT_LATE_Z + 1024, range(1))
+        quantize_w2(1, 1, None, None, range(1, 4))
 
         out_view = out.rearrange("(b o t i) m -> b t o i m", b=GROUPS, o=32, t=4)
         y_of, y_sb, diffs, diff_of, squares = {}, {}, {}, {}, {}

@@ -25,6 +25,7 @@ LAST0 = P - 16 * PASSES
 PAIR0 = LAST0 + 16
 LAP = 64
 BANK_OF = (0, 1, 2, 3, 4, 0, 1, 2, 5, 6, 7, 3, 4, 0, 1, 2)
+SPARE_BANK = 5
 SINE_LAG = 2
 AMP_ON_VECTOR = (0, 1, 2, 3)
 EARLY_PICKS = (1, 3, 5)
@@ -33,8 +34,7 @@ AT_FIRST_GROUPED = 0
 AT_W1_GROUP1 = AT_FIRST_GROUPED + 4096 - LAP
 AT_TAB0 = AT_W1_GROUP1 + 3072 - LAP
 AT_TAB1 = AT_TAB0 + 8192 + LAP
-AT_LAST_PASS = AT_TAB1 + 8192 + LAP
-AT_TAB_SC = AT_LAST_PASS + 768
+AT_TAB_SC = AT_TAB1 + 8192 + LAP
 AT_TAB2 = AT_TAB_SC + 2048 - LAP
 CHAIN0 = AT_TAB2 + 8192
 STEP = 2048 + CODE_BYTES
@@ -152,7 +152,8 @@ def tile_list_passacaglia_variation_surprise_kernel(
         pick_codes(0)
         pick_codes(1)
         pick_codes(2, 0, BANK)
-        pick_codes(2, BANK, BANK)
+        pick_codes(2, BANK, BANK // 2)
+        pick_codes(2, BANK + BANK // 2, BANK // 2)
 
         w1_codes, w1_sc = {}, []
 
@@ -165,13 +166,11 @@ def tile_list_passacaglia_variation_surprise_kernel(
             w1_sc.append(sc)
 
         code_tiles = {}
-        APART = {(0, 0): None, (0, 1): AT_SECOND_PASS, (0, 2): AT_LAST_PASS}
-        APART.update({(j, 2): AT_LAST_PASS + 256 * j for j in (1, 2)})
+        APART = {(0, 0): None, (0, 1): AT_SECOND_PASS, (0, 2): None}
 
         def order_codes(j, copy, view, first, count):
             if (j, first) in APART:
-                width = CODE_BYTES if (j, first) == (0, 2) else count * 2 * P
-                codes = tile([P, width], U8, f"w1_codes{j}_{first}", APART[(j, first)])[:, 0 : count * 2 * P]
+                codes = tile([P, count * 2 * P], U8, f"w1_codes{j}_{first}", APART[(j, first)])[:]
             else:
                 if j not in code_tiles:
                     code_tiles[j] = tile([P, CODE_BYTES], U8, f"w1_codes{j}", at_codes(j))
@@ -186,7 +185,7 @@ def tile_list_passacaglia_variation_surprise_kernel(
 
         order_codes(0, nc.scalar.copy, U32, 0, 1)
         for j in range(1, 4):
-            order_codes(j, nc.scalar.copy, U32, 0, PASSES if j == 3 else 2)
+            order_codes(j, nc.scalar.copy, U32, 0, PASSES)
         order_scales(0, nc.scalar.copy, U32)
         order_codes(0, nc.scalar.copy, U32, 1, 1)
         order_codes(0, nc.scalar.copy, U32, 2, 1)
@@ -256,7 +255,7 @@ def tile_list_passacaglia_variation_surprise_kernel(
 
         def first_stage_pass(j, half, a, first=0, width=BANK):
             if a == 0:
-                slot = BANK_OF[2 * j + half]
+                slot = SPARE_BANK if first else BANK_OF[2 * j + half]
                 banks[(j, half, first)] = psum.tile([P, width], F32, name=f"h_ps{j}_{half}_{first}", tag=f"bank{slot}")
             at = a * 512 + (j % 4) * P
             col = half * BANK + first
@@ -324,19 +323,18 @@ def tile_list_passacaglia_variation_surprise_kernel(
                 out=z_codes[b][:, cols].bitcast(FP8X4), scales=z_sc[b][:, cols], in_=z_grouped[(b, cols.start)][:]
             )
 
-        for half in range(2):
-            first_stage_pass(0, half, 0)
+        first_tile = ((0, 0, 0, BANK), (0, 1, 0, BANK // 2), (0, 1, BANK // 2, BANK // 2))
+        behind_it = ((1, 0, 0, BANK), (1, 1, 0, BANK), (2, 0, 0, BANK))
+        for j, half, first, width in first_tile:
+            first_stage_pass(j, half, 0, first, width)
         turn_vectors()
-        for j, half in ((1, 0), (1, 1), (2, 0)):
-            first_stage_pass(j, half, 0)
-        early = ((0, 0), (0, 1), (1, 0), (1, 1), (2, 0))
-        for j, half in early:
-            first_stage_pass(j, half, 1)
-        for j, half in early:
-            if j and not half:
-                order_codes(j, nc.vector.tensor_copy, I32, 2, 1)
-            first_stage_pass(j, half, 2)
-            empty_bank(j, half)
+        for j, half, first, width in behind_it:
+            first_stage_pass(j, half, 0, first, width)
+        for a in (1, 2):
+            for j, half, first, width in first_tile + behind_it:
+                first_stage_pass(j, half, a, first, width)
+                if a == 2:
+                    empty_bank(j, half, first, width)
         fill_bank(2, 1)
         for j in range(4, TILES):
             order_codes(j, nc.vector.tensor_copy, I32, 0, PASSES)
@@ -345,7 +343,7 @@ def tile_list_passacaglia_variation_surprise_kernel(
             fill_bank(j, 1)
         group_w2_on_gpsimd(0, 0, AT_FIRST_GROUPED)
         group_w2_on_gpsimd(1, 0, None)
-        group_w2_on_gpsimd(1, 1, None, range(1))
+        group_w2_on_gpsimd(1, 1, None, range(2))
         group_w2_on_gpsimd(0, 1, None)
         for j in range(TILES):
             pick_theme(j)
@@ -373,9 +371,9 @@ def tile_list_passacaglia_variation_surprise_kernel(
         quantize_w2(0, 0, None, AT_LATE_Z, range(2, 4))
         quantize_w2(1, 0, None, AT_LATE_Z + 256, range(2, 4))
         quantize_w2(0, 1, None, AT_LATE_Z + 512)
-        group_w2_on_scalar(1, 1, "z_rows1", range(1, 4))
-        quantize_w2(1, 1, None, AT_LATE_Z + 1024, range(1))
-        quantize_w2(1, 1, None, None, range(1, 4))
+        group_w2_on_scalar(1, 1, "z_rows1", range(2, 4))
+        quantize_w2(1, 1, None, AT_LATE_Z + 1024, range(2))
+        quantize_w2(1, 1, None, None, range(2, 4))
 
         out_view = out.rearrange("(b o t i) m -> b t o i m", b=GROUPS, o=32, t=4)
         y_of, y_sb, diffs, diff_of, squares = {}, {}, {}, {}, {}

from contextlib import ExitStack

import concourse.mybir as mybir

K, T, S, NP, H = 1536, 2048, 1024, 512, 1024
FLOPS = 2 * K * S * H + 2 * H * H * NP

F32 = mybir.dt.float32
BF16 = mybir.dt.bfloat16
I32 = mybir.dt.int32
U32 = mybir.dt.uint32
U16 = mybir.dt.uint16
U8 = mybir.dt.uint8
FP8X4 = mybir.dt.float8_e4m3fn_x4
FP4X4 = mybir.dt.float4_e2m1fn_x4
ACT = mybir.ActivationFunctionType
ALU = mybir.AluOpType

P = 128
PASSES = K // 512
GROUPS = H // 512
TILES = H // P
BANK = 512
LAST0 = P - 16 * PASSES
PAIR0 = LAST0 + 16
LAP = 64
BANK_OF = (0, 1, 2, 3, 4, 0, 1, 2, 5, 6, 7, 3, 4, 0, 1, 2)
SPARE_BANK = 5
SINE_LAG = 2
AMP_ON_VECTOR = (0, 1, 2, 3)
EARLY_PICKS = (1, 3, 5)
CODE_BYTES = PASSES * 2 * P
AT_FIRST_GROUPED = 0
AT_W1_GROUP1 = AT_FIRST_GROUPED + 4096 - LAP
AT_TAB0 = AT_W1_GROUP1 + 3072 - LAP
AT_TAB1 = AT_TAB0 + 8192 + LAP
AT_TAB_SC = AT_TAB1 + 8192 + LAP
AT_TAB2 = AT_TAB_SC + 2048 - LAP
CHAIN0 = AT_TAB2 + 8192
STEP = 2048 + CODE_BYTES


def at_codes(j):
    return CHAIN0 + (j - 4) % 8 * STEP + 2048 - LAP


AT_GATE = at_codes(3) + CODE_BYTES
AT_LAST_CHUNK = AT_GATE + LAP
AT_SECOND_PASS = AT_LAST_CHUNK + 8192 - LAP


AT_LATE_Z = AT_TAB0 + LAP


def sine_place(j):
    if j + SINE_LAG < TILES:
        return at_codes(j + SINE_LAG) - 2048 + LAP
    return f"theme{j - 1}"


def tile_list_passacaglia_variation_surprise_kernel(
    tc, tab_words, tab_scales, offs, pos1, pos2, w1_words, w1_scales, w2, phase, amp, mrg, out
):
    nc = tc.nc
    with ExitStack() as ctx:
        lists = ctx.enter_context(tc.tile_pool(name="lists", bufs=1))
        sb = ctx.enter_context(tc.tile_pool(name="sb", bufs=1))
        hand = ctx.enter_context(tc.tile_pool(name="hand", bufs=1))
        psum = ctx.enter_context(tc.psum_pool(name="psum", bufs=1))

        def tile(shape, dtype, name, place=None):
            if isinstance(place, int):
                return hand.tile(shape, dtype, name=name, align_bytes=64, offset=place)
            return sb.tile(shape, dtype, name=name, tag=place or name, align_bytes=64)

        offs_sb = lists.tile([P, S // 16], U16, name="offs_sb")
        pos1_sb = lists.tile([P, NP // 16], U16, name="pos1_sb")
        pos2_sb = lists.tile([P, NP // 16], U16, name="pos2_sb")

        tab_sc = tile([P, T], U8, "tab_sc", AT_TAB_SC)
        v_sc = tile([P, PASSES * S], U8, "v_sc")
        zeros = tile([P, 16], F32, "zeros")
        tabs = []

        def load_tab(a):
            tab = tile([P, T + (STEP if a == 2 else 0)], I32, f"tab{a}", (AT_TAB0, AT_TAB1, AT_TAB2)[a])[:, 0:T]
            nc.sync.dma_start(out=tab, in_=tab_words[a].rearrange("p t i -> p (t i)").bitcast(I32))
            tabs.append(tab)

        nc.sync.dma_start(offs_sb[:], offs)
        nc.scalar.dma_start(out=tab_sc[LAST0:PAIR0, :].bitcast(I32), in_=tab_scales[2].bitcast(I32))
        nc.scalar.dma_start(
            out=tab_sc[PAIR0:P, :].bitcast(I32), in_=tab_scales[0:2].rearrange("a q t -> q a t").bitcast(I32)
        )
        vec_rows = tile([P, P], F32, "vec_rows")
        nc.gpsimd.memset(vec_rows[:], 0.0)
        nc.vector.memset(zeros[:, 0:1], 0.0)
        nc.scalar.activation(out=zeros[:, 8:9], in_=zeros[:, 0:1], func=ACT.Sin)
        for v, vector in enumerate((phase, amp, mrg)):
            nc.gpsimd.dma_start(out=vec_rows[v:P:16, :], in_=vector.rearrange("(b q c) -> q b c", b=GROUPS, q=4))
        nc.sync.dma_start(pos1_sb[:], pos1)
        load_tab(0)
        nc.sync.dma_start(pos2_sb[:], pos2)
        w1_raw = {}
        w1_sc_raw = tile([P, PASSES, 256], I32, "w1_sc_raw")
        w1_view = w1_words.rearrange("a p (b c) -> b p a c", b=GROUPS)

        def load_w1(b, first, count, place):
            raw = tile([P, count, 256], I32, f"w1_raw{b}_{first}", place)
            nc.sync.dma_start(out=raw[:], in_=w1_view[b, :, first : first + count].bitcast(I32))
            for n in range(count):
                w1_raw[(b, first + n)] = raw[:, n:count]

        def load_w1_scales():
            for r in range(4):
                nc.sync.dma_start(
                    out=w1_sc_raw[r:P:32],
                    in_=w1_scales[:, r:16:4, :].rearrange("a q n -> q a n").bitcast(I32),
                )

        load_w1(0, 0, PASSES, None)
        nc.vector.memset(w1_sc_raw[:], 0)
        load_w1_scales()
        nc.vector.memset(tab_sc[0:LAST0, :].bitcast(I32), 0)
        nc.vector.memset(v_sc[:].bitcast(I32), 0)
        load_tab(1)

        picked_sc = tile([P, S], U8, "picked_sc")
        nc.vector.tensor_copy(picked_sc[:], tab_sc[:].indirect(offs_sb[:]))
        for q in range(4):
            nc.sync.dma_start(
                out=v_sc[32 * q : 32 * q + 4, 0 : 2 * S].bitcast(I32),
                in_=picked_sc[PAIR0 + 8 * q : PAIR0 + 8 * q + 8, :].bitcast(I32),
            )
        load_tab(2)
        for q in range(4):
            nc.sync.dma_start(
                out=v_sc[32 * q : 32 * q + 4, 2 * S :].bitcast(I32),
                in_=picked_sc[LAST0 + 4 * q : LAST0 + 4 * q + 4, :].bitcast(I32),
            )

        load_w1(1, 0, PASSES, AT_W1_GROUP1)

        v_codes = [tile([P, S], U32, f"v_codes{a}") for a in range(PASSES)]

        def pick_codes(a, first=0, width=S):
            nc.vector.tensor_copy(
                v_codes[a][:, first : first + width],
                tabs[a].bitcast(U32).indirect(offs_sb[:, first // 16 : (first + width) // 16]),
            )

        pick_codes(0)
        pick_codes(1)
        pick_codes(2, 0, BANK)
        pick_codes(2, BANK, BANK // 2)
        pick_codes(2, BANK + BANK // 2, BANK // 2)

        w1_codes, w1_sc = {}, []

        def order_scales(b, copy, view):
            sc = tile([P, PASSES * 512], U8, f"w1_sc{b}", None if b else AT_TAB_SC + LAP)
            copy(
                out=sc[:].bitcast(view).rearrange("p (a t o) -> p a t o", t=4, o=32),
                in_=w1_sc_raw[:, :, 128 * b : 128 * (b + 1)].bitcast(view).rearrange("p a (o t) -> p a t o", t=4),
            )
            w1_sc.append(sc)

        code_tiles = {}
        APART = {(0, 0): None, (0, 1): AT_SECOND_PASS, (0, 2): None}

        def order_codes(j, copy, view, first, count):
            if (j, first) in APART:
                codes = tile([P, count * 2 * P], U8, f"w1_codes{j}_{first}", APART[(j, first)])[:]
            else:
                if j not in code_tiles:
                    code_tiles[j] = tile([P, CODE_BYTES], U8, f"w1_codes{j}", at_codes(j))
                codes = code_tiles[j][:, first * 2 * P : (first + count) * 2 * P]
            by_tile = w1_raw[(j // 4, first)].bitcast(view).rearrange("p a (o t w) -> p t a o w", t=4, w=2)
            copy(
                out=codes.bitcast(view).rearrange("p (a o w) -> p a o w", a=count, w=2),
                in_=by_tile[:, j % 4, 0:count],
            )
            for n in range(count):
                w1_codes[(j, first + n)] = codes[:, 2 * n * P : 2 * (n + 1) * P]

        order_codes(0, nc.scalar.copy, U32, 0, 1)
        for j in range(1, 4):
            order_codes(j, nc.scalar.copy, U32, 0, PASSES)
        order_scales(0, nc.scalar.copy, U32)
        order_codes(0, nc.scalar.copy, U32, 1, 1)
        order_codes(0, nc.scalar.copy, U32, 2, 1)
        order_scales(1, nc.scalar.copy, U32)
        vec = tile([P, 4, 32], F32, "vec")
        vec_ordered = tile([P, P], F32, "vec_ordered", "w1_codes0_0")[:]

        def turn_vectors():
            nc.scalar.copy(
                out=vec_ordered.rearrange("p (t o i) -> p t o i", t=4, i=4),
                in_=vec_rows[:].rearrange("p (o t i) -> p t o i", t=4, i=4),
            )
            nc.vector.transpose(vec[:].rearrange("p t r -> p (t r)"), vec_ordered)

        def per_channel(v, j):
            col = 16 * (j // 4) + v
            return vec[:, j % 4, col : col + 1]

        w2_view = w2.rearrange("(b o t i) (c n) -> b c t o i n", b=GROUPS, o=32, t=4, c=GROUPS)
        w2_raw, w2_grouped, w2_codes, w2_sc = {}, {}, {}, {}

        def load_w2(b, c, place):
            raw = tile([P, 4, 512], F32, f"w2_raw{b}{c}", place)
            for t in range(4):
                nc.sync.dma_start(out=raw[:, t, :], in_=w2_view[b, c, t])
            w2_raw[(b, c)] = raw

        def group_w2_on_gpsimd(b, c, place, tiles=range(4)):
            grouped = tile([P, len(tiles) * 512], BF16, f"w2_grouped{b}{c}", place)
            dst = grouped[:].rearrange("p (u o l t) -> p u o l t", o=32, l=4, t=4)
            src = w2_raw[(b, c)][:].rearrange("p t (o u l) -> p u o l t", u=4, o=32)
            for u in tiles:
                nc.gpsimd.tensor_scalar(
                    out=dst[:, u], in0=src[:, u], scalar1=1.0, scalar2=0.0, op0=ALU.mult, op1=ALU.add
                )
                w2_grouped[(b, c, u)] = grouped[:, u * 512 :]

        def group_w2_on_scalar(b, c, place, tiles):
            grouped = tile([P, len(tiles) * 512], BF16, f"w2_grouped{b}{c}_late", place)
            src = w2_raw[(b, c)][:].rearrange("p t (o u l) -> p u o t l", u=4, o=32)
            nc.scalar.copy(
                out=grouped[:].rearrange("p (u o l t) -> p u o t l", o=32, l=4, t=4),
                in_=src[:, tiles[0] : tiles[-1] + 1],
            )
            w2_grouped[(b, c, tiles[0])] = grouped[:]

        def quantize_w2(b, c, place, scale_place=None, tiles=range(4)):
            first, count = tiles[0] * P, len(tiles) * P
            codes = tile([P, count], U32, f"w2_codes{b}{c}_{first}", place)
            scales = tile([P, count], U8, f"w2_sc{b}{c}_{first}", scale_place)
            grouped = w2_grouped[(b, c, tiles[0])][:, 0 : 4 * count]
            nc.vector.quantize_mx(out=codes[:].bitcast(FP8X4), scales=scales[:], in_=grouped)
            for n, u in enumerate(tiles):
                w2_codes[(b, c, u)] = codes[:, n * P : (n + 1) * P]
                w2_sc[(b, c, u)] = scales[:, n * P : (n + 1) * P]

        load_w2(0, 0, AT_TAB0 + LAP)
        load_w2(1, 0, AT_TAB1)
        load_w2(1, 1, AT_TAB2)
        load_w2(0, 1, AT_LAST_CHUNK)

        h = [tile([P, S], F32, f"h{j}") for j in range(TILES)]
        theme, sines, banks = {}, {}, {}
        z_rows = [tile([P, 4, NP], BF16, f"z_rows{b}", None if b else AT_LAST_CHUNK) for b in range(GROUPS)]
        z_codes = [tile([P, NP], U32, "z_codes0")]
        z_sc = [tile([P, NP], U8, f"z_sc{b}") for b in range(GROUPS)]

        def first_stage_pass(j, half, a, first=0, width=BANK):
            if a == 0:
                slot = SPARE_BANK if first else BANK_OF[2 * j + half]
                banks[(j, half, first)] = psum.tile([P, width], F32, name=f"h_ps{j}_{half}_{first}", tag=f"bank{slot}")
            at = a * 512 + (j % 4) * P
            col = half * BANK + first
            nc.tensor.matmul_mx(
                out=banks[(j, half, first)][:],
                lhsT=w1_codes[(j, a)].bitcast(FP4X4),
                lhsT_scale=w1_sc[j // 4][:, at : at + P],
                rhs=v_codes[a][:, col : col + width].bitcast(FP8X4),
                rhs_scale=v_sc[:, a * S + col : a * S + col + width],
                start=(a == 0),
                stop=(a == PASSES - 1),
            )

        def empty_bank(j, half, first=0, width=BANK):
            col = half * BANK + first
            nc.scalar.copy(out=h[j][:, col : col + width], in_=banks[(j, half, first)][:])

        def fill_bank(j, half):
            for a in range(PASSES):
                first_stage_pass(j, half, a)
            empty_bank(j, half)

        WHOLE = slice(0, NP)
        HALVES = [slice(0, NP // 2), slice(NP // 2, NP)]

        def pick_theme(j, cols=WHOLE):
            if cols.start == 0:
                theme[j] = tile([P, NP], F32, f"theme{j}", None if j else AT_W1_GROUP1 + LAP)
            picks = pos1_sb[:, cols.start // 16 : cols.stop // 16]
            nc.vector.tensor_copy(theme[j][:, cols], h[j][:].indirect(picks))

        actual = {}

        def pick_actual(j):
            actual[j] = tile([P, NP], F32, f"actual{j}")
            nc.vector.tensor_copy(actual[j][:], h[j][:].indirect(pos2_sb[:]))

        def take_sine(j, cols=WHOLE):
            if cols.start == 0:
                sines[j] = tile([P, NP], F32, f"sine{j}", sine_place(j))
            nc.scalar.activation(out=sines[j][:, cols], in_=theme[j][:, cols], func=ACT.Sin, bias=per_channel(0, j))

        def scale_by_amp(j, cols=WHOLE):
            rows = z_rows[j // 4][:, j % 4, cols]
            if j in AMP_ON_VECTOR:
                nc.vector.tensor_scalar(
                    out=rows, in0=sines[j][:, cols], scalar1=per_channel(1, j), scalar2=None, op0=ALU.mult
                )
            else:
                nc.scalar.activation(out=rows, in_=sines[j][:, cols], func=ACT.Copy, scale=per_channel(1, j))

        z_grouped = {}

        def group_z(b, cols, copy):
            place = AT_LATE_Z if cols.start else None
            grouped = tile([P, 4 * (cols.stop - cols.start)], BF16, f"z_grouped{b}_{cols.start}", place)
            copy(
                out=grouped[:].rearrange("p (c i t) -> p c t i", i=4, t=4),
                in_=z_rows[b][:, :, cols].rearrange("p t (c i) -> p c t i", i=4),
            )
            z_grouped[(b, cols.start)] = grouped

        def quantize_z(b, cols):
            nc.vector.quantize_mx(
                out=z_codes[b][:, cols].bitcast(FP8X4), scales=z_sc[b][:, cols], in_=z_grouped[(b, cols.start)][:]
            )

        first_tile = ((0, 0, 0, BANK), (0, 1, 0, BANK // 2), (0, 1, BANK // 2, BANK // 2))
        behind_it = ((1, 0, 0, BANK), (1, 1, 0, BANK), (2, 0, 0, BANK))
        for j, half, first, width in first_tile:
            first_stage_pass(j, half, 0, first, width)
        turn_vectors()
        for j, half, first, width in behind_it:
            first_stage_pass(j, half, 0, first, width)
        for a in (1, 2):
            for j, half, first, width in first_tile + behind_it:
                first_stage_pass(j, half, a, first, width)
                if a == 2:
                    empty_bank(j, half, first, width)
        fill_bank(2, 1)
        for j in range(4, TILES):
            order_codes(j, nc.vector.tensor_copy, I32, 0, PASSES)
        for j in range(3, TILES):
            fill_bank(j, 0)
            fill_bank(j, 1)
        group_w2_on_gpsimd(0, 0, AT_FIRST_GROUPED)
        group_w2_on_gpsimd(1, 0, None)
        group_w2_on_gpsimd(1, 1, None, range(2))
        group_w2_on_gpsimd(0, 1, None)
        for j in range(TILES):
            pick_theme(j)
        for j in EARLY_PICKS:
            pick_actual(j)
        for j in range(TILES - 1):
            take_sine(j)
            if j not in AMP_ON_VECTOR:
                scale_by_amp(j)
        for j in AMP_ON_VECTOR:
            scale_by_amp(j)
        quantize_w2(0, 0, None, AT_LAST_CHUNK + 4096, range(2))
        group_z(0, WHOLE, nc.vector.tensor_copy)
        quantize_w2(1, 0, None, AT_LAST_CHUNK + 4096 + 256, range(2))
        quantize_z(0, WHOLE)
        z_codes.append(tile([P, NP], U32, "z_codes1", "z_grouped0_0"))
        for cols in HALVES:
            take_sine(7, cols)
        for cols in HALVES:
            scale_by_amp(7, cols)
        for cols in HALVES:
            group_z(1, cols, nc.scalar.copy)
        for cols in HALVES:
            quantize_z(1, cols)
        quantize_w2(0, 0, None, AT_LATE_Z, range(2, 4))
        quantize_w2(1, 0, None, AT_LATE_Z + 256, range(2, 4))
        quantize_w2(0, 1, None, AT_LATE_Z + 512)
        group_w2_on_scalar(1, 1, "z_rows1", range(2, 4))
        quantize_w2(1, 1, None, AT_LATE_Z + 1024, range(2))
        quantize_w2(1, 1, None, None, range(2, 4))

        out_view = out.rearrange("(b o t i) m -> b t o i m", b=GROUPS, o=32, t=4)
        y_of, y_sb, diffs, diff_of, squares = {}, {}, {}, {}, {}

        def predict(j, bank, cols=WHOLE):
            c, u = j // 4, j % 4
            y = psum.tile([P, cols.stop - cols.start], F32, name=f"y{j}_{cols.start}", tag=f"bank{bank}")
            for b in range(GROUPS):
                nc.tensor.matmul_mx(
                    out=y[:],
                    lhsT=w2_codes[(b, c, u)].bitcast(FP8X4),
                    lhsT_scale=w2_sc[(b, c, u)],
                    rhs=z_codes[b][:, cols].bitcast(FP8X4),
                    rhs_scale=z_sc[b][:, cols],
                    start=(b == 0),
                    stop=(b == GROUPS - 1),
                )
            y_of[(j, cols.start)] = y

        def fetch_y(j, cols=WHOLE):
            if cols.start == 0:
                y_sb[j] = tile([P, NP], F32, f"y_sb{j}")
            nc.scalar.copy(out=y_sb[j][:, cols], in_=y_of[(j, cols.start)][:])

        def subtract(j, cols=WHOLE, place=None):
            if place is not None:
                diff = tile([P, cols.stop - cols.start], F32, f"diff{j}_{cols.start}", place)[:]
            else:
                if cols.start == 0:
                    diffs[j] = tile([P, NP], F32, f"diff{j}")
                diff = diffs[j][:, cols]
            diff_of[(j, cols.start)] = diff
            if j in EARLY_PICKS:
                nc.vector.tensor_tensor(out=diff, in0=actual[j][:], in1=y_of[(j, 0)][:], op=ALU.subtract)
                return
            picked = h[j][:].indirect(pos2_sb[:, cols.start // 16 : cols.stop // 16])
            nc.vector.tensor_tensor(out=diff, in0=picked, in1=y_sb[j][:, cols], op=ALU.subtract)

        def square_on_scalar(j, cols=WHOLE):
            if j not in squares:
                squares[j] = tile([P, NP], F32, f"square{j}", AT_TAB2 + 2048 if j == 3 else f"square{j % 3}")
            nc.scalar.activation(out=squares[j][:, cols], in_=diffs[j][:, cols], func=ACT.Square)

        marks = {}

        def store(j, cols=WHOLE, queue=nc.sync):
            queue.dma_start(out=out_view[j // 4, j % 4][:, :, cols], in_=marks[(j, cols.start)][:])

        def weigh_on_scalar(j, cols=WHOLE):
            place = AT_TAB1 + LAP + 2048 * j if j < 4 else None
            mark = tile([P, cols.stop - cols.start], F32, f"mark{j}_{cols.start}", place)
            nc.scalar.activation(out=mark[:], in_=squares[j][:, cols], func=ACT.Copy, scale=per_channel(2, j))
            marks[(j, cols.start)] = mark

        def finish_on_vector(j, cols=slice(0, NP), queue=nc.sync, place=None):
            mark = tile([P, cols.stop - cols.start], F32, f"mark{j}_{cols.start}", place)
            diff = diff_of[(j, cols.start)]
            nc.vector.scalar_tensor_tensor(
                out=mark[:], in0=diff, scalar=per_channel(2, j), in1=diff, op0=ALU.mult, op1=ALU.mult
            )
            queue.dma_start(out=out_view[j // 4, j % 4][:, :, cols], in_=mark[:])

        for n, j in enumerate((1, 0, 2, 3, 4, 5, 6, 7)):
            predict(j, n)
        for j in range(TILES):
            if j not in EARLY_PICKS:
                fetch_y(j)
        subtract(1)
        subtract(0)
        finish_on_vector(1)
        for j in range(2, 7):
            subtract(j)
        subtract(7, HALVES[0])
        on_scalar = (0, 2, 3, 4, 5)
        square_on_scalar(0)
        for before, j in zip(on_scalar, on_scalar[1:]):
            square_on_scalar(j)
            weigh_on_scalar(before)
            if j < 5:
                store(before)
        square_on_scalar(6, HALVES[0])
        store(4, WHOLE, nc.scalar)
        weigh_on_scalar(5)
        weigh_on_scalar(6, HALVES[0])
        store(5, WHOLE, nc.scalar)
        store(6, HALVES[0], nc.scalar)
        diff_of[(6, HALVES[1].start)] = diffs[6][:, HALVES[1]]
        finish_on_vector(6, HALVES[1], place=AT_TAB2 + 1024 + LAP)
        subtract(7, HALVES[1], AT_TAB2 + 2048 + LAP + 1024)
        finish_on_vector(7, HALVES[0], place=AT_TAB2 + 2048 + LAP)
        finish_on_vector(7, HALVES[1], nc.scalar, place="diff5")
